import numpy as np
import ml_dtypes


def mxq(x, axis, fmt="e4m3"):
    dtype, down = {"e4m3": (ml_dtypes.float8_e4m3fn, 7), "e5m2": (ml_dtypes.float8_e5m2, 14)}[fmt]
    v = np.moveaxis(np.asarray(x, np.float32).astype(ml_dtypes.bfloat16).astype(np.float64), axis, -1)
    blocks = v.reshape(v.shape[:-1] + (-1, 32))
    amax = np.abs(blocks).max(-1, keepdims=True)
    byte = np.maximum(np.where(amax > 0, np.frexp(amax)[1] - 1 + 127, 0) - down, 1)
    scale = np.exp2(byte - 127.0)
    codes = (blocks / scale).astype(np.float32).astype(dtype).astype(np.float64)
    return np.moveaxis((codes * scale).reshape(v.shape), -1, axis)


WIDE = False


def mx_kscale(k):
    if not WIDE:
        return np.ones(k)
    levels = np.array([10, -10, 5, -5, 0])
    if k % 512:
        return np.exp2(np.random.permutation(np.resize(levels, k // 32))).repeat(32)
    a = np.empty((k // 512, 16))
    for p in range(k // 512):
        a[p, :8] = np.random.permutation(np.resize(levels, 8))
        for g in range(8):
            far = levels[np.abs(levels - a[p, g]) >= 10]
            a[p, g + 8] = far[np.random.randint(len(far))]
    return np.exp2(a.ravel()).repeat(32)


def f64(x):
    return np.asarray(x).astype(np.float64)


def striped(idx):
    return np.tile(idx.reshape(-1, 16).T, (8, 1)).astype(np.uint16)


def unstriped(offs):
    return offs[:16].T.reshape(-1).astype(np.int64)


def pack_weight(w):
    k, n = w.shape
    w = f64(np.asarray(w, np.float32).astype(ml_dtypes.bfloat16)).reshape(k // 32, 32, n)
    amax = np.abs(w).max(1)
    byte = np.clip(np.where(amax > 0, np.frexp(amax)[1] - 1 + 127 - 7, 1), 1, 254)
    scaled = (w * np.exp2(127.0 - byte)[:, None, :]).reshape(k, n).astype(np.float32)
    words = np.ascontiguousarray(scaled.reshape(k // 512, 128, 4, n).transpose(0, 1, 3, 2)).astype(ml_dtypes.float8_e4m3fn).view(np.uint8)
    return words, np.ascontiguousarray(byte.astype(np.uint8).reshape(k // 512, 16, n))


def unpack_weight(words, scales):
    g, p, n, _ = words.shape
    vals = np.ascontiguousarray(words).view(ml_dtypes.float8_e4m3fn).astype(np.float64) * np.repeat(np.exp2(scales.astype(np.float64) - 127.0), 8, axis=1)[..., None]
    return vals.transpose(0, 1, 3, 2).reshape(g * 512, n)


def relu(v):
    return np.maximum(v, 0.0)


K, T, S, D, V, H, N, U = 1024, 2048, 512, 2, 512, 512, 128, 1024
P = 2 ** 7


def setup_inputs():
    n = np.random.standard_normal
    s = mx_kscale(K)[:, None]
    u = mx_kscale(H)
    packed_xT = pack_weight(n((K, T)) * s)
    return {
        "x_words": packed_xT[0],
        "x_scales": packed_xT[1],
        "w1": (n((K, H)) / np.sqrt(K) / s * u).astype(np.float32),
        "w2": (n((H, N)) / np.sqrt(H) / u[:, None]).astype(np.float32),
        "gate": np.tile(np.random.uniform(0.2, 0.6, (D, 1, V)), (1, P, 1)).astype(np.float32),
        "emb": (0.5 * n((H, U)) * u[:, None]).astype(np.float32),
        "offs": striped(np.random.permutation(T)[:S]),
        "cell": striped(np.random.permutation(U)[:S]),
        "pos1": striped(np.random.permutation(U)[:V]),
        "pos2": striped(np.random.permutation(U)[:V]),
    }


def reference(x_words, x_scales, w1, w2, gate, emb, offs, cell, pos1, pos2):
    xq = unpack_weight(x_words, x_scales)[:, unstriped(offs)]
    up = np.zeros((H, U))
    up[:, unstriped(cell)] = relu(mxq(f64(w1), 0, "e4m3").T @ xq)
    z = up + f64(emb)
    y = mxq(f64(w2), 0, "e4m3").T @ mxq(z, 0, "e4m3")
    return y[:, unstriped(pos1)] * f64(gate)[0, :1] + y[:, unstriped(pos2)] * f64(gate)[1, :1]

@@ -1,0 +1,250 @@
+from contextlib import ExitStack
+
+import concourse.mybir as mybir
+from concourse.masks import make_identity
+
+K, T, S, V, H, N, U = 1024, 2048, 512, 512, 512, 128, 1024
+FLOPS = 2 * (K * H * S + H * N * U)
+
+F32 = mybir.dt.float32
+BF16 = mybir.dt.bfloat16
+I32 = mybir.dt.int32
+U32 = mybir.dt.uint32
+U16 = mybir.dt.uint16
+U8 = mybir.dt.uint8
+FP8X4 = mybir.dt.float8_e4m3fn_x4
+RELU = mybir.ActivationFunctionType.Relu
+COPY = mybir.ActivationFunctionType.Copy
+MULT = mybir.AluOpType.mult
+ADD = mybir.AluOpType.add
+
+P = 128
+PACK = 4
+K_PASS = P * PACK
+PASSES = K // K_PASS
+PLANES = H // P
+HALF = S // 2
+LIST_COLS = S // 16
+CELL_BLOCKS = U // P
+BANK_BLOCKS = 4
+QUARTER = U // 4
+
+
+def tile_picked_devox_none_p_kernel(tc, x_words, x_scales, w1, w2, gate, emb, offs, cell, pos1, pos2, out):
+    nc = tc.nc
+    with ExitStack() as ctx:
+        keep = ctx.enter_context(tc.tile_pool(name="keep", bufs=1))
+        psum = ctx.enter_context(tc.psum_pool(name="psum", bufs=1))
+
+        def bank(index, name):
+            return psum.tile([P, 512], F32, name=name, tag=f"bank{index}")
+
+        def load_list(src, name):
+            tile = keep.tile([P, LIST_COLS], U16, name=name)
+            nc.sync.dma_start(tile[:], src)
+            return tile
+
+        def half_cols(half):
+            return slice(half * LIST_COLS // 2, (half + 1) * LIST_COLS // 2)
+
+        x_scale_rows = keep.tile([P, PASSES, T], U8, name="x_scale_rows", align_bytes=64)
+        scale_words = x_scale_rows[:].rearrange("p g c -> p (g c)").bitcast(I32)
+        nc.gpsimd.memset(scale_words[:, :704], 0)
+        nc.vector.memset(scale_words[:, 704:], 0)
+
+        def load_scales():
+            for q in range(4):
+                nc.sync.dma_start(
+                    out=x_scale_rows[32 * q : 32 * q + 4].bitcast(I32),
+                    in_=x_scales[:, 4 * q : 4 * q + 4, :].rearrange("g r c -> r g c").bitcast(I32),
+                )
+
+        offs_t = load_list(offs, "offs_t")
+
+        def load_w1(t):
+            raw = keep.tile([P, PASSES, PACK, P], F32, name=f"w1_raw{t}", tag=f"w1_raw{t}")
+            for g in range(PASSES):
+                rows = w1[g * K_PASS : (g + 1) * K_PASS, t * P : (t + 1) * P]
+                nc.sync.dma_start(out=raw[:, g], in_=rows.rearrange("(p j) c -> p j c", j=PACK))
+                if t == 0 and g == 1:
+                    load_scales()
+            return raw
+
+        def load_emb(t):
+            tile = keep.tile([P, U], F32, name=f"emb{t}")
+            nc.sync.dma_start(out=tile[:], in_=emb[t * P : (t + 1) * P, :])
+            return tile
+
+        w1_raw = [load_w1(0)]
+        x_tiles = []
+        for g in range(PASSES):
+            tile = keep.tile([P, T], I32, name=f"x_words{g}")
+            nc.sync.dma_start(out=tile[:], in_=x_words[g].rearrange("p n t -> p (n t)").bitcast(I32))
+            x_tiles.append(tile)
+        cell_t = load_list(cell, "cell_t")
+        w1_raw.append(load_w1(1))
+        emb_tiles = []
+        for t in range(PLANES):
+            if t + 2 < PLANES:
+                w1_raw.append(load_w1(t + 2))
+            emb_tiles.append(load_emb(t))
+        w2_raw = keep.tile([P, PACK, N], F32, name="w2_raw", tag="w2_raw")
+        nc.sync.dma_start(out=w2_raw[:], in_=w2.rearrange("(p j) n -> p j n", j=PACK))
+        pos_t = [load_list(pos1, "pos1_t"), load_list(pos2, "pos2_t")]
+        gate_t = keep.tile([P, 2, V], F32, name="gate_t")
+        nc.sync.dma_start(out=gate_t[:], in_=gate.rearrange("d p v -> p d v"))
+
+        ident = keep.tile([P, P], F32, name="ident")
+        make_identity(nc, ident[:])
+
+        windows = []
+        for t in range(PLANES):
+            tile = keep.tile([P, U], F32, name=f"window{t}")
+            (nc.vector if t < 2 else nc.gpsimd).memset(tile[:].bitcast(I32), 0)
+            windows.append(tile)
+
+        def interleave_w1(t):
+            grouped = keep.tile([P, PASSES, P, PACK], BF16, name=f"w1_grouped{t}", align_bytes=64)
+            for g in range(PASSES):
+                nc.scalar.activation(
+                    grouped[:, g].rearrange("p (c i) j -> p c j i", i=4),
+                    w1_raw[t][:, g].rearrange("p j (c i) -> p c j i", i=4),
+                    COPY,
+                )
+            return grouped
+
+        def quantize(grouped_flat, width, name):
+            codes = keep.tile([P, width], U32, name=name + "_codes", align_bytes=64)
+            scales = keep.tile([P, width], U8, name=name + "_scales", align_bytes=64)
+            nc.vector.quantize_mx(out=codes[:].bitcast(FP8X4), scales=scales[:], in_=grouped_flat)
+            return codes, scales
+
+        def quantize_w1(t):
+            grouped = interleave_w1(t)
+            return quantize(grouped[:].rearrange("p g c j -> p (g c j)"), PASSES * P, f"w1q{t}")
+
+        xg_scales = keep.tile([P, PASSES, S], U8, name="xg_scales", align_bytes=64)
+        for g in range(PASSES):
+            nc.vector.tensor_copy(xg_scales[:, g], x_scale_rows[:, g].indirect(offs_t[:]))
+        w1q = quantize_w1(0)
+        xg_words = [keep.tile([P, S], U32, name=f"xg_words{g}", align_bytes=64) for g in range(PASSES)]
+        nc.vector.tensor_copy(xg_words[0][:], x_tiles[0][:].bitcast(U32).indirect(offs_t[:]))
+        for half in range(2):
+            nc.vector.tensor_copy(
+                xg_words[1][:, half * HALF : (half + 1) * HALF],
+                x_tiles[1][:].bitcast(U32).indirect(offs_t[:, half_cols(half)]),
+            )
+
+        def first_product(t, half, w1q_t):
+            codes, scales = w1q_t
+            acc = bank(half, f"h{t}_{half}")
+            cols = slice(half * HALF, (half + 1) * HALF)
+            for g in range(PASSES):
+                nc.tensor.matmul_mx(
+                    out=acc[:, :HALF],
+                    lhsT=codes[:, g * P : (g + 1) * P].bitcast(FP8X4),
+                    lhsT_scale=scales[:, g * P : (g + 1) * P],
+                    rhs=xg_words[g][:, cols].bitcast(FP8X4),
+                    rhs_scale=xg_scales[:, g, cols],
+                    start=(g == 0),
+                    stop=(g == PASSES - 1),
+                )
+            return acc
+
+        def relu_and_scatter(t, half, acc, tag):
+            staged = keep.tile([P, HALF], F32, name=f"hs{t}_{half}", tag=tag)
+            nc.scalar.activation(staged[:], acc[:, :HALF], RELU)
+            nc.vector.tensor_copy(windows[t][:].indirect(cell_t[:, half_cols(half)]), staged[:])
+            if (t, half) == (0, 0):
+                clock = keep.tile([P, 1], F32, name="clock0")
+                nc.gpsimd.tensor_copy(clock[:], staged[:, 0:1])
+            if (t, half) == (3, 1):
+                clock = keep.tile([P, 1], F32, name="clock1")
+                nc.gpsimd.tensor_copy(clock[:], windows[t][:, 0:1])
+
+        z_rows = [keep.tile([P, BANK_BLOCKS * H], BF16, name=f"z_rows{b}") for b in range(2)]
+
+        def transposes(acc, src, b, first, last):
+            for rb in range(BANK_BLOCKS):
+                c0 = (b * BANK_BLOCKS + rb) * P
+                nc.tensor.matmul(
+                    acc[:, rb * P : (rb + 1) * P],
+                    src[:, c0 : c0 + P],
+                    ident[:],
+                    start=(first and rb == 0),
+                    stop=(last and rb == BANK_BLOCKS - 1),
+                    is_transpose=True,
+                )
+
+        def add_emb(t):
+            accs = [bank(2 + 2 * (t % 2) + b, f"zt{t}_{b}") for b in range(2)]
+            for b in range(2):
+                transposes(accs[b], emb_tiles[t], b, True, False)
+            for b in range(2):
+                transposes(accs[b], windows[t], b, False, True)
+            for b in range(2):
+                dst = z_rows[b][:].rearrange("r (rb u p e) -> r rb u p e", rb=BANK_BLOCKS, u=2, e=2)[:, :, :, 32 * t : 32 * (t + 1), :]
+                src = accs[b][:].rearrange("r (rb p u e) -> r rb u p e", rb=BANK_BLOCKS, u=2, e=2)
+                if t == PLANES - 1 and b == 1:
+                    nc.vector.tensor_copy(dst, src)
+                else:
+                    nc.scalar.copy(dst, src)
+
+        accs = [first_product(0, half, w1q) for half in range(2)]
+        relu_and_scatter(0, 0, accs[0], "hs0")
+        for t in range(PLANES):
+            if t + 1 < PLANES:
+                w1q = quantize_w1(t + 1)
+                relu_and_scatter(t, 1, accs[1], f"w1_raw{t + 1}")
+                accs = [first_product(t + 1, half, w1q) for half in range(2)]
+                relu_and_scatter(t + 1, 0, accs[0], f"hs{t + 1}")
+            else:
+                w2_grouped = keep.tile([P, N, PACK], BF16, name="w2_grouped", align_bytes=64)
+                nc.scalar.activation(
+                    w2_grouped[:].rearrange("p (c i) j -> p c j i", i=4),
+                    w2_raw[:].rearrange("p j (c i) -> p c j i", i=4),
+                    COPY,
+                )
+                w2_codes, w2_scales = quantize(w2_grouped[:].rearrange("p c j -> p (c j)"), N, "w2q")
+                relu_and_scatter(t, 1, accs[1], "w2_raw")
+            add_emb(t)
+
+        zq = []
+        for q in range(4):
+            acc = bank((0, 1, 6, 7)[q], f"zw{q}")
+            words = z_rows[q // 2][:].bitcast(F32)
+            for rb in range(2):
+                for u in range(2):
+                    c0 = ((2 * (q % 2) + rb) * 2 + u) * P
+                    nc.tensor.transpose(acc[:, (2 * rb + u) * P : (2 * rb + u + 1) * P], words[:, c0 : c0 + P], ident[:])
+            grouped = keep.tile([P, QUARTER * PACK], BF16, name=f"z_grouped{q}", align_bytes=64)
+            nc.scalar.copy(
+                grouped[:].bitcast(F32).rearrange("p (rb r u) -> p rb r u", rb=2, u=2),
+                acc[:].rearrange("p (rb u r) -> p rb r u", rb=2, u=2),
+            )
+            zq.append(quantize(grouped[:], QUARTER, f"zq{q}"))
+
+        y = keep.tile([P, U], F32, name="y")
+        for q in range(4):
+            acc = bank(2 + q, f"y{q}")
+            nc.tensor.matmul_mx(
+                out=acc[:, :QUARTER],
+                lhsT=w2_codes[:].bitcast(FP8X4),
+                lhsT_scale=w2_scales[:],
+                rhs=zq[q][0][:].bitcast(FP8X4),
+                rhs_scale=zq[q][1][:],
+                start=True,
+                stop=True,
+            )
+            nc.vector.tensor_copy(y[:, q * QUARTER : (q + 1) * QUARTER], acc[:, :QUARTER])
+
+        for half in range(2):
+            cols = slice(half * HALF, (half + 1) * HALF)
+            terms = []
+            for d in range(2):
+                term = keep.tile([P, HALF], F32, name=f"term{half}_{d}")
+                nc.vector.tensor_tensor(term[:], y[:].indirect(pos_t[d][:, half_cols(half)]), gate_t[:, d, cols], MULT)
+                terms.append(term)
+            result = keep.tile([P, HALF], F32, name=f"result{half}")
+            nc.vector.tensor_tensor(result[:], terms[0][:], terms[1][:], ADD)
+            nc.sync.dma_start(out=out[:, cols], in_=result[:])

@@ -103,8 +103,14 @@ def tile_picked_devox_none_p_kernel(tc, x_words, x_scales, w1, w2, gate, emb, of
             (nc.vector if t < 2 else nc.gpsimd).memset(tile[:].bitcast(I32), 0)
             windows.append(tile)
 
+        zero_bias = []
+        for t in range(PLANES):
+            tile = keep.tile([P, 1], F32, name=f"zero_bias{t}", tag=f"grouped{t + 1}", align_bytes=64)
+            nc.gpsimd.memset(tile[:], 0.0)
+            zero_bias.append(tile)
+
         def interleave_w1(t):
-            grouped = keep.tile([P, PASSES, P, PACK], BF16, name=f"w1_grouped{t}", align_bytes=64)
+            grouped = keep.tile([P, PASSES, P, PACK], BF16, name=f"w1_grouped{t}", tag=f"grouped{t}", align_bytes=64)
             for g in range(PASSES):
                 nc.scalar.activation(
                     grouped[:, g].rearrange("p (c i) j -> p c j i", i=4),
@@ -127,11 +133,12 @@ def tile_picked_devox_none_p_kernel(tc, x_words, x_scales, w1, w2, gate, emb, of
         for g in range(PASSES):
             nc.vector.tensor_copy(xg_scales[:, g], x_scale_rows[:, g].indirect(offs_t[:]))
         w1q = quantize_w1(0)
-        xg_words = [keep.tile([P, S], U32, name=f"xg_words{g}", align_bytes=64) for g in range(PASSES)]
-        nc.vector.tensor_copy(xg_words[0][:], x_tiles[0][:].bitcast(U32).indirect(offs_t[:]))
+        xg_first = keep.tile([P, S], U32, name="xg_first", align_bytes=64)
+        nc.vector.tensor_copy(xg_first[:], x_tiles[0][:].bitcast(U32).indirect(offs_t[:]))
+        xg_second = [keep.tile([P, HALF], U32, name=f"xg_second{half}", align_bytes=64) for half in range(2)]
         for half in range(2):
             nc.vector.tensor_copy(
-                xg_words[1][:, half * HALF : (half + 1) * HALF],
+                xg_second[half][:],
                 x_tiles[1][:].bitcast(U32).indirect(offs_t[:, half_cols(half)]),
             )
 
@@ -144,7 +151,7 @@ def tile_picked_devox_none_p_kernel(tc, x_words, x_scales, w1, w2, gate, emb, of
                     out=acc[:, :HALF],
                     lhsT=codes[:, g * P : (g + 1) * P].bitcast(FP8X4),
                     lhsT_scale=scales[:, g * P : (g + 1) * P],
-                    rhs=xg_words[g][:, cols].bitcast(FP8X4),
+                    rhs=(xg_first[:, cols], xg_second[half][:])[g].bitcast(FP8X4),
                     rhs_scale=xg_scales[:, g, cols],
                     start=(g == 0),
                     stop=(g == PASSES - 1),
@@ -153,14 +160,11 @@ def tile_picked_devox_none_p_kernel(tc, x_words, x_scales, w1, w2, gate, emb, of
 
         def relu_and_scatter(t, half, acc, tag):
             staged = keep.tile([P, HALF], F32, name=f"hs{t}_{half}", tag=tag)
-            nc.scalar.activation(staged[:], acc[:, :HALF], RELU)
+            if half == 0:
+                nc.scalar.activation(staged[:], acc[:, :HALF], RELU, bias=zero_bias[t][:])
+            else:
+                nc.scalar.activation(staged[:], acc[:, :HALF], RELU)
             nc.vector.tensor_copy(windows[t][:].indirect(cell_t[:, half_cols(half)]), staged[:])
-            if (t, half) == (0, 0):
-                clock = keep.tile([P, 1], F32, name="clock0")
-                nc.gpsimd.tensor_copy(clock[:], staged[:, 0:1])
-            if (t, half) == (3, 1):
-                clock = keep.tile([P, 1], F32, name="clock1")
-                nc.gpsimd.tensor_copy(clock[:], windows[t][:, 0:1])
 
         z_rows = [keep.tile([P, BANK_BLOCKS * H], BF16, name=f"z_rows{b}") for b in range(2)]
 
@@ -199,7 +203,7 @@ def tile_picked_devox_none_p_kernel(tc, x_words, x_scales, w1, w2, gate, emb, of
                 accs = [first_product(t + 1, half, w1q) for half in range(2)]
                 relu_and_scatter(t + 1, 0, accs[0], f"hs{t + 1}")
             else:
-                w2_grouped = keep.tile([P, N, PACK], BF16, name="w2_grouped", align_bytes=64)
+                w2_grouped = keep.tile([P, N, PACK], BF16, name="w2_grouped", tag=f"grouped{PLANES}", align_bytes=64)
                 nc.scalar.activation(
                     w2_grouped[:].rearrange("p (c i) j -> p c j i", i=4),
                     w2_raw[:].rearrange("p j (c i) -> p c j i", i=4),
@@ -207,7 +211,9 @@ def tile_picked_devox_none_p_kernel(tc, x_words, x_scales, w1, w2, gate, emb, of
                 )
                 w2_codes, w2_scales = quantize(w2_grouped[:].rearrange("p c j -> p (c j)"), N, "w2q")
                 relu_and_scatter(t, 1, accs[1], "w2_raw")
-            add_emb(t)
+            if t > 0:
+                add_emb(t - 1)
+        add_emb(PLANES - 1)
 
         zq = []
         for q in range(4):

@@ -87,9 +87,10 @@ def tile_picked_devox_none_p_kernel(tc, x_words, x_scales, w1, w2, gate, emb, of
         for t in range(PLANES):
             if t + 2 < PLANES:
                 w1_raw.append(load_w1(t + 2))
+            if t == 1:
+                w2_raw = keep.tile([P, PACK, N], F32, name="w2_raw", tag="w2_raw")
+                nc.sync.dma_start(out=w2_raw[:], in_=w2.rearrange("(p j) n -> p j n", j=PACK))
             emb_tiles.append(load_emb(t))
-        w2_raw = keep.tile([P, PACK, N], F32, name="w2_raw", tag="w2_raw")
-        nc.sync.dma_start(out=w2_raw[:], in_=w2.rearrange("(p j) n -> p j n", j=PACK))
         pos_t = [load_list(pos1, "pos1_t"), load_list(pos2, "pos2_t")]
         gate_t = keep.tile([P, 2, V], F32, name="gate_t")
         nc.sync.dma_start(out=gate_t[:], in_=gate.rearrange("d p v -> p d v"))
@@ -144,7 +145,7 @@ def tile_picked_devox_none_p_kernel(tc, x_words, x_scales, w1, w2, gate, emb, of
 
         def first_product(t, half, w1q_t):
             codes, scales = w1q_t
-            acc = bank(half, f"h{t}_{half}")
+            acc = bank((0, 0, 2, 4)[t] + half, f"h{t}_{half}")
             cols = slice(half * HALF, (half + 1) * HALF)
             for g in range(PASSES):
                 nc.tensor.matmul_mx(
@@ -181,7 +182,7 @@ def tile_picked_devox_none_p_kernel(tc, x_words, x_scales, w1, w2, gate, emb, of
                 )
 
         def add_emb(t):
-            accs = [bank(2 + 2 * (t % 2) + b, f"zt{t}_{b}") for b in range(2)]
+            accs = [bank((2, 4, 6, 0)[t] + b, f"zt{t}_{b}") for b in range(2)]
             for b in range(2):
                 transposes(accs[b], emb_tiles[t], b, True, False)
             for b in range(2):
@@ -200,6 +201,8 @@ def tile_picked_devox_none_p_kernel(tc, x_words, x_scales, w1, w2, gate, emb, of
             if t + 1 < PLANES:
                 w1q = quantize_w1(t + 1)
                 relu_and_scatter(t, 1, accs[1], f"w1_raw{t + 1}")
+                if t > 0:
+                    add_emb(t - 1)
                 accs = [first_product(t + 1, half, w1q) for half in range(2)]
                 relu_and_scatter(t + 1, 0, accs[0], f"hs{t + 1}")
             else:
@@ -211,30 +214,30 @@ def tile_picked_devox_none_p_kernel(tc, x_words, x_scales, w1, w2, gate, emb, of
                 )
                 w2_codes, w2_scales = quantize(w2_grouped[:].rearrange("p c j -> p (c j)"), N, "w2q")
                 relu_and_scatter(t, 1, accs[1], "w2_raw")
-            if t > 0:
-                add_emb(t - 1)
+        add_emb(PLANES - 2)
         add_emb(PLANES - 1)
 
+        chunks = ((0, 2), (2, 2), (4, 2), (6, 1), (7, 1))
         zq = []
-        for q in range(4):
-            acc = bank((0, 1, 6, 7)[q], f"zw{q}")
-            words = z_rows[q // 2][:].bitcast(F32)
-            for rb in range(2):
+        for q, (first, count) in enumerate(chunks):
+            acc = bank(2 + q, f"zw{q}")
+            words = z_rows[first // BANK_BLOCKS][:].bitcast(F32)
+            for rb in range(count):
                 for u in range(2):
-                    c0 = ((2 * (q % 2) + rb) * 2 + u) * P
+                    c0 = ((first % BANK_BLOCKS + rb) * 2 + u) * P
                     nc.tensor.transpose(acc[:, (2 * rb + u) * P : (2 * rb + u + 1) * P], words[:, c0 : c0 + P], ident[:])
-            grouped = keep.tile([P, QUARTER * PACK], BF16, name=f"z_grouped{q}", align_bytes=64)
+            grouped = keep.tile([P, count * P * PACK], BF16, name=f"z_grouped{q}", align_bytes=64)
             nc.scalar.copy(
-                grouped[:].bitcast(F32).rearrange("p (rb r u) -> p rb r u", rb=2, u=2),
-                acc[:].rearrange("p (rb u r) -> p rb r u", rb=2, u=2),
+                grouped[:].bitcast(F32).rearrange("p (rb r u) -> p rb r u", rb=count, u=2),
+                acc[:, : count * 2 * P].rearrange("p (rb u r) -> p rb r u", rb=count, u=2),
             )
-            zq.append(quantize(grouped[:], QUARTER, f"zq{q}"))
+            zq.append(quantize(grouped[:], count * P, f"zq{q}"))
 
         y = keep.tile([P, U], F32, name="y")
-        for q in range(4):
-            acc = bank(2 + q, f"y{q}")
+        for q, (first, count) in enumerate(chunks):
+            acc = bank((7 + q) % 8, f"y{q}")
             nc.tensor.matmul_mx(
-                out=acc[:, :QUARTER],
+                out=acc[:, : count * P],
                 lhsT=w2_codes[:].bitcast(FP8X4),
                 lhsT_scale=w2_scales[:],
                 rhs=zq[q][0][:].bitcast(FP8X4),
@@ -242,7 +245,7 @@ def tile_picked_devox_none_p_kernel(tc, x_words, x_scales, w1, w2, gate, emb, of
                 start=True,
                 stop=True,
             )
-            nc.vector.tensor_copy(y[:, q * QUARTER : (q + 1) * QUARTER], acc[:, :QUARTER])
+            nc.vector.tensor_copy(y[:, first * P : (first + count) * P], acc[:, : count * P])
 
         for half in range(2):
             cols = slice(half * HALF, (half + 1) * HALF)

@@ -1,7 +1,6 @@
 from contextlib import ExitStack
 
 import concourse.mybir as mybir
-from concourse.masks import make_identity
 
 K, T, S, V, H, N, U = 1024, 2048, 512, 512, 512, 128, 1024
 FLOPS = 2 * (K * H * S + H * N * U)
@@ -22,12 +21,14 @@ P = 128
 PACK = 4
 K_PASS = P * PACK
 PASSES = K // K_PASS
-PLANES = H // P
-HALF = S // 2
 LIST_COLS = S // 16
 CELL_BLOCKS = U // P
-BANK_BLOCKS = 4
-QUARTER = U // 4
+SLOT_ORDER = (0, 2, 3, 1)
+FIRST_PIECES = ((0, 128), (128, 128), (256, 256))
+CELL_CHUNKS = ((0, 2), (2, 2), (4, 2), (6, 1), (7, 1))
+PAIR_TILES = ((0, 2), (2, 2), (4, 4))
+WOVEN_BY_SCALAR = 3
+OUT_PIECES = ((0, 256), (256, 256))
 
 
 def tile_picked_devox_none_p_kernel(tc, x_words, x_scales, w1, w2, gate, emb, offs, cell, pos1, pos2, out):
@@ -44,81 +45,13 @@ def tile_picked_devox_none_p_kernel(tc, x_words, x_scales, w1, w2, gate, emb, of
             nc.sync.dma_start(tile[:], src)
             return tile
 
-        def half_cols(half):
-            return slice(half * LIST_COLS // 2, (half + 1) * LIST_COLS // 2)
+        def entries(tile, first, count):
+            return tile[:, first // 16 : (first + count) // 16]
 
-        x_scale_rows = keep.tile([P, PASSES, T], U8, name="x_scale_rows", align_bytes=64)
-        scale_words = x_scale_rows[:].rearrange("p g c -> p (g c)").bitcast(I32)
-        nc.gpsimd.memset(scale_words[:, :704], 0)
-        nc.vector.memset(scale_words[:, 704:], 0)
-
-        def load_scales():
-            for q in range(4):
-                nc.sync.dma_start(
-                    out=x_scale_rows[32 * q : 32 * q + 4].bitcast(I32),
-                    in_=x_scales[:, 4 * q : 4 * q + 4, :].rearrange("g r c -> r g c").bitcast(I32),
-                )
-
-        offs_t = load_list(offs, "offs_t")
-
-        def load_w1(t):
-            raw = keep.tile([P, PASSES, PACK, P], F32, name=f"w1_raw{t}", tag=f"w1_raw{t}")
-            for g in range(PASSES):
-                rows = w1[g * K_PASS : (g + 1) * K_PASS, t * P : (t + 1) * P]
-                nc.sync.dma_start(out=raw[:, g], in_=rows.rearrange("(p j) c -> p j c", j=PACK))
-                if t == 0 and g == 1:
-                    load_scales()
-            return raw
-
-        def load_emb(t):
-            tile = keep.tile([P, U], F32, name=f"emb{t}")
-            nc.sync.dma_start(out=tile[:], in_=emb[t * P : (t + 1) * P, :])
-            return tile
-
-        w1_raw = [load_w1(0)]
-        x_tiles = []
-        for g in range(PASSES):
+        def load_words(g):
             tile = keep.tile([P, T], I32, name=f"x_words{g}")
             nc.sync.dma_start(out=tile[:], in_=x_words[g].rearrange("p n t -> p (n t)").bitcast(I32))
-            x_tiles.append(tile)
-        cell_t = load_list(cell, "cell_t")
-        w1_raw.append(load_w1(1))
-        emb_tiles = []
-        for t in range(PLANES):
-            if t + 2 < PLANES:
-                w1_raw.append(load_w1(t + 2))
-            if t == 1:
-                w2_raw = keep.tile([P, PACK, N], F32, name="w2_raw", tag="w2_raw")
-                nc.sync.dma_start(out=w2_raw[:], in_=w2.rearrange("(p j) n -> p j n", j=PACK))
-            emb_tiles.append(load_emb(t))
-        pos_t = [load_list(pos1, "pos1_t"), load_list(pos2, "pos2_t")]
-        gate_t = keep.tile([P, 2, V], F32, name="gate_t")
-        nc.sync.dma_start(out=gate_t[:], in_=gate.rearrange("d p v -> p d v"))
-
-        ident = keep.tile([P, P], F32, name="ident")
-        make_identity(nc, ident[:])
-
-        windows = []
-        for t in range(PLANES):
-            tile = keep.tile([P, U], F32, name=f"window{t}")
-            (nc.vector if t < 2 else nc.gpsimd).memset(tile[:].bitcast(I32), 0)
-            windows.append(tile)
-
-        zero_bias = []
-        for t in range(PLANES):
-            tile = keep.tile([P, 1], F32, name=f"zero_bias{t}", tag=f"grouped{t + 1}", align_bytes=64)
-            nc.gpsimd.memset(tile[:], 0.0)
-            zero_bias.append(tile)
-
-        def interleave_w1(t):
-            grouped = keep.tile([P, PASSES, P, PACK], BF16, name=f"w1_grouped{t}", tag=f"grouped{t}", align_bytes=64)
-            for g in range(PASSES):
-                nc.scalar.activation(
-                    grouped[:, g].rearrange("p (c i) j -> p c j i", i=4),
-                    w1_raw[t][:, g].rearrange("p j (c i) -> p c j i", i=4),
-                    COPY,
-                )
-            return grouped
+            return tile
 
         def quantize(grouped_flat, width, name):
             codes = keep.tile([P, width], U32, name=name + "_codes", align_bytes=64)
@@ -126,134 +59,160 @@ def tile_picked_devox_none_p_kernel(tc, x_words, x_scales, w1, w2, gate, emb, of
             nc.vector.quantize_mx(out=codes[:].bitcast(FP8X4), scales=scales[:], in_=grouped_flat)
             return codes, scales
 
-        def quantize_w1(t):
-            grouped = interleave_w1(t)
-            return quantize(grouped[:].rearrange("p g c j -> p (g c j)"), PASSES * P, f"w1q{t}")
+        x_scale_rows = keep.tile([P, PASSES, T], U8, name="x_scale_rows", align_bytes=64)
+        scale_words = x_scale_rows[:].rearrange("p g c -> p (g c)").bitcast(I32)
+        nc.gpsimd.memset(scale_words[:, :704], 0)
+        nc.vector.memset(scale_words[:, 704:], 0)
+
+        offs_t = load_list(offs, "offs_t")
+        cell_t = load_list(cell, "cell_t")
+        w1_raw = []
+        x_tiles = []
+        for g in range(PASSES):
+            for half in range(2):
+                raw = keep.tile([P, PACK, H // 2], F32, name=f"w1_raw{g}_{half}")
+                rows = w1[g * K_PASS : (g + 1) * K_PASS, half * H // 2 : (half + 1) * H // 2]
+                nc.sync.dma_start(out=raw[:], in_=rows.rearrange("(p j) c -> p j c", j=PACK))
+                w1_raw.append(raw)
+                if g == 0 and half == 0:
+                    for q in range(4):
+                        nc.sync.dma_start(
+                            out=x_scale_rows[32 * q : 32 * q + 4].bitcast(I32),
+                            in_=x_scales[:, 4 * q : 4 * q + 4, :].rearrange("g r c -> r g c").bitcast(I32),
+                        )
+            x_tiles.append(load_words(g))
+        w2_raw = keep.tile([P, PACK, N], F32, name="w2_raw")
+        nc.sync.dma_start(out=w2_raw[:], in_=w2.rearrange("(p j) n -> p j n", j=PACK))
+        emb_rows = emb.rearrange("(p t) u -> p t u", t=PACK)
+        emb_tiles = {}
+        for t in SLOT_ORDER:
+            tile = keep.tile([P, U], F32, name=f"emb{t}", tag=f"emb{t}")
+            nc.sync.dma_start(out=tile[:], in_=emb_rows[:, t, :])
+            emb_tiles[t] = tile
+        pos_t = [load_list(pos1, "pos1_t"), load_list(pos2, "pos2_t")]
+        gate_t = keep.tile([P, 2, V], F32, name="gate_t")
+        nc.sync.dma_start(out=gate_t[:], in_=gate.rearrange("d p v -> p d v"))
+
+        windows = {}
+        for n, t in enumerate(SLOT_ORDER):
+            tile = keep.tile([P, U], F32, name=f"window{t}")
+            (nc.vector if n < 2 else nc.gpsimd).memset(tile[:].bitcast(I32), 0)
+            windows[t] = tile
 
         xg_scales = keep.tile([P, PASSES, S], U8, name="xg_scales", align_bytes=64)
         for g in range(PASSES):
             nc.vector.tensor_copy(xg_scales[:, g], x_scale_rows[:, g].indirect(offs_t[:]))
-        w1q = quantize_w1(0)
         xg_first = keep.tile([P, S], U32, name="xg_first", align_bytes=64)
         nc.vector.tensor_copy(xg_first[:], x_tiles[0][:].bitcast(U32).indirect(offs_t[:]))
-        xg_second = [keep.tile([P, HALF], U32, name=f"xg_second{half}", align_bytes=64) for half in range(2)]
-        for half in range(2):
-            nc.vector.tensor_copy(
-                xg_second[half][:],
-                x_tiles[1][:].bitcast(U32).indirect(offs_t[:, half_cols(half)]),
+
+        w1q = []
+        for g in range(PASSES):
+            grouped = keep.tile([P, PACK, P, PACK], BF16, name=f"w1_grouped{g}", align_bytes=64)
+            for half in range(2):
+                nc.scalar.activation(
+                    grouped[:, :, half * P // 2 : (half + 1) * P // 2, :].rearrange("p t m j -> p m j t"),
+                    w1_raw[2 * g + half][:].rearrange("p j (m t) -> p m j t", t=PACK),
+                    COPY,
+                )
+            w1q.append(quantize(grouped[:].rearrange("p t m j -> p (t m j)"), H, f"w1q{g}"))
+
+        pieces = [(SLOT_ORDER[0], first, count) for first, count in FIRST_PIECES]
+        pieces.extend((t, 0, S) for t in SLOT_ORDER[1:])
+        accs = [bank(n, f"h{n}") for n in range(len(pieces))]
+
+        def first_product(n, g, words):
+            t, first, count = pieces[n]
+            codes, scales = w1q[g]
+            nc.tensor.matmul_mx(
+                out=accs[n][:, :count],
+                lhsT=codes[:, t * P : (t + 1) * P].bitcast(FP8X4),
+                lhsT_scale=scales[:, t * P : (t + 1) * P],
+                rhs=words[:, first : first + count].bitcast(FP8X4),
+                rhs_scale=xg_scales[:, g, first : first + count],
+                start=(g == 0),
+                stop=(g == PASSES - 1),
             )
 
-        def first_product(t, half, w1q_t):
-            codes, scales = w1q_t
-            acc = bank((0, 0, 2, 4)[t] + half, f"h{t}_{half}")
-            cols = slice(half * HALF, (half + 1) * HALF)
-            for g in range(PASSES):
-                nc.tensor.matmul_mx(
-                    out=acc[:, :HALF],
-                    lhsT=codes[:, g * P : (g + 1) * P].bitcast(FP8X4),
-                    lhsT_scale=scales[:, g * P : (g + 1) * P],
-                    rhs=(xg_first[:, cols], xg_second[half][:])[g].bitcast(FP8X4),
-                    rhs_scale=xg_scales[:, g, cols],
-                    start=(g == 0),
-                    stop=(g == PASSES - 1),
-                )
-            return acc
+        for n in range(len(FIRST_PIECES)):
+            first_product(n, 0, xg_first)
 
-        def relu_and_scatter(t, half, acc, tag):
-            staged = keep.tile([P, HALF], F32, name=f"hs{t}_{half}", tag=tag)
-            if half == 0:
-                nc.scalar.activation(staged[:], acc[:, :HALF], RELU, bias=zero_bias[t][:])
-            else:
-                nc.scalar.activation(staged[:], acc[:, :HALF], RELU)
-            nc.vector.tensor_copy(windows[t][:].indirect(cell_t[:, half_cols(half)]), staged[:])
+        xg_second = keep.tile([P, S], U32, name="xg_second", align_bytes=64)
+        for half in range(2):
+            nc.vector.tensor_copy(
+                xg_second[:, half * S // 2 : (half + 1) * S // 2],
+                x_tiles[1][:].bitcast(U32).indirect(entries(offs_t, half * S // 2, S // 2)),
+            )
 
-        z_rows = [keep.tile([P, BANK_BLOCKS * H], BF16, name=f"z_rows{b}") for b in range(2)]
+        pairs = [keep.tile([P, 2, count * P, 2], BF16, name=f"pairs{first}") for first, count in PAIR_TILES]
 
-        def transposes(acc, src, b, first, last):
-            for rb in range(BANK_BLOCKS):
-                c0 = (b * BANK_BLOCKS + rb) * P
-                nc.tensor.matmul(
-                    acc[:, rb * P : (rb + 1) * P],
-                    src[:, c0 : c0 + P],
-                    ident[:],
-                    start=(first and rb == 0),
-                    stop=(last and rb == BANK_BLOCKS - 1),
-                    is_transpose=True,
-                )
+        def add_emb(engine, t):
+            for tile, (first, count) in zip(pairs, PAIR_TILES):
+                cols = slice(first * P, (first + count) * P)
+                engine.tensor_tensor(tile[:, t // 2, :, t % 2], windows[t][:, cols], emb_tiles[t][:, cols], ADD)
 
-        def add_emb(t):
-            accs = [bank((2, 4, 6, 0)[t] + b, f"zt{t}_{b}") for b in range(2)]
-            for b in range(2):
-                transposes(accs[b], emb_tiles[t], b, True, False)
-            for b in range(2):
-                transposes(accs[b], windows[t], b, False, True)
-            for b in range(2):
-                dst = z_rows[b][:].rearrange("r (rb u p e) -> r rb u p e", rb=BANK_BLOCKS, u=2, e=2)[:, :, :, 32 * t : 32 * (t + 1), :]
-                src = accs[b][:].rearrange("r (rb p u e) -> r rb u p e", rb=BANK_BLOCKS, u=2, e=2)
-                if t == PLANES - 1 and b == 1:
-                    nc.vector.tensor_copy(dst, src)
-                else:
-                    nc.scalar.copy(dst, src)
+        def pair_words(first, count, word):
+            for tile, (start, size) in zip(pairs, PAIR_TILES):
+                if start <= first < start + size:
+                    words = tile[:].rearrange("p u r e -> p (u r e)").bitcast(word).rearrange("p (u r) -> p r u", u=2)
+                    return words[:, (first - start) * P : (first - start + count) * P]
 
-        accs = [first_product(0, half, w1q) for half in range(2)]
-        relu_and_scatter(0, 0, accs[0], "hs0")
-        for t in range(PLANES):
-            if t + 1 < PLANES:
-                w1q = quantize_w1(t + 1)
-                relu_and_scatter(t, 1, accs[1], f"w1_raw{t + 1}")
-                if t > 0:
-                    add_emb(t - 1)
-                accs = [first_product(t + 1, half, w1q) for half in range(2)]
-                relu_and_scatter(t + 1, 0, accs[0], f"hs{t + 1}")
-            else:
-                w2_grouped = keep.tile([P, N, PACK], BF16, name="w2_grouped", tag=f"grouped{PLANES}", align_bytes=64)
+        for n, (t, first, count) in enumerate(pieces):
+            if n >= len(FIRST_PIECES):
+                first_product(n, 0, xg_first)
+            first_product(n, 1, xg_second)
+            last = n == len(pieces) - 1
+            if last:
+                w2_grouped = keep.tile([P, N, PACK], BF16, name="w2_grouped", align_bytes=64)
                 nc.scalar.activation(
                     w2_grouped[:].rearrange("p (c i) j -> p c j i", i=4),
                     w2_raw[:].rearrange("p j (c i) -> p c j i", i=4),
                     COPY,
                 )
                 w2_codes, w2_scales = quantize(w2_grouped[:].rearrange("p c j -> p (c j)"), N, "w2q")
-                relu_and_scatter(t, 1, accs[1], "w2_raw")
-        add_emb(PLANES - 2)
-        add_emb(PLANES - 1)
+            staged = keep.tile([P, count], F32, name=f"h_sb{n}", tag=(f"emb{SLOT_ORDER[0]}" if last else f"h_sb{n}"))
+            nc.scalar.activation(staged[:], accs[n][:, :count], RELU)
+            nc.vector.tensor_copy(windows[t][:].indirect(entries(cell_t, first, count)), staged[:])
+            if first + count == S and not last:
+                add_emb(nc.gpsimd, t)
 
-        chunks = ((0, 2), (2, 2), (4, 2), (6, 1), (7, 1))
-        zq = []
-        for q, (first, count) in enumerate(chunks):
-            acc = bank(2 + q, f"zw{q}")
-            words = z_rows[first // BANK_BLOCKS][:].bitcast(F32)
-            for rb in range(count):
-                for u in range(2):
-                    c0 = ((first % BANK_BLOCKS + rb) * 2 + u) * P
-                    nc.tensor.transpose(acc[:, (2 * rb + u) * P : (2 * rb + u + 1) * P], words[:, c0 : c0 + P], ident[:])
+        add_emb(nc.vector, SLOT_ORDER[-1])
+
+        z_grouped = []
+        for q, (first, count) in enumerate(CELL_CHUNKS):
             grouped = keep.tile([P, count * P * PACK], BF16, name=f"z_grouped{q}", align_bytes=64)
-            nc.scalar.copy(
-                grouped[:].bitcast(F32).rearrange("p (rb r u) -> p rb r u", rb=count, u=2),
-                acc[:, : count * 2 * P].rearrange("p (rb u r) -> p rb r u", rb=count, u=2),
-            )
-            zq.append(quantize(grouped[:], count * P, f"zq{q}"))
+            word = U32 if q < WOVEN_BY_SCALAR else I32
+            dst = grouped[:].bitcast(word).rearrange("p (r u) -> p r u", u=2)
+            src = pair_words(first, count, word)
+            if q < WOVEN_BY_SCALAR:
+                nc.scalar.copy(dst, src)
+            else:
+                nc.vector.tensor_copy(dst, src)
+            z_grouped.append(grouped)
 
         y = keep.tile([P, U], F32, name="y")
-        for q, (first, count) in enumerate(chunks):
-            acc = bank((7 + q) % 8, f"y{q}")
+        for q, (first, count) in enumerate(CELL_CHUNKS):
+            codes, scales = quantize(z_grouped[q][:], count * P, f"zq{q}")
+            acc = bank((6 + q) % 8, f"y{q}")
             nc.tensor.matmul_mx(
                 out=acc[:, : count * P],
                 lhsT=w2_codes[:].bitcast(FP8X4),
                 lhsT_scale=w2_scales[:],
-                rhs=zq[q][0][:].bitcast(FP8X4),
-                rhs_scale=zq[q][1][:],
+                rhs=codes[:].bitcast(FP8X4),
+                rhs_scale=scales[:],
                 start=True,
                 stop=True,
             )
-            nc.vector.tensor_copy(y[:, first * P : (first + count) * P], acc[:, : count * P])
+            if q < 3:
+                nc.scalar.copy(y[:, first * P : (first + count) * P], acc[:, : count * P])
+            else:
+                nc.vector.tensor_copy(y[:, first * P : (first + count) * P], acc[:, : count * P])
 
-        for half in range(2):
-            cols = slice(half * HALF, (half + 1) * HALF)
-            terms = []
+        terms = []
+        for n, (first, count) in enumerate(OUT_PIECES):
             for d in range(2):
-                term = keep.tile([P, HALF], F32, name=f"term{half}_{d}")
-                nc.vector.tensor_tensor(term[:], y[:].indirect(pos_t[d][:, half_cols(half)]), gate_t[:, d, cols], MULT)
+                term = keep.tile([P, count], F32, name=f"term{n}_{d}")
+                nc.vector.tensor_tensor(term[:], y[:].indirect(entries(pos_t[d], first, count)), gate_t[:, d, first : first + count], MULT)
                 terms.append(term)
-            result = keep.tile([P, HALF], F32, name=f"result{half}")
-            nc.vector.tensor_tensor(result[:], terms[0][:], terms[1][:], ADD)
-            nc.sync.dma_start(out=out[:, cols], in_=result[:])
+            result = keep.tile([P, count], F32, name=f"result{n}")
+            nc.vector.tensor_tensor(result[:], terms[-2][:], terms[-1][:], ADD)
+            nc.sync.dma_start(out=out[:, first : first + count], in_=result[:])

@@ -86,7 +86,7 @@ def tile_picked_devox_none_p_kernel(tc, x_words, x_scales, w1, w2, gate, emb, of
         emb_rows = emb.rearrange("(p t) u -> p t u", t=PACK)
         emb_tiles = {}
         for t in SLOT_ORDER:
-            tile = keep.tile([P, U], F32, name=f"emb{t}", tag=f"emb{t}")
+            tile = keep.tile([P, U], F32, name=f"emb{t}")
             nc.sync.dma_start(out=tile[:], in_=emb_rows[:, t, :])
             emb_tiles[t] = tile
         pos_t = [load_list(pos1, "pos1_t"), load_list(pos2, "pos2_t")]
@@ -110,8 +110,8 @@ def tile_picked_devox_none_p_kernel(tc, x_words, x_scales, w1, w2, gate, emb, of
             grouped = keep.tile([P, PACK, P, PACK], BF16, name=f"w1_grouped{g}", align_bytes=64)
             for half in range(2):
                 nc.scalar.activation(
-                    grouped[:, :, half * P // 2 : (half + 1) * P // 2, :].rearrange("p t m j -> p m j t"),
-                    w1_raw[2 * g + half][:].rearrange("p j (m t) -> p m j t", t=PACK),
+                    grouped[:, :, half * P // 2 : (half + 1) * P // 2, :].rearrange("p t m j -> p m t j"),
+                    w1_raw[2 * g + half][:].rearrange("p j (m t) -> p m t j", t=PACK),
                     COPY,
                 )
             w1q.append(quantize(grouped[:].rearrange("p t m j -> p (t m j)"), H, f"w1q{g}"))
@@ -145,10 +145,18 @@ def tile_picked_devox_none_p_kernel(tc, x_words, x_scales, w1, w2, gate, emb, of
 
         pairs = [keep.tile([P, 2, count * P, 2], BF16, name=f"pairs{first}") for first, count in PAIR_TILES]
 
-        def add_emb(engine, t):
+        def add_emb_early(t):
+            total = keep.tile([P, U], F32, name=f"z_sum{t}")
+            for half in range(2):
+                cols = slice(half * U // 2, (half + 1) * U // 2)
+                nc.gpsimd.tensor_tensor(total[:, cols], windows[t][:, cols], emb_tiles[t][:, cols], ADD)
+            for tile, (first, count) in zip(pairs, PAIR_TILES):
+                nc.scalar.copy(tile[:, t // 2, :, t % 2], total[:, first * P : (first + count) * P])
+
+        def add_emb_last(t):
             for tile, (first, count) in zip(pairs, PAIR_TILES):
                 cols = slice(first * P, (first + count) * P)
-                engine.tensor_tensor(tile[:, t // 2, :, t % 2], windows[t][:, cols], emb_tiles[t][:, cols], ADD)
+                nc.vector.tensor_tensor(tile[:, t // 2, :, t % 2], windows[t][:, cols], emb_tiles[t][:, cols], ADD)
 
         def pair_words(first, count, word):
             for tile, (start, size) in zip(pairs, PAIR_TILES):
@@ -169,13 +177,13 @@ def tile_picked_devox_none_p_kernel(tc, x_words, x_scales, w1, w2, gate, emb, of
                     COPY,
                 )
                 w2_codes, w2_scales = quantize(w2_grouped[:].rearrange("p c j -> p (c j)"), N, "w2q")
-            staged = keep.tile([P, count], F32, name=f"h_sb{n}", tag=(f"emb{SLOT_ORDER[0]}" if last else f"h_sb{n}"))
+            staged = keep.tile([P, count], F32, name=f"h_sb{n}")
             nc.scalar.activation(staged[:], accs[n][:, :count], RELU)
             nc.vector.tensor_copy(windows[t][:].indirect(entries(cell_t, first, count)), staged[:])
             if first + count == S and not last:
-                add_emb(nc.gpsimd, t)
+                add_emb_early(t)
 
-        add_emb(nc.vector, SLOT_ORDER[-1])
+        add_emb_last(SLOT_ORDER[-1])
 
         z_grouped = []
         for q, (first, count) in enumerate(CELL_CHUNKS):

@@ -1,6 +1,7 @@
 from contextlib import ExitStack
 
 import concourse.mybir as mybir
+from concourse.masks import make_identity
 
 K, T, S, V, H, N, U = 1024, 2048, 512, 512, 512, 128, 1024
 FLOPS = 2 * (K * H * S + H * N * U)
@@ -23,11 +24,12 @@ K_PASS = P * PACK
 PASSES = K // K_PASS
 LIST_COLS = S // 16
 CELL_BLOCKS = U // P
-SLOT_ORDER = (0, 2, 3, 1)
+SLOT_ORDER = (2, 3, 0, 1)
 FIRST_PIECES = ((0, 128), (128, 128), (256, 256))
 CELL_CHUNKS = ((0, 2), (2, 2), (4, 2), (6, 1), (7, 1))
-PAIR_TILES = ((0, 2), (2, 2), (4, 4))
-WOVEN_BY_SCALAR = 3
+PAIR_TILES = ((0, 2), (2, 2), (4, 2), (6, 2))
+CAST_BY_SCALAR = (128, 56)
+COPIED_BY_SCALAR = 3
 OUT_PIECES = ((0, 256), (256, 256))
 
 
@@ -59,61 +61,59 @@ def tile_picked_devox_none_p_kernel(tc, x_words, x_scales, w1, w2, gate, emb, of
             nc.vector.quantize_mx(out=codes[:].bitcast(FP8X4), scales=scales[:], in_=grouped_flat)
             return codes, scales
 
-        x_scale_rows = keep.tile([P, PASSES, T], U8, name="x_scale_rows", align_bytes=64)
-        scale_words = x_scale_rows[:].rearrange("p g c -> p (g c)").bitcast(I32)
-        nc.gpsimd.memset(scale_words[:, :704], 0)
-        nc.vector.memset(scale_words[:, 704:], 0)
+        x_scale_rows = keep.tile([P, T], U8, name="x_scale_rows", align_bytes=64)
+        nc.gpsimd.memset(x_scale_rows[:].bitcast(I32), 0)
 
         offs_t = load_list(offs, "offs_t")
         cell_t = load_list(cell, "cell_t")
+        pos_t = [load_list(pos1, "pos1_t"), load_list(pos2, "pos2_t")]
         w1_raw = []
         x_tiles = []
         for g in range(PASSES):
-            for half in range(2):
-                raw = keep.tile([P, PACK, H // 2], F32, name=f"w1_raw{g}_{half}")
-                rows = w1[g * K_PASS : (g + 1) * K_PASS, half * H // 2 : (half + 1) * H // 2]
-                nc.sync.dma_start(out=raw[:], in_=rows.rearrange("(p j) c -> p j c", j=PACK))
-                w1_raw.append(raw)
-                if g == 0 and half == 0:
-                    for q in range(4):
-                        nc.sync.dma_start(
-                            out=x_scale_rows[32 * q : 32 * q + 4].bitcast(I32),
-                            in_=x_scales[:, 4 * q : 4 * q + 4, :].rearrange("g r c -> r g c").bitcast(I32),
-                        )
+            raw = keep.tile([P, PACK, H], F32, name=f"w1_raw{g}")
+            nc.sync.dma_start(out=raw[:], in_=w1[g * K_PASS : (g + 1) * K_PASS, :].rearrange("(p j) c -> p j c", j=PACK))
+            w1_raw.append(raw)
+            if g == 0:
+                for q in range(4):
+                    nc.sync.dma_start(
+                        out=x_scale_rows[32 * q : 32 * q + 4 * PASSES].bitcast(I32),
+                        in_=x_scales[:, 4 * q : 4 * q + 4, :].bitcast(I32),
+                    )
             x_tiles.append(load_words(g))
         w2_raw = keep.tile([P, PACK, N], F32, name="w2_raw")
         nc.sync.dma_start(out=w2_raw[:], in_=w2.rearrange("(p j) n -> p j n", j=PACK))
         emb_rows = emb.rearrange("(p t) u -> p t u", t=PACK)
         emb_tiles = {}
-        for t in SLOT_ORDER:
-            tile = keep.tile([P, U], F32, name=f"emb{t}")
-            nc.sync.dma_start(out=tile[:], in_=emb_rows[:, t, :])
-            emb_tiles[t] = tile
-        pos_t = [load_list(pos1, "pos1_t"), load_list(pos2, "pos2_t")]
+        windows = {}
+        for t in SLOT_ORDER[:2]:
+            emb_tiles[t] = keep.tile([P, U], F32, name=f"emb{t}")
+            nc.sync.dma_start(out=emb_tiles[t][:], in_=emb_rows[:, t, :])
+            windows[t] = keep.tile([P, U], F32, name=f"window{t}")
+        for t in SLOT_ORDER[2:]:
+            windows[t] = keep.tile([P, 2 * U], F32, name=f"window{t}")
+            nc.sync.dma_start(out=windows[t][:, U:], in_=emb_rows[:, 1 - t, :])
         gate_t = keep.tile([P, 2, V], F32, name="gate_t")
         nc.sync.dma_start(out=gate_t[:], in_=gate.rearrange("d p v -> p d v"))
 
-        windows = {}
+        ident = keep.tile([P, P], F32, name="ident")
+        make_identity(nc, ident[:])
         for n, t in enumerate(SLOT_ORDER):
-            tile = keep.tile([P, U], F32, name=f"window{t}")
-            (nc.vector if n < 2 else nc.gpsimd).memset(tile[:].bitcast(I32), 0)
-            windows[t] = tile
+            (nc.vector if n < 2 else nc.gpsimd).memset(windows[t][:, :U].bitcast(I32), 0)
 
-        xg_scales = keep.tile([P, PASSES, S], U8, name="xg_scales", align_bytes=64)
-        for g in range(PASSES):
-            nc.vector.tensor_copy(xg_scales[:, g], x_scale_rows[:, g].indirect(offs_t[:]))
+        xg_scales = keep.tile([P, S], U8, name="xg_scales", align_bytes=64)
+        nc.vector.tensor_copy(xg_scales[:], x_scale_rows[:].indirect(offs_t[:]))
         xg_first = keep.tile([P, S], U32, name="xg_first", align_bytes=64)
         nc.vector.tensor_copy(xg_first[:], x_tiles[0][:].bitcast(U32).indirect(offs_t[:]))
 
         w1q = []
         for g in range(PASSES):
             grouped = keep.tile([P, PACK, P, PACK], BF16, name=f"w1_grouped{g}", align_bytes=64)
-            for half in range(2):
-                nc.scalar.activation(
-                    grouped[:, :, half * P // 2 : (half + 1) * P // 2, :].rearrange("p t m j -> p m t j"),
-                    w1_raw[2 * g + half][:].rearrange("p j (m t) -> p m t j", t=PACK),
-                    COPY,
-                )
+            dst = grouped[:].rearrange("p t m j -> p m t j")
+            src = w1_raw[g][:].rearrange("p j (m t) -> p m t j", t=PACK)
+            share = CAST_BY_SCALAR[g]
+            nc.scalar.activation(dst[:, :share], src[:, :share], COPY)
+            if share < P:
+                nc.vector.tensor_copy(dst[:, share:], src[:, share:])
             w1q.append(quantize(grouped[:].rearrange("p t m j -> p (t m j)"), H, f"w1q{g}"))
 
         pieces = [(SLOT_ORDER[0], first, count) for first, count in FIRST_PIECES]
@@ -128,7 +128,7 @@ def tile_picked_devox_none_p_kernel(tc, x_words, x_scales, w1, w2, gate, emb, of
                 lhsT=codes[:, t * P : (t + 1) * P].bitcast(FP8X4),
                 lhsT_scale=scales[:, t * P : (t + 1) * P],
                 rhs=words[:, first : first + count].bitcast(FP8X4),
-                rhs_scale=xg_scales[:, g, first : first + count],
+                rhs_scale=xg_scales[4 * g :, first : first + count],
                 start=(g == 0),
                 stop=(g == PASSES - 1),
             )
@@ -144,25 +144,6 @@ def tile_picked_devox_none_p_kernel(tc, x_words, x_scales, w1, w2, gate, emb, of
             )
 
         pairs = [keep.tile([P, 2, count * P, 2], BF16, name=f"pairs{first}") for first, count in PAIR_TILES]
-
-        def add_emb_early(t):
-            total = keep.tile([P, U], F32, name=f"z_sum{t}")
-            for half in range(2):
-                cols = slice(half * U // 2, (half + 1) * U // 2)
-                nc.gpsimd.tensor_tensor(total[:, cols], windows[t][:, cols], emb_tiles[t][:, cols], ADD)
-            for tile, (first, count) in zip(pairs, PAIR_TILES):
-                nc.scalar.copy(tile[:, t // 2, :, t % 2], total[:, first * P : (first + count) * P])
-
-        def add_emb_last(t):
-            for tile, (first, count) in zip(pairs, PAIR_TILES):
-                cols = slice(first * P, (first + count) * P)
-                nc.vector.tensor_tensor(tile[:, t // 2, :, t % 2], windows[t][:, cols], emb_tiles[t][:, cols], ADD)
-
-        def pair_words(first, count, word):
-            for tile, (start, size) in zip(pairs, PAIR_TILES):
-                if start <= first < start + size:
-                    words = tile[:].rearrange("p u r e -> p (u r e)").bitcast(word).rearrange("p (u r) -> p r u", u=2)
-                    return words[:, (first - start) * P : (first - start + count) * P]
 
         for n, (t, first, count) in enumerate(pieces):
             if n >= len(FIRST_PIECES):
@@ -180,26 +161,43 @@ def tile_picked_devox_none_p_kernel(tc, x_words, x_scales, w1, w2, gate, emb, of
             staged = keep.tile([P, count], F32, name=f"h_sb{n}")
             nc.scalar.activation(staged[:], accs[n][:, :count], RELU)
             nc.vector.tensor_copy(windows[t][:].indirect(entries(cell_t, first, count)), staged[:])
-            if first + count == S and not last:
-                add_emb_early(t)
 
-        add_emb_last(SLOT_ORDER[-1])
+        sums = [bank((6 + q) % 8, f"zt{q}") for q in range(len(PAIR_TILES))]
+        steps = [(emb_tiles, t) for t in SLOT_ORDER[:2]] + [(windows, t) for t in SLOT_ORDER[:2]]
+        for n, (tiles, t) in enumerate(steps):
+            for acc, (first, count) in zip(sums, PAIR_TILES):
+                for b in range(count):
+                    nc.tensor.matmul(
+                        acc[:, (2 * b + t % 2) * P : (2 * b + t % 2 + 1) * P],
+                        tiles[t][:, (first + b) * P : (first + b + 1) * P],
+                        ident[:],
+                        start=(n == 0 and b == 0),
+                        stop=(n == len(steps) - 1 and b == count - 1),
+                        is_transpose=True,
+                    )
+        for q, (first, count) in enumerate(PAIR_TILES):
+            rows = keep.tile([P, count, P, 2], BF16, name=f"z_rows{q}")
+            nc.scalar.copy(rows[:], sums[q][:].rearrange("r (b e p) -> r b p e", b=count, e=2))
+            words = rows[:].rearrange("r b p e -> r (b p e)").bitcast(F32)
+            back = bank(2 + q, f"zw{q}")
+            for b in range(count):
+                nc.tensor.transpose(back[:, b * P : (b + 1) * P], words[:, b * P : (b + 1) * P], ident[:])
+            nc.scalar.copy(pairs[q][:, 1].rearrange("p r e -> p (r e)").bitcast(F32), back[:, : count * P])
 
-        z_grouped = []
-        for q, (first, count) in enumerate(CELL_CHUNKS):
-            grouped = keep.tile([P, count * P * PACK], BF16, name=f"z_grouped{q}", align_bytes=64)
-            word = U32 if q < WOVEN_BY_SCALAR else I32
-            dst = grouped[:].bitcast(word).rearrange("p (r u) -> p r u", u=2)
-            src = pair_words(first, count, word)
-            if q < WOVEN_BY_SCALAR:
-                nc.scalar.copy(dst, src)
-            else:
-                nc.vector.tensor_copy(dst, src)
-            z_grouped.append(grouped)
+        own = windows[0][:].rearrange("p (e c i) -> p c e i", e=2, i=4)
+        other = windows[1][:].rearrange("p (e c i) -> p c e i", e=2, i=4)[:, :, ::-1, :]
+        for tile, (first, count) in zip(pairs, PAIR_TILES):
+            quads = slice(first * P // 4, (first + count) * P // 4)
+            nc.vector.tensor_tensor(tile[:, 0].rearrange("p (c i) e -> p c e i", i=4), own[:, quads], other[:, quads], ADD)
+
+        z_grouped = keep.tile([P, U * PACK], BF16, name="z_grouped", align_bytes=64)
+        for tile, (first, count) in zip(pairs, PAIR_TILES):
+            dst = z_grouped[:, first * P * PACK : (first + count) * P * PACK].bitcast(U32).rearrange("p (r u) -> p r u", u=2)
+            nc.scalar.copy(dst, tile[:].rearrange("p u r e -> p (u r e)").bitcast(U32).rearrange("p (u r) -> p r u", u=2))
 
         y = keep.tile([P, U], F32, name="y")
         for q, (first, count) in enumerate(CELL_CHUNKS):
-            codes, scales = quantize(z_grouped[q][:], count * P, f"zq{q}")
+            codes, scales = quantize(z_grouped[:, first * P * PACK : (first + count) * P * PACK], count * P, f"zq{q}")
             acc = bank((6 + q) % 8, f"y{q}")
             nc.tensor.matmul_mx(
                 out=acc[:, : count * P],
@@ -210,7 +208,7 @@ def tile_picked_devox_none_p_kernel(tc, x_words, x_scales, w1, w2, gate, emb, of
                 start=True,
                 stop=True,
             )
-            if q < 3:
+            if q < COPIED_BY_SCALAR:
                 nc.scalar.copy(y[:, first * P : (first + count) * P], acc[:, : count * P])
             else:
                 nc.vector.tensor_copy(y[:, first * P : (first + count) * P], acc[:, : count * P])

@@ -24,11 +24,11 @@ K_PASS = P * PACK
 PASSES = K // K_PASS
 LIST_COLS = S // 16
 CELL_BLOCKS = U // P
-SLOT_ORDER = (2, 3, 0, 1)
-FIRST_PIECES = ((0, 128), (128, 128), (256, 256))
+HALF_H = H // 2
+HALF_P = P // 2
+QUARTER = S // 4
+PAIR_BLOCKS = 2
 CELL_CHUNKS = ((0, 2), (2, 2), (4, 2), (6, 1), (7, 1))
-PAIR_TILES = ((0, 2), (2, 2), (4, 2), (6, 2))
-CAST_BY_SCALAR = (128, 56)
 COPIED_BY_SCALAR = 3
 OUT_PIECES = ((0, 256), (256, 256))
 
@@ -55,6 +55,12 @@ def tile_picked_devox_none_p_kernel(tc, x_words, x_scales, w1, w2, gate, emb, of
             nc.sync.dma_start(out=tile[:], in_=x_words[g].rearrange("p n t -> p (n t)").bitcast(I32))
             return tile
 
+        def load_w1(g, half):
+            raw = keep.tile([P, PACK, HALF_H], F32, name=f"w1_raw{g}_{half}", tag=f"w1_raw{g}_{half}")
+            rows = w1[g * K_PASS : (g + 1) * K_PASS, half * HALF_H : (half + 1) * HALF_H]
+            nc.sync.dma_start(out=raw[:], in_=rows.rearrange("(p j) c -> p j c", j=PACK))
+            return raw
+
         def quantize(grouped_flat, width, name):
             codes = keep.tile([P, width], U32, name=name + "_codes", align_bytes=64)
             scales = keep.tile([P, width], U8, name=name + "_scales", align_bytes=64)
@@ -67,138 +73,170 @@ def tile_picked_devox_none_p_kernel(tc, x_words, x_scales, w1, w2, gate, emb, of
         offs_t = load_list(offs, "offs_t")
         cell_t = load_list(cell, "cell_t")
         pos_t = [load_list(pos1, "pos1_t"), load_list(pos2, "pos2_t")]
-        w1_raw = []
-        x_tiles = []
+        w1_raw = {(0, 0): load_w1(0, 0)}
+        for q in range(4):
+            nc.sync.dma_start(
+                out=x_scale_rows[32 * q : 32 * q + 4 * PASSES].bitcast(I32),
+                in_=x_scales[:, 4 * q : 4 * q + 4, :].bitcast(I32),
+            )
+        x_tiles = [load_words(0)]
+        w1_raw[1, 0] = load_w1(1, 0)
+        x_tiles.append(load_words(1))
         for g in range(PASSES):
-            raw = keep.tile([P, PACK, H], F32, name=f"w1_raw{g}")
-            nc.sync.dma_start(out=raw[:], in_=w1[g * K_PASS : (g + 1) * K_PASS, :].rearrange("(p j) c -> p j c", j=PACK))
-            w1_raw.append(raw)
-            if g == 0:
-                for q in range(4):
-                    nc.sync.dma_start(
-                        out=x_scale_rows[32 * q : 32 * q + 4 * PASSES].bitcast(I32),
-                        in_=x_scales[:, 4 * q : 4 * q + 4, :].bitcast(I32),
-                    )
-            x_tiles.append(load_words(g))
+            w1_raw[g, 1] = load_w1(g, 1)
+
+        emb_rows = emb.rearrange("(p t) u -> p t u", t=PACK)
+        upper_emb, upper_windows, lower_windows = [], [], []
+        for half in range(2):
+            tile = keep.tile([P, U], F32, name=f"upper_emb{half}")
+            nc.sync.dma_start(out=tile[:], in_=emb_rows[half * HALF_P : (half + 1) * HALF_P, 2:4, :])
+            upper_emb.append(tile)
+            upper_windows.append(keep.tile([P, U], F32, name=f"upper_window{half}"))
+            tile = keep.tile([P, 2 * U], F32, name=f"lower_window{half}")
+            nc.sync.dma_start(out=tile[:, U:], in_=emb_rows[:, 1 - half, :])
+            lower_windows.append(tile)
         w2_raw = keep.tile([P, PACK, N], F32, name="w2_raw")
         nc.sync.dma_start(out=w2_raw[:], in_=w2.rearrange("(p j) n -> p j n", j=PACK))
-        emb_rows = emb.rearrange("(p t) u -> p t u", t=PACK)
-        emb_tiles = {}
-        windows = {}
-        for t in SLOT_ORDER[:2]:
-            emb_tiles[t] = keep.tile([P, U], F32, name=f"emb{t}")
-            nc.sync.dma_start(out=emb_tiles[t][:], in_=emb_rows[:, t, :])
-            windows[t] = keep.tile([P, U], F32, name=f"window{t}")
-        for t in SLOT_ORDER[2:]:
-            windows[t] = keep.tile([P, 2 * U], F32, name=f"window{t}")
-            nc.sync.dma_start(out=windows[t][:, U:], in_=emb_rows[:, 1 - t, :])
         gate_t = keep.tile([P, 2, V], F32, name="gate_t")
         nc.sync.dma_start(out=gate_t[:], in_=gate.rearrange("d p v -> p d v"))
 
         ident = keep.tile([P, P], F32, name="ident")
         make_identity(nc, ident[:])
-        for n, t in enumerate(SLOT_ORDER):
-            (nc.vector if n < 2 else nc.gpsimd).memset(windows[t][:, :U].bitcast(I32), 0)
+        for half in range(2):
+            nc.vector.memset(upper_windows[half][:].bitcast(I32), 0)
+            nc.gpsimd.memset(lower_windows[half][:, :U].bitcast(I32), 0)
+
+        upper_grouped = [keep.tile([P, PASSES, P, PACK], BF16, name=f"upper_grouped{half}", align_bytes=64) for half in range(2)]
+        lower_grouped = keep.tile([P, PASSES, 2, P, PACK], BF16, name="lower_grouped", align_bytes=64)
+
+        def cast_upper(g, half):
+            nc.scalar.activation(
+                upper_grouped[half][:, g].rearrange("p (m e) j -> p m j e", e=2),
+                w1_raw[g, half][:].rearrange("p j (m t) -> p m j t", t=PACK)[:, :, :, 2:4],
+                COPY,
+            )
+
+        def cast_lower(g, half):
+            nc.scalar.activation(
+                lower_grouped[:, g, :, half * HALF_P : (half + 1) * HALF_P, :].rearrange("p t m j -> p m j t"),
+                w1_raw[g, half][:].rearrange("p j (m t) -> p m j t", t=PACK)[:, :, :, 0:2],
+                COPY,
+            )
 
         xg_scales = keep.tile([P, S], U8, name="xg_scales", align_bytes=64)
         nc.vector.tensor_copy(xg_scales[:], x_scale_rows[:].indirect(offs_t[:]))
-        xg_first = keep.tile([P, S], U32, name="xg_first", align_bytes=64)
-        nc.vector.tensor_copy(xg_first[:], x_tiles[0][:].bitcast(U32).indirect(offs_t[:]))
+        xg = [keep.tile([P, S], U32, name=f"xg{g}", align_bytes=64) for g in range(PASSES)]
 
-        w1q = []
-        for g in range(PASSES):
-            grouped = keep.tile([P, PACK, P, PACK], BF16, name=f"w1_grouped{g}", align_bytes=64)
-            dst = grouped[:].rearrange("p t m j -> p m t j")
-            src = w1_raw[g][:].rearrange("p j (m t) -> p m t j", t=PACK)
-            share = CAST_BY_SCALAR[g]
-            nc.scalar.activation(dst[:, :share], src[:, :share], COPY)
-            if share < P:
-                nc.vector.tensor_copy(dst[:, share:], src[:, share:])
-            w1q.append(quantize(grouped[:].rearrange("p t m j -> p (t m j)"), H, f"w1q{g}"))
-
-        pieces = [(SLOT_ORDER[0], first, count) for first, count in FIRST_PIECES]
-        pieces.extend((t, 0, S) for t in SLOT_ORDER[1:])
-        accs = [bank(n, f"h{n}") for n in range(len(pieces))]
-
-        def first_product(n, g, words):
-            t, first, count = pieces[n]
-            codes, scales = w1q[g]
+        def product(acc, weights, column, g, first, count):
+            codes, scales = weights
             nc.tensor.matmul_mx(
-                out=accs[n][:, :count],
-                lhsT=codes[:, t * P : (t + 1) * P].bitcast(FP8X4),
-                lhsT_scale=scales[:, t * P : (t + 1) * P],
-                rhs=words[:, first : first + count].bitcast(FP8X4),
+                out=acc[:, :count],
+                lhsT=codes[:, column : column + P].bitcast(FP8X4),
+                lhsT_scale=scales[:, column : column + P],
+                rhs=xg[g][:, first : first + count].bitcast(FP8X4),
                 rhs_scale=xg_scales[4 * g :, first : first + count],
                 start=(g == 0),
                 stop=(g == PASSES - 1),
             )
 
-        for n in range(len(FIRST_PIECES)):
-            first_product(n, 0, xg_first)
+        def relu(parts, name, tag=None):
+            staged = keep.tile([P, sum(count for acc, count in parts)], F32, name=name, tag=tag or name)
+            column = 0
+            for acc, count in parts:
+                nc.scalar.activation(staged[:, column : column + count], acc[:, :count], RELU)
+                column = column + count
+            return staged
 
-        xg_second = keep.tile([P, S], U32, name="xg_second", align_bytes=64)
-        for half in range(2):
-            nc.vector.tensor_copy(
-                xg_second[:, half * S // 2 : (half + 1) * S // 2],
-                x_tiles[1][:].bitcast(U32).indirect(entries(offs_t, half * S // 2, S // 2)),
-            )
+        def scatter(window, first, staged):
+            nc.vector.tensor_copy(window[:].indirect(entries(cell_t, first, staged.shape[1])), staged[:])
 
-        pairs = [keep.tile([P, 2, count * P, 2], BF16, name=f"pairs{first}") for first, count in PAIR_TILES]
+        first_groups = ((0, QUARTER), (QUARTER, 2 * QUARTER), (3 * QUARTER, QUARTER))
+        first_accs = [bank(n, f"h_first{n}") for n in range(len(first_groups))]
+        first_weights = []
+        for g in range(PASSES):
+            cast_upper(g, 0)
+            first_weights.append(quantize(upper_grouped[0][:, g].rearrange("p m j -> p (m j)"), P, f"w1_first{g}"))
+            if g == 0:
+                nc.vector.tensor_copy(xg[0][:], x_tiles[0][:].bitcast(U32).indirect(offs_t[:]))
+            else:
+                for half in range(2):
+                    nc.vector.tensor_copy(
+                        xg[1][:, half * S // 2 : (half + 1) * S // 2],
+                        x_tiles[1][:].bitcast(U32).indirect(entries(offs_t, half * S // 2, S // 2)),
+                    )
+            for acc, (first, count) in zip(first_accs, first_groups):
+                product(acc, first_weights[g], 0, g, first, count)
+            cast_lower(g, 0)
+        for n in range(2):
+            first, count = first_groups[n]
+            scatter(upper_windows[0], first, relu([(first_accs[n], count)], f"h_sb_first{n}"))
 
-        for n, (t, first, count) in enumerate(pieces):
-            if n >= len(FIRST_PIECES):
-                first_product(n, 0, xg_first)
-            first_product(n, 1, xg_second)
-            last = n == len(pieces) - 1
-            if last:
-                w2_grouped = keep.tile([P, N, PACK], BF16, name="w2_grouped", align_bytes=64)
-                nc.scalar.activation(
-                    w2_grouped[:].rearrange("p (c i) j -> p c j i", i=4),
-                    w2_raw[:].rearrange("p j (c i) -> p c j i", i=4),
-                    COPY,
-                )
-                w2_codes, w2_scales = quantize(w2_grouped[:].rearrange("p c j -> p (c j)"), N, "w2q")
-            staged = keep.tile([P, count], F32, name=f"h_sb{n}")
-            nc.scalar.activation(staged[:], accs[n][:, :count], RELU)
-            nc.vector.tensor_copy(windows[t][:].indirect(entries(cell_t, first, count)), staged[:])
+        for g in range(PASSES):
+            cast_upper(g, 1)
+            cast_lower(g, 1)
+        second_weights = quantize(upper_grouped[1][:].rearrange("p g m j -> p (g m j)"), PASSES * P, "w1_second")
+        lower_weights = quantize(lower_grouped[:].rearrange("p g t m j -> p (g t m j)"), PASSES * 2 * P, "w1_lower")
+        scatter(upper_windows[0], 3 * QUARTER, relu([(first_accs[2], QUARTER)], "h_sb_first2", tag="w1_raw1_1"))
 
-        sums = [bank((6 + q) % 8, f"zt{q}") for q in range(len(PAIR_TILES))]
-        steps = [(emb_tiles, t) for t in SLOT_ORDER[:2]] + [(windows, t) for t in SLOT_ORDER[:2]]
-        for n, (tiles, t) in enumerate(steps):
-            for acc, (first, count) in zip(sums, PAIR_TILES):
-                for b in range(count):
+        second_accs = [bank(3 + n, f"h_second{n}") for n in range(2)]
+        for n, acc in enumerate(second_accs):
+            for g in range(PASSES):
+                product(acc, second_weights, g * P, g, n * S // 2, S // 2)
+        scatter(upper_windows[1], 0, relu([(acc, S // 2) for acc in second_accs], "h_sb_second"))
+        for t in range(2):
+            acc = bank(5 + t, f"h_lower{t}")
+            for g in range(PASSES):
+                product(acc, lower_weights, (2 * g + t) * P, g, 0, S)
+            scatter(lower_windows[t], 0, relu([(acc, S)], f"h_sb_lower{t}"))
+
+        w2_grouped = keep.tile([P, N, PACK], BF16, name="w2_grouped", align_bytes=64)
+        nc.scalar.activation(
+            w2_grouped[:].rearrange("p (c i) j -> p c j i", i=4),
+            w2_raw[:].rearrange("p j (c i) -> p c j i", i=4),
+            COPY,
+        )
+        w2_codes, w2_scales = quantize(w2_grouped[:].rearrange("p c j -> p (c j)"), N, "w2q")
+
+        groups = CELL_BLOCKS // PAIR_BLOCKS
+        width = PAIR_BLOCKS * P
+        pairs = [keep.tile([P, 2, width, 2], BF16, name=f"pairs{q}") for q in range(groups)]
+        sums = [bank(3 + q, f"zt{q}") for q in range(groups)]
+        steps = [(upper_emb, 0), (upper_windows, 0), (upper_emb, 1), (upper_windows, 1)]
+        for n, (tiles, half) in enumerate(steps):
+            for q in range(groups):
+                for b in range(PAIR_BLOCKS):
                     nc.tensor.matmul(
-                        acc[:, (2 * b + t % 2) * P : (2 * b + t % 2 + 1) * P],
-                        tiles[t][:, (first + b) * P : (first + b + 1) * P],
+                        sums[q][:, (2 * b + half) * P : (2 * b + half + 1) * P],
+                        tiles[half][:, q * width + b * P : q * width + (b + 1) * P],
                         ident[:],
                         start=(n == 0 and b == 0),
-                        stop=(n == len(steps) - 1 and b == count - 1),
+                        stop=(n == len(steps) - 1 and b == PAIR_BLOCKS - 1),
                         is_transpose=True,
                     )
-        for q, (first, count) in enumerate(PAIR_TILES):
-            rows = keep.tile([P, count, P, 2], BF16, name=f"z_rows{q}")
-            nc.scalar.copy(rows[:], sums[q][:].rearrange("r (b e p) -> r b p e", b=count, e=2))
-            words = rows[:].rearrange("r b p e -> r (b p e)").bitcast(F32)
-            back = bank(2 + q, f"zw{q}")
-            for b in range(count):
+        for q in range(groups):
+            rows = keep.tile([P, 2 * width], BF16, name=f"z_rows{q}")
+            nc.scalar.copy(rows[:], sums[q][:])
+            words = rows[:].bitcast(F32)
+            back = bank((7 + q) % 8, f"zw{q}")
+            for b in range(PAIR_BLOCKS):
                 nc.tensor.transpose(back[:, b * P : (b + 1) * P], words[:, b * P : (b + 1) * P], ident[:])
-            nc.scalar.copy(pairs[q][:, 1].rearrange("p r e -> p (r e)").bitcast(F32), back[:, : count * P])
+            nc.scalar.copy(pairs[q][:, 1].rearrange("p r e -> p (r e)").bitcast(F32), back[:, :width])
 
-        own = windows[0][:].rearrange("p (e c i) -> p c e i", e=2, i=4)
-        other = windows[1][:].rearrange("p (e c i) -> p c e i", e=2, i=4)[:, :, ::-1, :]
-        for tile, (first, count) in zip(pairs, PAIR_TILES):
-            quads = slice(first * P // 4, (first + count) * P // 4)
-            nc.vector.tensor_tensor(tile[:, 0].rearrange("p (c i) e -> p c e i", i=4), own[:, quads], other[:, quads], ADD)
+        own = lower_windows[0][:].rearrange("p (e c i) -> p c e i", e=2, i=4)
+        other = lower_windows[1][:].rearrange("p (e c i) -> p c e i", e=2, i=4)[:, :, ::-1, :]
+        for q in range(groups):
+            quads = slice(q * width // 4, (q + 1) * width // 4)
+            nc.vector.tensor_tensor(pairs[q][:, 0].rearrange("p (c i) e -> p c e i", i=4), own[:, quads], other[:, quads], ADD)
 
         z_grouped = keep.tile([P, U * PACK], BF16, name="z_grouped", align_bytes=64)
-        for tile, (first, count) in zip(pairs, PAIR_TILES):
-            dst = z_grouped[:, first * P * PACK : (first + count) * P * PACK].bitcast(U32).rearrange("p (r u) -> p r u", u=2)
-            nc.scalar.copy(dst, tile[:].rearrange("p u r e -> p (u r e)").bitcast(U32).rearrange("p (u r) -> p r u", u=2))
+        for q in range(groups):
+            dst = z_grouped[:, q * width * PACK : (q + 1) * width * PACK].bitcast(U32).rearrange("p (r u) -> p r u", u=2)
+            nc.scalar.copy(dst, pairs[q][:].rearrange("p u r e -> p (u r e)").bitcast(U32).rearrange("p (u r) -> p r u", u=2))
 
         y = keep.tile([P, U], F32, name="y")
         for q, (first, count) in enumerate(CELL_CHUNKS):
             codes, scales = quantize(z_grouped[:, first * P * PACK : (first + count) * P * PACK], count * P, f"zq{q}")
-            acc = bank((6 + q) % 8, f"y{q}")
+            acc = bank(3 + q, f"y{q}")
             nc.tensor.matmul_mx(
                 out=acc[:, : count * P],
                 lhsT=w2_codes[:].bitcast(FP8X4),

@@ -28,9 +28,10 @@ HALF_H = H // 2
 HALF_P = P // 2
 QUARTER = S // 4
 PAIR_BLOCKS = 2
+BANK_BLOCKS = 4
 CELL_CHUNKS = ((0, 2), (2, 2), (4, 2), (6, 1), (7, 1))
 COPIED_BY_SCALAR = 3
-OUT_PIECES = ((0, 256), (256, 256))
+OUT_PIECES = ((0, 384), (384, 128))
 
 
 def tile_picked_devox_none_p_kernel(tc, x_words, x_scales, w1, w2, gate, emb, offs, cell, pos1, pos2, out):
@@ -55,11 +56,11 @@ def tile_picked_devox_none_p_kernel(tc, x_words, x_scales, w1, w2, gate, emb, of
             nc.sync.dma_start(out=tile[:], in_=x_words[g].rearrange("p n t -> p (n t)").bitcast(I32))
             return tile
 
-        def load_w1(g, half):
-            raw = keep.tile([P, PACK, HALF_H], F32, name=f"w1_raw{g}_{half}", tag=f"w1_raw{g}_{half}")
-            rows = w1[g * K_PASS : (g + 1) * K_PASS, half * HALF_H : (half + 1) * HALF_H]
+        def load_w1(g, first, count):
+            raw = keep.tile([P, PACK, count], F32, name=f"w1_raw{g}_{first}", tag=f"w1_raw{g}_{first}")
+            rows = w1[g * K_PASS : (g + 1) * K_PASS, first : first + count]
             nc.sync.dma_start(out=raw[:], in_=rows.rearrange("(p j) c -> p j c", j=PACK))
-            return raw
+            return raw[:].rearrange("p j (m t) -> p m j t", t=PACK)
 
         def quantize(grouped_flat, width, name):
             codes = keep.tile([P, width], U32, name=name + "_codes", align_bytes=64)
@@ -73,17 +74,17 @@ def tile_picked_devox_none_p_kernel(tc, x_words, x_scales, w1, w2, gate, emb, of
         offs_t = load_list(offs, "offs_t")
         cell_t = load_list(cell, "cell_t")
         pos_t = [load_list(pos1, "pos1_t"), load_list(pos2, "pos2_t")]
-        w1_raw = {(0, 0): load_w1(0, 0)}
+        whole = load_w1(0, 0, H)
+        w1_raw = {(0, half): whole[:, half * HALF_P : (half + 1) * HALF_P] for half in range(2)}
         for q in range(4):
             nc.sync.dma_start(
                 out=x_scale_rows[32 * q : 32 * q + 4 * PASSES].bitcast(I32),
                 in_=x_scales[:, 4 * q : 4 * q + 4, :].bitcast(I32),
             )
         x_tiles = [load_words(0)]
-        w1_raw[1, 0] = load_w1(1, 0)
+        w1_raw[1, 0] = load_w1(1, 0, HALF_H)
         x_tiles.append(load_words(1))
-        for g in range(PASSES):
-            w1_raw[g, 1] = load_w1(g, 1)
+        w1_raw[1, 1] = load_w1(1, HALF_H, HALF_H)
 
         emb_rows = emb.rearrange("(p t) u -> p t u", t=PACK)
         upper_emb, upper_windows, lower_windows = [], [], []
@@ -92,6 +93,7 @@ def tile_picked_devox_none_p_kernel(tc, x_words, x_scales, w1, w2, gate, emb, of
             nc.sync.dma_start(out=tile[:], in_=emb_rows[half * HALF_P : (half + 1) * HALF_P, 2:4, :])
             upper_emb.append(tile)
             upper_windows.append(keep.tile([P, U], F32, name=f"upper_window{half}"))
+        for half in range(2):
             tile = keep.tile([P, 2 * U], F32, name=f"lower_window{half}")
             nc.sync.dma_start(out=tile[:, U:], in_=emb_rows[:, 1 - half, :])
             lower_windows.append(tile)
@@ -106,20 +108,20 @@ def tile_picked_devox_none_p_kernel(tc, x_words, x_scales, w1, w2, gate, emb, of
             nc.vector.memset(upper_windows[half][:].bitcast(I32), 0)
             nc.gpsimd.memset(lower_windows[half][:, :U].bitcast(I32), 0)
 
-        upper_grouped = [keep.tile([P, PASSES, P, PACK], BF16, name=f"upper_grouped{half}", align_bytes=64) for half in range(2)]
-        lower_grouped = keep.tile([P, PASSES, 2, P, PACK], BF16, name="lower_grouped", align_bytes=64)
+        upper_grouped = [keep.tile([P, 2, P, PACK], BF16, name=f"upper_grouped{g}", align_bytes=64) for g in range(PASSES)]
+        lower_grouped = [keep.tile([P, 2, P, PACK], BF16, name=f"lower_grouped{g}", align_bytes=64) for g in range(PASSES)]
 
         def cast_upper(g, half):
             nc.scalar.activation(
-                upper_grouped[half][:, g].rearrange("p (m e) j -> p m j e", e=2),
-                w1_raw[g, half][:].rearrange("p j (m t) -> p m j t", t=PACK)[:, :, :, 2:4],
+                upper_grouped[g][:, half].rearrange("p (m e) j -> p m j e", e=2),
+                w1_raw[g, half][:, :, :, 2:4],
                 COPY,
             )
 
         def cast_lower(g, half):
             nc.scalar.activation(
-                lower_grouped[:, g, :, half * HALF_P : (half + 1) * HALF_P, :].rearrange("p t m j -> p m j t"),
-                w1_raw[g, half][:].rearrange("p j (m t) -> p m j t", t=PACK)[:, :, :, 0:2],
+                lower_grouped[g][:, :, half * HALF_P : (half + 1) * HALF_P, :].rearrange("p t m j -> p m j t"),
+                w1_raw[g, half][:, :, :, 0:2],
                 COPY,
             )
 
@@ -140,11 +142,11 @@ def tile_picked_devox_none_p_kernel(tc, x_words, x_scales, w1, w2, gate, emb, of
             )
 
         def relu(parts, name, tag=None):
-            staged = keep.tile([P, sum(count for acc, count in parts)], F32, name=name, tag=tag or name)
+            staged = keep.tile([P, sum(part.shape[1] for part in parts)], F32, name=name, tag=tag or name)
             column = 0
-            for acc, count in parts:
-                nc.scalar.activation(staged[:, column : column + count], acc[:, :count], RELU)
-                column = column + count
+            for part in parts:
+                nc.scalar.activation(staged[:, column : column + part.shape[1]], part, RELU)
+                column = column + part.shape[1]
             return staged
 
         def scatter(window, first, staged):
@@ -152,42 +154,55 @@ def tile_picked_devox_none_p_kernel(tc, x_words, x_scales, w1, w2, gate, emb, of
 
         first_groups = ((0, QUARTER), (QUARTER, 2 * QUARTER), (3 * QUARTER, QUARTER))
         first_accs = [bank(n, f"h_first{n}") for n in range(len(first_groups))]
-        first_weights = []
-        for g in range(PASSES):
-            cast_upper(g, 0)
-            first_weights.append(quantize(upper_grouped[0][:, g].rearrange("p m j -> p (m j)"), P, f"w1_first{g}"))
-            if g == 0:
-                nc.vector.tensor_copy(xg[0][:], x_tiles[0][:].bitcast(U32).indirect(offs_t[:]))
-            else:
-                for half in range(2):
-                    nc.vector.tensor_copy(
-                        xg[1][:, half * S // 2 : (half + 1) * S // 2],
-                        x_tiles[1][:].bitcast(U32).indirect(entries(offs_t, half * S // 2, S // 2)),
-                    )
-            for acc, (first, count) in zip(first_accs, first_groups):
-                product(acc, first_weights[g], 0, g, first, count)
-            cast_lower(g, 0)
+        second_accs = [bank(3 + n, f"h_second{n}") for n in range(2)]
+        lower_accs = [bank(5 + t, f"h_lower{t}") for t in range(2)]
+
+        def quantize_upper(g, half):
+            cast_upper(g, half)
+            return quantize(upper_grouped[g][:, half].rearrange("p m j -> p (m j)"), P, f"w1_upper{g}_{half}")
+
+        def quantize_lower(g):
+            return quantize(lower_grouped[g][:].rearrange("p t m j -> p (t m j)"), 2 * P, f"w1_lower{g}")
+
+        weights = quantize_upper(0, 0)
+        nc.vector.tensor_copy(xg[0][:], x_tiles[0][:].bitcast(U32).indirect(offs_t[:]))
+        for acc, (first, count) in zip(first_accs, first_groups):
+            product(acc, weights, 0, 0, first, count)
+        weights = quantize_upper(0, 1)
+        for n, acc in enumerate(second_accs):
+            product(acc, weights, 0, 0, n * S // 2, S // 2)
+        for half in range(2):
+            cast_lower(0, half)
+        weights = quantize_lower(0)
+        for t, acc in enumerate(lower_accs):
+            product(acc, weights, t * P, 0, 0, S)
+
+        weights = quantize_upper(1, 0)
+        for half in range(2):
+            nc.vector.tensor_copy(
+                xg[1][:, half * S // 2 : (half + 1) * S // 2],
+                x_tiles[1][:].bitcast(U32).indirect(entries(offs_t, half * S // 2, S // 2)),
+            )
+        for acc, (first, count) in zip(first_accs, first_groups):
+            product(acc, weights, 0, 1, first, count)
+        cast_lower(1, 0)
         for n in range(2):
             first, count = first_groups[n]
-            scatter(upper_windows[0], first, relu([(first_accs[n], count)], f"h_sb_first{n}"))
+            scatter(upper_windows[0], first, relu([first_accs[n][:, :count]], f"h_sb_first{n}"))
 
-        for g in range(PASSES):
-            cast_upper(g, 1)
-            cast_lower(g, 1)
-        second_weights = quantize(upper_grouped[1][:].rearrange("p g m j -> p (g m j)"), PASSES * P, "w1_second")
-        lower_weights = quantize(lower_grouped[:].rearrange("p g t m j -> p (g t m j)"), PASSES * 2 * P, "w1_lower")
-        scatter(upper_windows[0], 3 * QUARTER, relu([(first_accs[2], QUARTER)], "h_sb_first2", tag="w1_raw1_1"))
+        second_weights = quantize_upper(1, 1)
+        cast_lower(1, 1)
+        lower_weights = quantize_lower(1)
+        scatter(upper_windows[0], 3 * QUARTER, relu([first_accs[2][:, :QUARTER]], "h_sb_first2", tag=f"w1_raw1_{HALF_H}"))
 
-        second_accs = [bank(3 + n, f"h_second{n}") for n in range(2)]
         for n, acc in enumerate(second_accs):
-            for g in range(PASSES):
-                product(acc, second_weights, g * P, g, n * S // 2, S // 2)
-        scatter(upper_windows[1], 0, relu([(acc, S // 2) for acc in second_accs], "h_sb_second"))
-        for t in range(2):
-            acc = bank(5 + t, f"h_lower{t}")
-            for g in range(PASSES):
-                product(acc, lower_weights, (2 * g + t) * P, g, 0, S)
-            scatter(lower_windows[t], 0, relu([(acc, S)], f"h_sb_lower{t}"))
+            product(acc, second_weights, 0, 1, n * S // 2, S // 2)
+        scatter(upper_windows[1], 0, relu([second_accs[0][:, :QUARTER]], "h_sb_second0"))
+        rest = [second_accs[0][:, QUARTER : 2 * QUARTER], second_accs[1][:, : 2 * QUARTER]]
+        scatter(upper_windows[1], QUARTER, relu(rest, "h_sb_second1"))
+        for t, acc in enumerate(lower_accs):
+            product(acc, lower_weights, t * P, 1, 0, S)
+            scatter(lower_windows[t], 0, relu([acc[:]], f"h_sb_lower{t}"))
 
         w2_grouped = keep.tile([P, N, PACK], BF16, name="w2_grouped", align_bytes=64)
         nc.scalar.activation(
@@ -200,26 +215,29 @@ def tile_picked_devox_none_p_kernel(tc, x_words, x_scales, w1, w2, gate, emb, of
         groups = CELL_BLOCKS // PAIR_BLOCKS
         width = PAIR_BLOCKS * P
         pairs = [keep.tile([P, 2, width, 2], BF16, name=f"pairs{q}") for q in range(groups)]
-        sums = [bank(3 + q, f"zt{q}") for q in range(groups)]
-        steps = [(upper_emb, 0), (upper_windows, 0), (upper_emb, 1), (upper_windows, 1)]
-        for n, (tiles, half) in enumerate(steps):
-            for q in range(groups):
-                for b in range(PAIR_BLOCKS):
-                    nc.tensor.matmul(
-                        sums[q][:, (2 * b + half) * P : (2 * b + half + 1) * P],
-                        tiles[half][:, q * width + b * P : q * width + (b + 1) * P],
-                        ident[:],
-                        start=(n == 0 and b == 0),
-                        stop=(n == len(steps) - 1 and b == PAIR_BLOCKS - 1),
-                        is_transpose=True,
-                    )
+        rows = [keep.tile([P, BANK_BLOCKS, 2, P], BF16, name=f"z_rows{side}") for side in range(2)]
+        for half in range(2):
+            sums = [bank((7 + 2 * half + side) % 8, f"zt{half}_{side}") for side in range(2)]
+            for n, tile in enumerate((upper_emb[half], upper_windows[half])):
+                for side in range(2):
+                    for b in range(BANK_BLOCKS):
+                        column = (side * BANK_BLOCKS + b) * P
+                        nc.tensor.matmul(
+                            sums[side][:, b * P : (b + 1) * P],
+                            tile[:, column : column + P],
+                            ident[:],
+                            start=(n == 0 and b == 0),
+                            stop=(n == 1 and b == BANK_BLOCKS - 1),
+                            is_transpose=True,
+                        )
+            for side in range(2):
+                nc.scalar.copy(rows[side][:, :, half, :], sums[side][:].rearrange("r (b c) -> r b c", b=BANK_BLOCKS))
         for q in range(groups):
-            rows = keep.tile([P, 2 * width], BF16, name=f"z_rows{q}")
-            nc.scalar.copy(rows[:], sums[q][:])
-            words = rows[:].bitcast(F32)
-            back = bank((7 + q) % 8, f"zw{q}")
+            side, first = divmod(q * PAIR_BLOCKS, BANK_BLOCKS)
+            words = rows[side][:].rearrange("r b h c -> r (b h c)").bitcast(F32)
+            back = bank(3 + q, f"zw{q}")
             for b in range(PAIR_BLOCKS):
-                nc.tensor.transpose(back[:, b * P : (b + 1) * P], words[:, b * P : (b + 1) * P], ident[:])
+                nc.tensor.transpose(back[:, b * P : (b + 1) * P], words[:, (first + b) * P : (first + b + 1) * P], ident[:])
             nc.scalar.copy(pairs[q][:, 1].rearrange("p r e -> p (r e)").bitcast(F32), back[:, :width])
 
         own = lower_windows[0][:].rearrange("p (e c i) -> p c e i", e=2, i=4)
@@ -230,13 +248,13 @@ def tile_picked_devox_none_p_kernel(tc, x_words, x_scales, w1, w2, gate, emb, of
 
         z_grouped = keep.tile([P, U * PACK], BF16, name="z_grouped", align_bytes=64)
         for q in range(groups):
-            dst = z_grouped[:, q * width * PACK : (q + 1) * width * PACK].bitcast(U32).rearrange("p (r u) -> p r u", u=2)
-            nc.scalar.copy(dst, pairs[q][:].rearrange("p u r e -> p (u r e)").bitcast(U32).rearrange("p (u r) -> p r u", u=2))
+            dst = z_grouped[:, q * width * PACK : (q + 1) * width * PACK].bitcast(U32).rearrange("p (c i u) -> p c u i", i=2, u=2)
+            nc.scalar.copy(dst, pairs[q][:].rearrange("p u r e -> p (u r e)").bitcast(U32).rearrange("p (u c i) -> p c u i", u=2, i=2))
 
         y = keep.tile([P, U], F32, name="y")
         for q, (first, count) in enumerate(CELL_CHUNKS):
             codes, scales = quantize(z_grouped[:, first * P * PACK : (first + count) * P * PACK], count * P, f"zq{q}")
-            acc = bank(3 + q, f"y{q}")
+            acc = bank((7 + q) % 8, f"y{q}")
             nc.tensor.matmul_mx(
                 out=acc[:, : count * P],
                 lhsT=w2_codes[:].bitcast(FP8X4),

@@ -24,9 +24,9 @@ K_PASS = P * PACK
 PASSES = K // K_PASS
 LIST_COLS = S // 16
 CELL_BLOCKS = U // P
-HALF_H = H // 2
+SCALE_BASE = 96
 HALF_P = P // 2
-QUARTER = S // 4
+FIRST_PIECES = ((0, 128), (128, 128), (256, 256))
 PAIR_BLOCKS = 2
 BANK_BLOCKS = 4
 CELL_CHUNKS = ((0, 2), (2, 2), (4, 2), (6, 1), (7, 1))
@@ -56,10 +56,12 @@ def tile_picked_devox_none_p_kernel(tc, x_words, x_scales, w1, w2, gate, emb, of
             nc.sync.dma_start(out=tile[:], in_=x_words[g].rearrange("p n t -> p (n t)").bitcast(I32))
             return tile
 
-        def load_w1(g, first, count):
-            raw = keep.tile([P, PACK, count], F32, name=f"w1_raw{g}_{first}", tag=f"w1_raw{g}_{first}")
-            rows = w1[g * K_PASS : (g + 1) * K_PASS, first : first + count]
-            nc.sync.dma_start(out=raw[:], in_=rows.rearrange("(p j) c -> p j c", j=PACK))
+        def load_w1(g, parts):
+            raw = keep.tile([P, PACK, H], F32, name=f"w1_raw{g}")
+            rows = w1[g * K_PASS : (g + 1) * K_PASS, :].rearrange("(p j) c -> p j c", j=PACK)
+            step = PACK // parts
+            for j in range(0, PACK, step):
+                nc.sync.dma_start(out=raw[:, j : j + step], in_=rows[:, j : j + step])
             return raw[:].rearrange("p j (m t) -> p m j t", t=PACK)
 
         def quantize(grouped_flat, width, name):
@@ -68,23 +70,27 @@ def tile_picked_devox_none_p_kernel(tc, x_words, x_scales, w1, w2, gate, emb, of
             nc.vector.quantize_mx(out=codes[:].bitcast(FP8X4), scales=scales[:], in_=grouped_flat)
             return codes, scales
 
-        x_scale_rows = keep.tile([P, T], U8, name="x_scale_rows", align_bytes=64)
-        nc.gpsimd.memset(x_scale_rows[:].bitcast(I32), 0)
-
         offs_t = load_list(offs, "offs_t")
+        x_scale_rows = keep.tile([P, T], U8, name="x_scale_rows", align_bytes=64)
+        nc.gpsimd.memset(x_scale_rows[:SCALE_BASE].bitcast(I32), 0)
+        for g in range(PASSES):
+            nc.sync.dma_start(out=x_scale_rows[SCALE_BASE + g :: PASSES].bitcast(I32), in_=x_scales[g].bitcast(I32))
+        w1_raw = [load_w1(0, 1)]
+        x_tiles = [load_words(0)]
+        w1_raw.append(load_w1(1, 2))
+        x_tiles.append(load_words(1))
         cell_t = load_list(cell, "cell_t")
         pos_t = [load_list(pos1, "pos1_t"), load_list(pos2, "pos2_t")]
-        whole = load_w1(0, 0, H)
-        w1_raw = {(0, half): whole[:, half * HALF_P : (half + 1) * HALF_P] for half in range(2)}
+
+        picked_scales = keep.tile([P, S], U8, name="picked_scales", align_bytes=64)
+        nc.vector.tensor_copy(picked_scales[:], x_scale_rows[:].indirect(offs_t[:]))
+        xg_scales = keep.tile([P, PASSES, S], U8, name="xg_scales", align_bytes=64)
+        nc.gpsimd.memset(xg_scales[:].rearrange("p g s -> p (g s)").bitcast(I32), 0)
         for q in range(4):
             nc.sync.dma_start(
-                out=x_scale_rows[32 * q : 32 * q + 4 * PASSES].bitcast(I32),
-                in_=x_scales[:, 4 * q : 4 * q + 4, :].bitcast(I32),
+                out=xg_scales[32 * q : 32 * q + 4].bitcast(I32),
+                in_=picked_scales[SCALE_BASE + 8 * q : SCALE_BASE + 8 * q + 8].bitcast(I32),
             )
-        x_tiles = [load_words(0)]
-        w1_raw[1, 0] = load_w1(1, 0, HALF_H)
-        x_tiles.append(load_words(1))
-        w1_raw[1, 1] = load_w1(1, HALF_H, HALF_H)
 
         emb_rows = emb.rearrange("(p t) u -> p t u", t=PACK)
         upper_emb, upper_windows, lower_windows = [], [], []
@@ -108,25 +114,18 @@ def tile_picked_devox_none_p_kernel(tc, x_words, x_scales, w1, w2, gate, emb, of
             nc.vector.memset(upper_windows[half][:].bitcast(I32), 0)
             nc.gpsimd.memset(lower_windows[half][:, :U].bitcast(I32), 0)
 
-        upper_grouped = [keep.tile([P, 2, P, PACK], BF16, name=f"upper_grouped{g}", align_bytes=64) for g in range(PASSES)]
-        lower_grouped = [keep.tile([P, 2, P, PACK], BF16, name=f"lower_grouped{g}", align_bytes=64) for g in range(PASSES)]
+        w1q = []
+        for g in range(PASSES):
+            grouped = keep.tile([P, PACK, P, PACK], BF16, name=f"w1_grouped{g}", align_bytes=64)
+            upper = grouped[:, :2].rearrange("p h (m e) j -> p (h m) j e", e=2)
+            lower = grouped[:, 2:].rearrange("p t m j -> p m j t")
+            nc.scalar.activation(upper, w1_raw[g][:, :, :, 2:], COPY)
+            if g == 0:
+                nc.scalar.activation(lower, w1_raw[g][:, :, :, :2], COPY)
+            else:
+                nc.vector.tensor_copy(lower, w1_raw[g][:, :, :, :2])
+            w1q.append(quantize(grouped[:].rearrange("p t m j -> p (t m j)"), H, f"w1q{g}"))
 
-        def cast_upper(g, half):
-            nc.scalar.activation(
-                upper_grouped[g][:, half].rearrange("p (m e) j -> p m j e", e=2),
-                w1_raw[g, half][:, :, :, 2:4],
-                COPY,
-            )
-
-        def cast_lower(g, half):
-            nc.scalar.activation(
-                lower_grouped[g][:, :, half * HALF_P : (half + 1) * HALF_P, :].rearrange("p t m j -> p m j t"),
-                w1_raw[g, half][:, :, :, 0:2],
-                COPY,
-            )
-
-        xg_scales = keep.tile([P, S], U8, name="xg_scales", align_bytes=64)
-        nc.vector.tensor_copy(xg_scales[:], x_scale_rows[:].indirect(offs_t[:]))
         xg = [keep.tile([P, S], U32, name=f"xg{g}", align_bytes=64) for g in range(PASSES)]
 
         def product(acc, weights, column, g, first, count):
@@ -136,73 +135,26 @@ def tile_picked_devox_none_p_kernel(tc, x_words, x_scales, w1, w2, gate, emb, of
                 lhsT=codes[:, column : column + P].bitcast(FP8X4),
                 lhsT_scale=scales[:, column : column + P],
                 rhs=xg[g][:, first : first + count].bitcast(FP8X4),
-                rhs_scale=xg_scales[4 * g :, first : first + count],
+                rhs_scale=xg_scales[:, g, first : first + count],
                 start=(g == 0),
                 stop=(g == PASSES - 1),
             )
 
-        def relu(parts, name, tag=None):
-            staged = keep.tile([P, sum(part.shape[1] for part in parts)], F32, name=name, tag=tag or name)
-            column = 0
-            for part in parts:
-                nc.scalar.activation(staged[:, column : column + part.shape[1]], part, RELU)
-                column = column + part.shape[1]
-            return staged
-
-        def scatter(window, first, staged):
-            nc.vector.tensor_copy(window[:].indirect(entries(cell_t, first, staged.shape[1])), staged[:])
-
-        first_groups = ((0, QUARTER), (QUARTER, 2 * QUARTER), (3 * QUARTER, QUARTER))
-        first_accs = [bank(n, f"h_first{n}") for n in range(len(first_groups))]
-        second_accs = [bank(3 + n, f"h_second{n}") for n in range(2)]
-        lower_accs = [bank(5 + t, f"h_lower{t}") for t in range(2)]
-
-        def quantize_upper(g, half):
-            cast_upper(g, half)
-            return quantize(upper_grouped[g][:, half].rearrange("p m j -> p (m j)"), P, f"w1_upper{g}_{half}")
-
-        def quantize_lower(g):
-            return quantize(lower_grouped[g][:].rearrange("p t m j -> p (t m j)"), 2 * P, f"w1_lower{g}")
-
-        weights = quantize_upper(0, 0)
         nc.vector.tensor_copy(xg[0][:], x_tiles[0][:].bitcast(U32).indirect(offs_t[:]))
-        for acc, (first, count) in zip(first_accs, first_groups):
-            product(acc, weights, 0, 0, first, count)
-        weights = quantize_upper(0, 1)
-        for n, acc in enumerate(second_accs):
-            product(acc, weights, 0, 0, n * S // 2, S // 2)
-        for half in range(2):
-            cast_lower(0, half)
-        weights = quantize_lower(0)
-        for t, acc in enumerate(lower_accs):
-            product(acc, weights, t * P, 0, 0, S)
-
-        weights = quantize_upper(1, 0)
         for half in range(2):
             nc.vector.tensor_copy(
                 xg[1][:, half * S // 2 : (half + 1) * S // 2],
                 x_tiles[1][:].bitcast(U32).indirect(entries(offs_t, half * S // 2, S // 2)),
             )
-        for acc, (first, count) in zip(first_accs, first_groups):
-            product(acc, weights, 0, 1, first, count)
-        cast_lower(1, 0)
-        for n in range(2):
-            first, count = first_groups[n]
-            scatter(upper_windows[0], first, relu([first_accs[n][:, :count]], f"h_sb_first{n}"))
-
-        second_weights = quantize_upper(1, 1)
-        cast_lower(1, 1)
-        lower_weights = quantize_lower(1)
-        scatter(upper_windows[0], 3 * QUARTER, relu([first_accs[2][:, :QUARTER]], "h_sb_first2", tag=f"w1_raw1_{HALF_H}"))
-
-        for n, acc in enumerate(second_accs):
-            product(acc, second_weights, 0, 1, n * S // 2, S // 2)
-        scatter(upper_windows[1], 0, relu([second_accs[0][:, :QUARTER]], "h_sb_second0"))
-        rest = [second_accs[0][:, QUARTER : 2 * QUARTER], second_accs[1][:, : 2 * QUARTER]]
-        scatter(upper_windows[1], QUARTER, relu(rest, "h_sb_second1"))
-        for t, acc in enumerate(lower_accs):
-            product(acc, lower_weights, t * P, 1, 0, S)
-            scatter(lower_windows[t], 0, relu([acc[:]], f"h_sb_lower{t}"))
+        pieces = [(0, first, count) for first, count in FIRST_PIECES] + [(plane, 0, S) for plane in range(1, PACK)]
+        for n, (plane, first, count) in enumerate(pieces):
+            acc = bank(n % len(FIRST_PIECES), f"h{n}")
+            for g in range(PASSES):
+                product(acc, w1q[g], plane * P, g, first, count)
+            staged = keep.tile([P, count], F32, name=f"h_sb{n}")
+            nc.scalar.activation(staged[:], acc[:, :count], RELU)
+            window = (upper_windows + lower_windows)[plane]
+            nc.vector.tensor_copy(window[:].indirect(entries(cell_t, first, count)), staged[:])
 
         w2_grouped = keep.tile([P, N, PACK], BF16, name="w2_grouped", align_bytes=64)
         nc.scalar.activation(
@@ -217,7 +169,7 @@ def tile_picked_devox_none_p_kernel(tc, x_words, x_scales, w1, w2, gate, emb, of
         pairs = [keep.tile([P, 2, width, 2], BF16, name=f"pairs{q}") for q in range(groups)]
         rows = [keep.tile([P, BANK_BLOCKS, 2, P], BF16, name=f"z_rows{side}") for side in range(2)]
         for half in range(2):
-            sums = [bank((7 + 2 * half + side) % 8, f"zt{half}_{side}") for side in range(2)]
+            sums = [bank(3 + 2 * half + side, f"zt{half}_{side}") for side in range(2)]
             for n, tile in enumerate((upper_emb[half], upper_windows[half])):
                 for side in range(2):
                     for b in range(BANK_BLOCKS):
@@ -235,7 +187,7 @@ def tile_picked_devox_none_p_kernel(tc, x_words, x_scales, w1, w2, gate, emb, of
         for q in range(groups):
             side, first = divmod(q * PAIR_BLOCKS, BANK_BLOCKS)
             words = rows[side][:].rearrange("r b h c -> r (b h c)").bitcast(F32)
-            back = bank(3 + q, f"zw{q}")
+            back = bank((7 + q) % 8, f"zw{q}")
             for b in range(PAIR_BLOCKS):
                 nc.tensor.transpose(back[:, b * P : (b + 1) * P], words[:, (first + b) * P : (first + b + 1) * P], ident[:])
             nc.scalar.copy(pairs[q][:, 1].rearrange("p r e -> p (r e)").bitcast(F32), back[:, :width])
@@ -254,7 +206,7 @@ def tile_picked_devox_none_p_kernel(tc, x_words, x_scales, w1, w2, gate, emb, of
         y = keep.tile([P, U], F32, name="y")
         for q, (first, count) in enumerate(CELL_CHUNKS):
             codes, scales = quantize(z_grouped[:, first * P * PACK : (first + count) * P * PACK], count * P, f"zq{q}")
-            acc = bank((7 + q) % 8, f"y{q}")
+            acc = bank(3 + q, f"y{q}")
             nc.tensor.matmul_mx(
                 out=acc[:, : count * P],
                 lhsT=w2_codes[:].bitcast(FP8X4),

@@ -30,7 +30,7 @@ FIRST_PIECES = ((0, 128), (128, 128), (256, 256))
 PAIR_BLOCKS = 2
 BANK_BLOCKS = 4
 CELL_CHUNKS = ((0, 2), (2, 2), (4, 2), (6, 1), (7, 1))
-COPIED_BY_SCALAR = 3
+COPIED_BY_VECTOR = 3
 OUT_PIECES = ((0, 384), (384, 128))
 
 
@@ -73,8 +73,7 @@ def tile_picked_devox_none_p_kernel(tc, x_words, x_scales, w1, w2, gate, emb, of
         offs_t = load_list(offs, "offs_t")
         x_scale_rows = keep.tile([P, T], U8, name="x_scale_rows", align_bytes=64)
         nc.gpsimd.memset(x_scale_rows[:SCALE_BASE].bitcast(I32), 0)
-        for g in range(PASSES):
-            nc.sync.dma_start(out=x_scale_rows[SCALE_BASE + g :: PASSES].bitcast(I32), in_=x_scales[g].bitcast(I32))
+        nc.sync.dma_start(out=x_scale_rows[SCALE_BASE:].bitcast(I32), in_=x_scales.rearrange("g r c -> r g c").bitcast(I32))
         w1_raw = [load_w1(0, 1)]
         x_tiles = [load_words(0)]
         w1_raw.append(load_w1(1, 2))
@@ -216,7 +215,7 @@ def tile_picked_devox_none_p_kernel(tc, x_words, x_scales, w1, w2, gate, emb, of
                 start=True,
                 stop=True,
             )
-            if q < COPIED_BY_SCALAR:
+            if q != COPIED_BY_VECTOR:
                 nc.scalar.copy(y[:, first * P : (first + count) * P], acc[:, : count * P])
             else:
                 nc.vector.tensor_copy(y[:, first * P : (first + count) * P], acc[:, : count * P])

@@ -26,12 +26,13 @@ LIST_COLS = S // 16
 CELL_BLOCKS = U // P
 SCALE_BASE = 96
 HALF_P = P // 2
-FIRST_PIECES = ((0, 128), (128, 128), (256, 256))
+SCATTER_PIECES = ((0, 0, 128), (1, 0, 256), (0, 128, 384), (1, 256, 256), (2, 0, 512), (3, 0, 512))
+PRODUCT_BANKS = 4
 PAIR_BLOCKS = 2
 BANK_BLOCKS = 4
 CELL_CHUNKS = ((0, 2), (2, 2), (4, 2), (6, 1), (7, 1))
 COPIED_BY_VECTOR = 3
-OUT_PIECES = ((0, 384), (384, 128))
+OUT_PIECES = ((0, 256), (256, 128), (384, 128))
 
 
 def tile_picked_devox_none_p_kernel(tc, x_words, x_scales, w1, w2, gate, emb, offs, cell, pos1, pos2, out):
@@ -130,7 +131,7 @@ def tile_picked_devox_none_p_kernel(tc, x_words, x_scales, w1, w2, gate, emb, of
         def product(acc, weights, column, g, first, count):
             codes, scales = weights
             nc.tensor.matmul_mx(
-                out=acc[:, :count],
+                out=acc,
                 lhsT=codes[:, column : column + P].bitcast(FP8X4),
                 lhsT_scale=scales[:, column : column + P],
                 rhs=xg[g][:, first : first + count].bitcast(FP8X4),
@@ -145,11 +146,13 @@ def tile_picked_devox_none_p_kernel(tc, x_words, x_scales, w1, w2, gate, emb, of
                 xg[1][:, half * S // 2 : (half + 1) * S // 2],
                 x_tiles[1][:].bitcast(U32).indirect(entries(offs_t, half * S // 2, S // 2)),
             )
-        pieces = [(0, first, count) for first, count in FIRST_PIECES] + [(plane, 0, S) for plane in range(1, PACK)]
-        for n, (plane, first, count) in enumerate(pieces):
-            acc = bank(n % len(FIRST_PIECES), f"h{n}")
-            for g in range(PASSES):
-                product(acc, w1q[g], plane * P, g, first, count)
+        for n, (plane, first, count) in enumerate(SCATTER_PIECES):
+            acc = bank(n % PRODUCT_BANKS, f"h{n}")
+            lead = count % (S // 2)
+            for start, size in ((0, lead), (lead, count - lead)):
+                if size:
+                    for g in range(PASSES):
+                        product(acc[:, start : start + size], w1q[g], plane * P, g, first + start, size)
             staged = keep.tile([P, count], F32, name=f"h_sb{n}")
             nc.scalar.activation(staged[:], acc[:, :count], RELU)
             window = (upper_windows + lower_windows)[plane]
@@ -168,7 +171,7 @@ def tile_picked_devox_none_p_kernel(tc, x_words, x_scales, w1, w2, gate, emb, of
         pairs = [keep.tile([P, 2, width, 2], BF16, name=f"pairs{q}") for q in range(groups)]
         rows = [keep.tile([P, BANK_BLOCKS, 2, P], BF16, name=f"z_rows{side}") for side in range(2)]
         for half in range(2):
-            sums = [bank(3 + 2 * half + side, f"zt{half}_{side}") for side in range(2)]
+            sums = [bank(4 + 2 * half + side, f"zt{half}_{side}") for side in range(2)]
             for n, tile in enumerate((upper_emb[half], upper_windows[half])):
                 for side in range(2):
                     for b in range(BANK_BLOCKS):
@@ -186,7 +189,7 @@ def tile_picked_devox_none_p_kernel(tc, x_words, x_scales, w1, w2, gate, emb, of
         for q in range(groups):
             side, first = divmod(q * PAIR_BLOCKS, BANK_BLOCKS)
             words = rows[side][:].rearrange("r b h c -> r (b h c)").bitcast(F32)
-            back = bank((7 + q) % 8, f"zw{q}")
+            back = bank(q, f"zw{q}")
             for b in range(PAIR_BLOCKS):
                 nc.tensor.transpose(back[:, b * P : (b + 1) * P], words[:, (first + b) * P : (first + b + 1) * P], ident[:])
             nc.scalar.copy(pairs[q][:, 1].rearrange("p r e -> p (r e)").bitcast(F32), back[:, :width])
@@ -205,7 +208,7 @@ def tile_picked_devox_none_p_kernel(tc, x_words, x_scales, w1, w2, gate, emb, of
         y = keep.tile([P, U], F32, name="y")
         for q, (first, count) in enumerate(CELL_CHUNKS):
             codes, scales = quantize(z_grouped[:, first * P * PACK : (first + count) * P * PACK], count * P, f"zq{q}")
-            acc = bank(3 + q, f"y{q}")
+            acc = bank((4 + q) % 8, f"y{q}")
             nc.tensor.matmul_mx(
                 out=acc[:, : count * P],
                 lhsT=w2_codes[:].bitcast(FP8X4),
@@ -220,12 +223,22 @@ def tile_picked_devox_none_p_kernel(tc, x_words, x_scales, w1, w2, gate, emb, of
             else:
                 nc.vector.tensor_copy(y[:, first * P : (first + count) * P], acc[:, : count * P])
 
-        terms = []
-        for n, (first, count) in enumerate(OUT_PIECES):
-            for d in range(2):
-                term = keep.tile([P, count], F32, name=f"term{n}_{d}")
-                nc.vector.tensor_tensor(term[:], y[:].indirect(entries(pos_t[d], first, count)), gate_t[:, d, first : first + count], MULT)
-                terms.append(term)
-            result = keep.tile([P, count], F32, name=f"result{n}")
-            nc.vector.tensor_tensor(result[:], terms[-2][:], terms[-1][:], ADD)
+        first_term = keep.tile([P, V], F32, name="first_term")
+        nc.vector.tensor_tensor(first_term[:], y[:].indirect(pos_t[0][:]), gate_t[:, 0], MULT)
+
+        def second_term(first, count):
+            term = keep.tile([P, count], F32, name=f"second_term{first}")
+            nc.vector.tensor_tensor(term[:], y[:].indirect(entries(pos_t[1], first, count)), gate_t[:, 1, first : first + count], MULT)
+            return term
+
+        def add_and_store(first, count, term):
+            result = keep.tile([P, count], F32, name=f"result{first}")
+            nc.vector.tensor_tensor(result[:], first_term[:, first : first + count], term[:], ADD)
             nc.sync.dma_start(out=out[:, first : first + count], in_=result[:])
+
+        waiting = second_term(*OUT_PIECES[0])
+        for done, ahead in zip(OUT_PIECES, OUT_PIECES[1:]):
+            term = second_term(*ahead)
+            add_and_store(*done, waiting)
+            waiting = term
+        add_and_store(*OUT_PIECES[-1], waiting)

@@ -75,10 +75,8 @@ def tile_picked_devox_none_p_kernel(tc, x_words, x_scales, w1, w2, gate, emb, of
         x_scale_rows = keep.tile([P, T], U8, name="x_scale_rows", align_bytes=64)
         nc.gpsimd.memset(x_scale_rows[:SCALE_BASE].bitcast(I32), 0)
         nc.sync.dma_start(out=x_scale_rows[SCALE_BASE:].bitcast(I32), in_=x_scales.rearrange("g r c -> r g c").bitcast(I32))
-        w1_raw = [load_w1(0, 1)]
-        x_tiles = [load_words(0)]
-        w1_raw.append(load_w1(1, 2))
-        x_tiles.append(load_words(1))
+        w1_raw = [load_w1(0, 1), load_w1(1, 2)]
+        x_tiles = [load_words(g) for g in range(PASSES)]
         cell_t = load_list(cell, "cell_t")
         pos_t = [load_list(pos1, "pos1_t"), load_list(pos2, "pos2_t")]
 

@@ -23,15 +23,16 @@ PACK = 4
 K_PASS = P * PACK
 PASSES = K // K_PASS
 LIST_COLS = S // 16
-CELL_BLOCKS = U // P
 SCALE_BASE = 96
 HALF_P = P // 2
-SCATTER_PIECES = ((0, 0, 128), (1, 0, 256), (0, 128, 384), (1, 256, 256), (2, 0, 512), (3, 0, 512))
-PRODUCT_BANKS = 4
-PAIR_BLOCKS = 2
+HALF_H = H // 2
+PLANES = ((0, 1), (0, 0), (1, 1), (1, 0))
+OPENING = 128
 BANK_BLOCKS = 4
+PAIR_BLOCKS = 2
 CELL_CHUNKS = ((0, 2), (2, 2), (4, 2), (6, 1), (7, 1))
-COPIED_BY_VECTOR = 3
+WOVEN_BY_VECTOR = (1,)
+COPIED_BY_VECTOR = (3,)
 OUT_PIECES = ((0, 256), (256, 128), (384, 128))
 
 
@@ -41,44 +42,55 @@ def tile_picked_devox_none_p_kernel(tc, x_words, x_scales, w1, w2, gate, emb, of
         keep = ctx.enter_context(tc.tile_pool(name="keep", bufs=1))
         psum = ctx.enter_context(tc.psum_pool(name="psum", bufs=1))
 
+        def tile(shape, dtype, name, tag=None):
+            return keep.tile(shape, dtype, name=name, tag=tag or name, align_bytes=64)
+
         def bank(index, name):
             return psum.tile([P, 512], F32, name=name, tag=f"bank{index}")
 
         def load_list(src, name):
-            tile = keep.tile([P, LIST_COLS], U16, name=name)
-            nc.sync.dma_start(tile[:], src)
-            return tile
+            offsets = keep.tile([P, LIST_COLS], U16, name=name)
+            nc.sync.dma_start(offsets[:], src)
+            return offsets
 
-        def entries(tile, first, count):
-            return tile[:, first // 16 : (first + count) // 16]
+        def entries(offsets, first, count):
+            return offsets[:, first // 16 : (first + count) // 16]
 
         def load_words(g):
-            tile = keep.tile([P, T], I32, name=f"x_words{g}")
-            nc.sync.dma_start(out=tile[:], in_=x_words[g].rearrange("p n t -> p (n t)").bitcast(I32))
-            return tile
+            words = tile([P, T], I32, f"x_words{g}")
+            nc.sync.dma_start(out=words[:], in_=x_words[g].rearrange("p n t -> p (n t)").bitcast(I32))
+            return words
 
-        def load_w1(g, parts):
-            raw = keep.tile([P, PACK, H], F32, name=f"w1_raw{g}")
-            rows = w1[g * K_PASS : (g + 1) * K_PASS, :].rearrange("(p j) c -> p j c", j=PACK)
-            step = PACK // parts
-            for j in range(0, PACK, step):
-                nc.sync.dma_start(out=raw[:, j : j + step], in_=rows[:, j : j + step])
-            return raw[:].rearrange("p j (m t) -> p m j t", t=PACK)
+        def load_w1(g, half):
+            raw = tile([P, PACK, HALF_H], F32, f"w1_raw{half}{g}", f"w1_raw{g}")
+            rows = w1[g * K_PASS : (g + 1) * K_PASS, half * HALF_H : (half + 1) * HALF_H]
+            nc.sync.dma_start(out=raw[:], in_=rows.rearrange("(p j) c -> p j c", j=PACK))
+            return raw
 
         def quantize(grouped_flat, width, name):
-            codes = keep.tile([P, width], U32, name=name + "_codes", align_bytes=64)
-            scales = keep.tile([P, width], U8, name=name + "_scales", align_bytes=64)
+            codes = tile([P, width], U32, name + "_codes")
+            scales = tile([P, width], U8, name + "_scales")
             nc.vector.quantize_mx(out=codes[:].bitcast(FP8X4), scales=scales[:], in_=grouped_flat)
             return codes, scales
+
+        def quantize_w1(raws, half, tag):
+            grouped = tile([P, 2 * PASSES * K_PASS], BF16, f"w1_grouped{half}", tag)
+            for g in range(PASSES):
+                columns = raws[g][:].rearrange("p j (m t) -> p m j t", t=PACK)
+                for u in range(2):
+                    first = (2 * g + u) * K_PASS
+                    part = grouped[:, first : first + K_PASS].rearrange("p (m e j) -> p m j e", e=2, j=PACK)
+                    nc.scalar.activation(part, columns[:, :, :, 2 * u : 2 * u + 2], COPY)
+            return quantize(grouped[:], 2 * PASSES * P, f"w1q{half}")
 
         offs_t = load_list(offs, "offs_t")
         x_scale_rows = keep.tile([P, T], U8, name="x_scale_rows", align_bytes=64)
         nc.gpsimd.memset(x_scale_rows[:SCALE_BASE].bitcast(I32), 0)
         nc.sync.dma_start(out=x_scale_rows[SCALE_BASE:].bitcast(I32), in_=x_scales.rearrange("g r c -> r g c").bitcast(I32))
-        w1_raw = [load_w1(0, 1), load_w1(1, 2)]
-        x_tiles = [load_words(g) for g in range(PASSES)]
+        left_raw = [load_w1(g, 0) for g in range(PASSES)]
         cell_t = load_list(cell, "cell_t")
         pos_t = [load_list(pos1, "pos1_t"), load_list(pos2, "pos2_t")]
+        x_tiles = [load_words(g) for g in range(PASSES)]
 
         picked_scales = keep.tile([P, S], U8, name="picked_scales", align_bytes=64)
         nc.vector.tensor_copy(picked_scales[:], x_scale_rows[:].indirect(offs_t[:]))
@@ -90,72 +102,69 @@ def tile_picked_devox_none_p_kernel(tc, x_words, x_scales, w1, w2, gate, emb, of
                 in_=picked_scales[SCALE_BASE + 8 * q : SCALE_BASE + 8 * q + 8].bitcast(I32),
             )
 
-        emb_rows = emb.rearrange("(p t) u -> p t u", t=PACK)
-        upper_emb, upper_windows, lower_windows = [], [], []
-        for half in range(2):
-            tile = keep.tile([P, U], F32, name=f"upper_emb{half}")
-            nc.sync.dma_start(out=tile[:], in_=emb_rows[half * HALF_P : (half + 1) * HALF_P, 2:4, :])
-            upper_emb.append(tile)
-            upper_windows.append(keep.tile([P, U], F32, name=f"upper_window{half}"))
-        for half in range(2):
-            tile = keep.tile([P, 2 * U], F32, name=f"lower_window{half}")
-            nc.sync.dma_start(out=tile[:, U:], in_=emb_rows[:, 1 - half, :])
-            lower_windows.append(tile)
-        w2_raw = keep.tile([P, PACK, N], F32, name="w2_raw")
-        nc.sync.dma_start(out=w2_raw[:], in_=w2.rearrange("(p j) n -> p j n", j=PACK))
-        gate_t = keep.tile([P, 2, V], F32, name="gate_t")
-        nc.sync.dma_start(out=gate_t[:], in_=gate.rearrange("d p v -> p d v"))
-
-        ident = keep.tile([P, P], F32, name="ident")
+        ident = tile([P, P], F32, "ident")
         make_identity(nc, ident[:])
-        for half in range(2):
-            nc.vector.memset(upper_windows[half][:].bitcast(I32), 0)
-            nc.gpsimd.memset(lower_windows[half][:, :U].bitcast(I32), 0)
+        windows = [tile([P, U], F32, f"window{n}") for n in range(4)]
+        for n in range(4):
+            (nc.vector if n < 2 else nc.gpsimd).memset(windows[n][:].bitcast(I32), 0)
 
-        w1q = []
-        for g in range(PASSES):
-            grouped = keep.tile([P, PACK, P, PACK], BF16, name=f"w1_grouped{g}", align_bytes=64)
-            upper = grouped[:, :2].rearrange("p h (m e) j -> p (h m) j e", e=2)
-            lower = grouped[:, 2:].rearrange("p t m j -> p m j t")
-            nc.scalar.activation(upper, w1_raw[g][:, :, :, 2:], COPY)
-            if g == 0:
-                nc.scalar.activation(lower, w1_raw[g][:, :, :, :2], COPY)
-            else:
-                nc.vector.tensor_copy(lower, w1_raw[g][:, :, :, :2])
-            w1q.append(quantize(grouped[:].rearrange("p t m j -> p (t m j)"), H, f"w1q{g}"))
+        w1q = [quantize_w1(left_raw, 0, "left_grouped")]
+        right_raw = [load_w1(g, 1) for g in range(PASSES)]
 
-        xg = [keep.tile([P, S], U32, name=f"xg{g}", align_bytes=64) for g in range(PASSES)]
-
-        def product(acc, weights, column, g, first, count):
-            codes, scales = weights
-            nc.tensor.matmul_mx(
-                out=acc,
-                lhsT=codes[:, column : column + P].bitcast(FP8X4),
-                lhsT_scale=scales[:, column : column + P],
-                rhs=xg[g][:, first : first + count].bitcast(FP8X4),
-                rhs_scale=xg_scales[:, g, first : first + count],
-                start=(g == 0),
-                stop=(g == PASSES - 1),
-            )
-
+        xg = [tile([P, S], U32, f"xg{g}") for g in range(PASSES)]
         nc.vector.tensor_copy(xg[0][:], x_tiles[0][:].bitcast(U32).indirect(offs_t[:]))
         for half in range(2):
             nc.vector.tensor_copy(
                 xg[1][:, half * S // 2 : (half + 1) * S // 2],
                 x_tiles[1][:].bitcast(U32).indirect(entries(offs_t, half * S // 2, S // 2)),
             )
-        for n, (plane, first, count) in enumerate(SCATTER_PIECES):
-            acc = bank(n % PRODUCT_BANKS, f"h{n}")
+
+        emb_rows = emb.rearrange("(p t) u -> p t u", t=PACK)
+
+        def load_emb(n, tag):
+            half, u = PLANES[n]
+            rows = tile([P, U], F32, f"emb{n}", tag)
+            nc.sync.dma_start(out=rows[:], in_=emb_rows[half * HALF_P : (half + 1) * HALF_P, 2 * u : 2 * u + 2, :])
+            return rows
+
+        def scatter(index, n, first, count, tag):
+            half, u = PLANES[n]
+            codes, scales = w1q[half]
+            acc = bank(index, f"h{n}_{first}")
             lead = count % (S // 2)
             for start, size in ((0, lead), (lead, count - lead)):
                 if size:
                     for g in range(PASSES):
-                        product(acc[:, start : start + size], w1q[g], plane * P, g, first + start, size)
-            staged = keep.tile([P, count], F32, name=f"h_sb{n}")
+                        column = (2 * g + u) * P
+                        nc.tensor.matmul_mx(
+                            out=acc[:, start : start + size],
+                            lhsT=codes[:, column : column + P].bitcast(FP8X4),
+                            lhsT_scale=scales[:, column : column + P],
+                            rhs=xg[g][:, first + start : first + start + size].bitcast(FP8X4),
+                            rhs_scale=xg_scales[:, g, first + start : first + start + size],
+                            start=(g == 0),
+                            stop=(g == PASSES - 1),
+                        )
+            staged = tile([P, count], F32, f"h_sb{n}_{first}", tag)
             nc.scalar.activation(staged[:], acc[:, :count], RELU)
-            window = (upper_windows + lower_windows)[plane]
-            nc.vector.tensor_copy(window[:].indirect(entries(cell_t, first, count)), staged[:])
+            nc.vector.tensor_copy(windows[n][:].indirect(entries(cell_t, first, count)), staged[:])
 
+        emb_t = [load_emb(0, "left_grouped")]
+        scatter(0, 0, 0, OPENING, "staged0")
+        scatter(1, 1, 0, OPENING, "staged1")
+        scatter(2, 0, OPENING, S - OPENING, "staged2")
+        emb_t.append(load_emb(1, "staged1"))
+        w1q.append(quantize_w1(right_raw, 1, "staged0"))
+        scatter(3, 1, OPENING, S - OPENING, "w1_raw1")
+        emb_t.append(load_emb(2, "w1_raw0"))
+        emb_t.append(load_emb(3, "staged2"))
+        scatter(0, 2, 0, S, "staged4")
+        scatter(1, 3, 0, S, "staged5")
+
+        w2_raw = tile([P, PACK, N], F32, "w2_raw", "staged0")
+        nc.sync.dma_start(out=w2_raw[:], in_=w2.rearrange("(p j) n -> p j n", j=PACK))
+        gate_t = tile([P, 2, V], F32, "gate_t", "w1_raw1")
+        nc.sync.dma_start(out=gate_t[:], in_=gate.rearrange("d p v -> p d v"))
         w2_grouped = keep.tile([P, N, PACK], BF16, name="w2_grouped", align_bytes=64)
         nc.scalar.activation(
             w2_grouped[:].rearrange("p (c i) j -> p c j i", i=4),
@@ -164,48 +173,62 @@ def tile_picked_devox_none_p_kernel(tc, x_words, x_scales, w1, w2, gate, emb, of
         )
         w2_codes, w2_scales = quantize(w2_grouped[:].rearrange("p c j -> p (c j)"), N, "w2q")
 
-        groups = CELL_BLOCKS // PAIR_BLOCKS
-        width = PAIR_BLOCKS * P
-        pairs = [keep.tile([P, 2, width, 2], BF16, name=f"pairs{q}") for q in range(groups)]
-        rows = [keep.tile([P, BANK_BLOCKS, 2, P], BF16, name=f"z_rows{side}") for side in range(2)]
-        for half in range(2):
-            sums = [bank(4 + 2 * half + side, f"zt{half}_{side}") for side in range(2)]
-            for n, tile in enumerate((upper_emb[half], upper_windows[half])):
+        rows = [[tile([P, BANK_BLOCKS, 2, P], BF16, f"z_rows{u}{side}") for side in range(2)] for u in range(2)]
+
+        def add_emb(n):
+            half, u = PLANES[n]
+            sums = [bank(4 + 2 * (n % 2) + side, f"zt{n}_{side}") for side in range(2)]
+            for k, source in enumerate((emb_t[n], windows[n])):
                 for side in range(2):
                     for b in range(BANK_BLOCKS):
                         column = (side * BANK_BLOCKS + b) * P
                         nc.tensor.matmul(
                             sums[side][:, b * P : (b + 1) * P],
-                            tile[:, column : column + P],
+                            source[:, column : column + P],
                             ident[:],
-                            start=(n == 0 and b == 0),
-                            stop=(n == 1 and b == BANK_BLOCKS - 1),
+                            start=(k == 0 and b == 0),
+                            stop=(k == 1 and b == BANK_BLOCKS - 1),
                             is_transpose=True,
                         )
             for side in range(2):
-                nc.scalar.copy(rows[side][:, :, half, :], sums[side][:].rearrange("r (b c) -> r b c", b=BANK_BLOCKS))
-        for q in range(groups):
+                blocks = sums[side][:].rearrange("r (b c) -> r b c", b=BANK_BLOCKS)
+                if n == 3 and side == 1:
+                    nc.vector.tensor_copy(rows[u][side][:, :, half, :], blocks)
+                else:
+                    nc.scalar.copy(rows[u][side][:, :, half, :], blocks)
+
+        groups = U // P // PAIR_BLOCKS
+        width = PAIR_BLOCKS * P
+        backs = [bank(q, f"zw{q}") for q in range(groups)]
+
+        def turn_back(u, q):
             side, first = divmod(q * PAIR_BLOCKS, BANK_BLOCKS)
-            words = rows[side][:].rearrange("r b h c -> r (b h c)").bitcast(F32)
-            back = bank(q, f"zw{q}")
+            words = rows[u][side][:].rearrange("r b h c -> r (b h c)").bitcast(F32)
             for b in range(PAIR_BLOCKS):
-                nc.tensor.transpose(back[:, b * P : (b + 1) * P], words[:, (first + b) * P : (first + b + 1) * P], ident[:])
-            nc.scalar.copy(pairs[q][:, 1].rearrange("p r e -> p (r e)").bitcast(F32), back[:, :width])
+                column = u * width + b * P
+                nc.tensor.transpose(backs[q][:, column : column + P], words[:, (first + b) * P : (first + b + 1) * P], ident[:])
 
-        own = lower_windows[0][:].rearrange("p (e c i) -> p c e i", e=2, i=4)
-        other = lower_windows[1][:].rearrange("p (e c i) -> p c e i", e=2, i=4)[:, :, ::-1, :]
+        for n in range(3):
+            add_emb(n)
         for q in range(groups):
-            quads = slice(q * width // 4, (q + 1) * width // 4)
-            nc.vector.tensor_tensor(pairs[q][:, 0].rearrange("p (c i) e -> p c e i", i=4), own[:, quads], other[:, quads], ADD)
-
-        z_grouped = keep.tile([P, U * PACK], BF16, name="z_grouped", align_bytes=64)
+            turn_back(1, q)
+        add_emb(3)
+        z_grouped = []
         for q in range(groups):
-            dst = z_grouped[:, q * width * PACK : (q + 1) * width * PACK].bitcast(U32).rearrange("p (c i u) -> p c u i", i=2, u=2)
-            nc.scalar.copy(dst, pairs[q][:].rearrange("p u r e -> p (u r e)").bitcast(U32).rearrange("p (u c i) -> p c u i", u=2, i=2))
+            turn_back(0, q)
+            grouped = tile([P, width * PACK], BF16, f"z_grouped{q}")
+            woven = grouped[:].bitcast(F32).rearrange("p (c i u) -> p c u i", i=2, u=2)
+            pairs = backs[q][:].rearrange("p (u c i) -> p c u i", u=2, i=2)
+            if q in WOVEN_BY_VECTOR:
+                nc.vector.tensor_copy(woven, pairs)
+            else:
+                nc.scalar.copy(woven, pairs)
+            z_grouped.append(grouped)
 
         y = keep.tile([P, U], F32, name="y")
         for q, (first, count) in enumerate(CELL_CHUNKS):
-            codes, scales = quantize(z_grouped[:, first * P * PACK : (first + count) * P * PACK], count * P, f"zq{q}")
+            group, start = divmod(first, PAIR_BLOCKS)
+            codes, scales = quantize(z_grouped[group][:, start * P * PACK : (start + count) * P * PACK], count * P, f"zq{q}")
             acc = bank((4 + q) % 8, f"y{q}")
             nc.tensor.matmul_mx(
                 out=acc[:, : count * P],
@@ -216,7 +239,7 @@ def tile_picked_devox_none_p_kernel(tc, x_words, x_scales, w1, w2, gate, emb, of
                 start=True,
                 stop=True,
             )
-            if q != COPIED_BY_VECTOR:
+            if q not in COPIED_BY_VECTOR:
                 nc.scalar.copy(y[:, first * P : (first + count) * P], acc[:, : count * P])
             else:
                 nc.vector.tensor_copy(y[:, first * P : (first + count) * P], acc[:, : count * P])

@@ -31,6 +31,7 @@ OPENING = 128
 BANK_BLOCKS = 4
 PAIR_BLOCKS = 2
 CELL_CHUNKS = ((0, 2), (2, 2), (4, 2), (6, 1), (7, 1))
+ROUNDED_BY_VECTOR = (1, 3)
 WOVEN_BY_VECTOR = (1,)
 COPIED_BY_VECTOR = (3,)
 OUT_PIECES = ((0, 256), (256, 128), (384, 128))
@@ -173,49 +174,53 @@ def tile_picked_devox_none_p_kernel(tc, x_words, x_scales, w1, w2, gate, emb, of
         )
         w2_codes, w2_scales = quantize(w2_grouped[:].rearrange("p c j -> p (c j)"), N, "w2q")
 
-        rows = [[tile([P, BANK_BLOCKS, 2, P], BF16, f"z_rows{u}{side}") for side in range(2)] for u in range(2)]
+        groups = U // P // PAIR_BLOCKS
+        width = PAIR_BLOCKS * P
+        rows = [[tile([P, PAIR_BLOCKS, 2, P], BF16, f"z_rows{u}{q}") for q in range(groups)] for u in range(2)]
 
-        def add_emb(n):
+        def transpose(target, source, start, stop):
+            nc.tensor.matmul(target, source, ident[:], start=start, stop=stop, is_transpose=True)
+
+        def round_out(n, q, sums, by_vector=False):
             half, u = PLANES[n]
+            blocks = sums.rearrange("r (b c) -> r b c", b=PAIR_BLOCKS)
+            if by_vector:
+                nc.vector.tensor_copy(rows[u][q][:, :, half, :], blocks)
+            else:
+                nc.scalar.copy(rows[u][q][:, :, half, :], blocks)
+
+        def words(u, q, b):
+            return rows[u][q][:].rearrange("r b h c -> r (b h c)").bitcast(F32)[:, b * P : (b + 1) * P]
+
+        for n in range(3):
             sums = [bank(4 + 2 * (n % 2) + side, f"zt{n}_{side}") for side in range(2)]
             for k, source in enumerate((emb_t[n], windows[n])):
                 for side in range(2):
                     for b in range(BANK_BLOCKS):
                         column = (side * BANK_BLOCKS + b) * P
-                        nc.tensor.matmul(
-                            sums[side][:, b * P : (b + 1) * P],
-                            source[:, column : column + P],
-                            ident[:],
-                            start=(k == 0 and b == 0),
-                            stop=(k == 1 and b == BANK_BLOCKS - 1),
-                            is_transpose=True,
-                        )
-            for side in range(2):
-                blocks = sums[side][:].rearrange("r (b c) -> r b c", b=BANK_BLOCKS)
-                if n == 3 and side == 1:
-                    nc.vector.tensor_copy(rows[u][side][:, :, half, :], blocks)
-                else:
-                    nc.scalar.copy(rows[u][side][:, :, half, :], blocks)
+                        first, last = k == 0 and b == 0, k == 1 and b == BANK_BLOCKS - 1
+                        transpose(sums[side][:, b * P : (b + 1) * P], source[:, column : column + P], first, last)
+            for q in range(groups):
+                side, part = divmod(q, 2)
+                round_out(n, q, sums[side][:, part * width : (part + 1) * width])
 
-        groups = U // P // PAIR_BLOCKS
-        width = PAIR_BLOCKS * P
         backs = [bank(q, f"zw{q}") for q in range(groups)]
-
-        def turn_back(u, q):
-            side, first = divmod(q * PAIR_BLOCKS, BANK_BLOCKS)
-            words = rows[u][side][:].rearrange("r b h c -> r (b h c)").bitcast(F32)
-            for b in range(PAIR_BLOCKS):
-                column = u * width + b * P
-                nc.tensor.transpose(backs[q][:, column : column + P], words[:, (first + b) * P : (first + b + 1) * P], ident[:])
-
-        for n in range(3):
-            add_emb(n)
         for q in range(groups):
-            turn_back(1, q)
-        add_emb(3)
+            for b in range(PAIR_BLOCKS):
+                column = q * width + b * P
+                transpose(backs[q][:, b * P : (b + 1) * P], emb_t[3][:, column : column + P], b == 0, False)
+        for q in range(groups):
+            for b in range(PAIR_BLOCKS):
+                transpose(backs[q][:, width + b * P : width + (b + 1) * P], words(1, q, b), False, False)
+        for q in range(groups):
+            for b in range(PAIR_BLOCKS):
+                column = q * width + b * P
+                transpose(backs[q][:, b * P : (b + 1) * P], windows[3][:, column : column + P], False, b == PAIR_BLOCKS - 1)
+            round_out(3, q, backs[q][:, :width], q in ROUNDED_BY_VECTOR)
         z_grouped = []
         for q in range(groups):
-            turn_back(0, q)
+            for b in range(PAIR_BLOCKS):
+                transpose(backs[q][:, b * P : (b + 1) * P], words(0, q, b), True, True)
             grouped = tile([P, width * PACK], BF16, f"z_grouped{q}")
             woven = grouped[:].bitcast(F32).rearrange("p (c i u) -> p c u i", i=2, u=2)
             pairs = backs[q][:].rearrange("p (u c i) -> p c u i", u=2, i=2)
@@ -229,7 +234,7 @@ def tile_picked_devox_none_p_kernel(tc, x_words, x_scales, w1, w2, gate, emb, of
         for q, (first, count) in enumerate(CELL_CHUNKS):
             group, start = divmod(first, PAIR_BLOCKS)
             codes, scales = quantize(z_grouped[group][:, start * P * PACK : (start + count) * P * PACK], count * P, f"zq{q}")
-            acc = bank((4 + q) % 8, f"y{q}")
+            acc = bank(4 + (q + 2) % 4, f"y{q}")
             nc.tensor.matmul_mx(
                 out=acc[:, : count * P],
                 lhsT=w2_codes[:].bitcast(FP8X4),

@@ -74,24 +74,25 @@ def tile_picked_devox_none_p_kernel(tc, x_words, x_scales, w1, w2, gate, emb, of
             nc.vector.quantize_mx(out=codes[:].bitcast(FP8X4), scales=scales[:], in_=grouped_flat)
             return codes, scales
 
-        def quantize_w1(raws, half, tag):
-            grouped = tile([P, 2 * PASSES * K_PASS], BF16, f"w1_grouped{half}", tag)
-            for g in range(PASSES):
-                columns = raws[g][:].rearrange("p j (m t) -> p m j t", t=PACK)
-                for u in range(2):
-                    first = (2 * g + u) * K_PASS
-                    part = grouped[:, first : first + K_PASS].rearrange("p (m e j) -> p m j e", e=2, j=PACK)
+        def quantize_w1(raws, half, tags):
+            planes = {}
+            for u in (1, 0):
+                grouped = tile([P, PASSES * K_PASS], BF16, f"w1_grouped{half}{u}", tags[u])
+                for g in range(PASSES):
+                    columns = raws[g][:].rearrange("p j (m t) -> p m j t", t=PACK)
+                    part = grouped[:, g * K_PASS : (g + 1) * K_PASS].rearrange("p (m e j) -> p m j e", e=2, j=PACK)
                     nc.scalar.activation(part, columns[:, :, :, 2 * u : 2 * u + 2], COPY)
-            return quantize(grouped[:], 2 * PASSES * P, f"w1q{half}")
+                planes[u] = quantize(grouped[:], PASSES * P, f"w1q{half}{u}")
+            return planes
 
         offs_t = load_list(offs, "offs_t")
         x_scale_rows = keep.tile([P, T], U8, name="x_scale_rows", align_bytes=64)
         nc.gpsimd.memset(x_scale_rows[:SCALE_BASE].bitcast(I32), 0)
         nc.sync.dma_start(out=x_scale_rows[SCALE_BASE:].bitcast(I32), in_=x_scales.rearrange("g r c -> r g c").bitcast(I32))
         left_raw = [load_w1(g, 0) for g in range(PASSES)]
+        x_tiles = [load_words(g) for g in range(PASSES)]
         cell_t = load_list(cell, "cell_t")
         pos_t = [load_list(pos1, "pos1_t"), load_list(pos2, "pos2_t")]
-        x_tiles = [load_words(g) for g in range(PASSES)]
 
         picked_scales = keep.tile([P, S], U8, name="picked_scales", align_bytes=64)
         nc.vector.tensor_copy(picked_scales[:], x_scale_rows[:].indirect(offs_t[:]))
@@ -109,7 +110,7 @@ def tile_picked_devox_none_p_kernel(tc, x_words, x_scales, w1, w2, gate, emb, of
         for n in range(4):
             (nc.vector if n < 2 else nc.gpsimd).memset(windows[n][:].bitcast(I32), 0)
 
-        w1q = [quantize_w1(left_raw, 0, "left_grouped")]
+        w1q = [quantize_w1(left_raw, 0, ("left_grouped0", "left_grouped1"))]
         right_raw = [load_w1(g, 1) for g in range(PASSES)]
 
         xg = [tile([P, S], U32, f"xg{g}") for g in range(PASSES)]
@@ -130,13 +131,13 @@ def tile_picked_devox_none_p_kernel(tc, x_words, x_scales, w1, w2, gate, emb, of
 
         def scatter(index, n, first, count, tag):
             half, u = PLANES[n]
-            codes, scales = w1q[half]
+            codes, scales = w1q[half][u]
             acc = bank(index, f"h{n}_{first}")
             lead = count % (S // 2)
             for start, size in ((0, lead), (lead, count - lead)):
                 if size:
                     for g in range(PASSES):
-                        column = (2 * g + u) * P
+                        column = g * P
                         nc.tensor.matmul_mx(
                             out=acc[:, start : start + size],
                             lhsT=codes[:, column : column + P].bitcast(FP8X4),
@@ -150,12 +151,12 @@ def tile_picked_devox_none_p_kernel(tc, x_words, x_scales, w1, w2, gate, emb, of
             nc.scalar.activation(staged[:], acc[:, :count], RELU)
             nc.vector.tensor_copy(windows[n][:].indirect(entries(cell_t, first, count)), staged[:])
 
-        emb_t = [load_emb(0, "left_grouped")]
+        emb_t = [load_emb(0, "left_grouped0")]
         scatter(0, 0, 0, OPENING, "staged0")
         scatter(1, 1, 0, OPENING, "staged1")
         scatter(2, 0, OPENING, S - OPENING, "staged2")
-        emb_t.append(load_emb(1, "staged1"))
-        w1q.append(quantize_w1(right_raw, 1, "staged0"))
+        emb_t.append(load_emb(1, "left_grouped1"))
+        w1q.append(quantize_w1(right_raw, 1, ("staged1", "staged0")))
         scatter(3, 1, OPENING, S - OPENING, "w1_raw1")
         emb_t.append(load_emb(2, "w1_raw0"))
         emb_t.append(load_emb(3, "staged2"))

@@ -210,6 +210,18 @@ def tile_picked_devox_none_p_kernel(tc, x_words, x_scales, w1, w2, gate, emb, of
             for b in range(PAIR_BLOCKS):
                 column = q * width + b * P
                 transpose(backs[q][:, b * P : (b + 1) * P], emb_t[3][:, column : column + P], b == 0, False)
+        unread = bank(4, "warm_up")
+        codes, scales = w1q[1][0]
+        for g in range(PASSES):
+            nc.tensor.matmul_mx(
+                out=unread[:],
+                lhsT=codes[:, g * P : (g + 1) * P].bitcast(FP8X4),
+                lhsT_scale=scales[:, g * P : (g + 1) * P],
+                rhs=xg[g][:].bitcast(FP8X4),
+                rhs_scale=xg_scales[:, g],
+                start=(g == 0),
+                stop=(g == PASSES - 1),
+            )
         for q in range(groups):
             for b in range(PAIR_BLOCKS):
                 transpose(backs[q][:, width + b * P : width + (b + 1) * P], words(1, q, b), False, False)

@@ -212,16 +212,15 @@ def tile_picked_devox_none_p_kernel(tc, x_words, x_scales, w1, w2, gate, emb, of
                 transpose(backs[q][:, b * P : (b + 1) * P], emb_t[3][:, column : column + P], b == 0, False)
         unread = bank(4, "warm_up")
         codes, scales = w1q[1][0]
-        for g in range(PASSES):
-            nc.tensor.matmul_mx(
-                out=unread[:],
-                lhsT=codes[:, g * P : (g + 1) * P].bitcast(FP8X4),
-                lhsT_scale=scales[:, g * P : (g + 1) * P],
-                rhs=xg[g][:].bitcast(FP8X4),
-                rhs_scale=xg_scales[:, g],
-                start=(g == 0),
-                stop=(g == PASSES - 1),
-            )
+        nc.tensor.matmul_mx(
+            out=unread[:],
+            lhsT=codes[:, :P].bitcast(FP8X4),
+            lhsT_scale=scales[:, :P],
+            rhs=xg[0][:].bitcast(FP8X4),
+            rhs_scale=xg_scales[:, 0],
+            start=True,
+            stop=True,
+        )
         for q in range(groups):
             for b in range(PAIR_BLOCKS):
                 transpose(backs[q][:, width + b * P : width + (b + 1) * P], words(1, q, b), False, False)

@@ -65,7 +65,7 @@ def tile_picked_devox_none_p_kernel(tc, x_words, x_scales, w1, w2, gate, emb, of
         def load_w1(g, half):
             raw = tile([P, PACK, HALF_H], F32, f"w1_raw{half}{g}", f"w1_raw{g}")
             rows = w1[g * K_PASS : (g + 1) * K_PASS, half * HALF_H : (half + 1) * HALF_H]
-            nc.sync.dma_start(out=raw[:], in_=rows.rearrange("(p j) c -> p j c", j=PACK))
+            (nc.sync if half else nc.scalar).dma_start(out=raw[:], in_=rows.rearrange("(p j) c -> p j c", j=PACK))
             return raw
 
         def quantize(grouped_flat, width, name):
@@ -148,7 +148,10 @@ def tile_picked_devox_none_p_kernel(tc, x_words, x_scales, w1, w2, gate, emb, of
                             stop=(g == PASSES - 1),
                         )
             staged = tile([P, count], F32, f"h_sb{n}_{first}", tag)
-            nc.scalar.activation(staged[:], acc[:, :count], RELU)
+            if index == 0 and n == 0:
+                nc.vector.tensor_scalar_max(staged[:], acc[:, :count], 0.0)
+            else:
+                nc.scalar.activation(staged[:], acc[:, :count], RELU)
             nc.vector.tensor_copy(windows[n][:].indirect(entries(cell_t, first, count)), staged[:])
 
         emb_t = [load_emb(0, "left_grouped0")]

@@ -1,7 +1,6 @@
 from contextlib import ExitStack
 
 import concourse.mybir as mybir
-from concourse.masks import make_identity
 
 K, T, S, V, H, N, U = 1024, 2048, 512, 512, 512, 128, 1024
 FLOPS = 2 * (K * H * S + H * N * U)
@@ -24,23 +23,19 @@ K_PASS = P * PACK
 PASSES = K // K_PASS
 LIST_COLS = S // 16
 SCALE_BASE = 96
-HALF_P = P // 2
-HALF_H = H // 2
-PLANES = ((0, 1), (0, 0), (1, 1), (1, 0))
-OPENING = 128
-BANK_BLOCKS = 4
-PAIR_BLOCKS = 2
-CELL_CHUNKS = ((0, 2), (2, 2), (4, 2), (6, 1), (7, 1))
-ROUNDED_BY_VECTOR = (1, 3)
-WOVEN_BY_VECTOR = (1,)
+HALF_S = S // 2
+CELL_CHUNKS = ((0, 256), (256, 256), (512, 256), (768, 128), (896, 128))
+PAIR_PLACES = (0, 6144, 2048, 4096, 5120)
+WOVEN_BY_VECTOR = (2,)
 COPIED_BY_VECTOR = (3,)
-OUT_PIECES = ((0, 256), (256, 128), (384, 128))
+OUT_PIECES = ((0, 256), (256, 256))
 
 
 def tile_picked_devox_none_p_kernel(tc, x_words, x_scales, w1, w2, gate, emb, offs, cell, pos1, pos2, out):
     nc = tc.nc
     with ExitStack() as ctx:
         keep = ctx.enter_context(tc.tile_pool(name="keep", bufs=1))
+        laid = ctx.enter_context(tc.tile_pool(name="laid", bufs=1))
         psum = ctx.enter_context(tc.psum_pool(name="psum", bufs=1))
 
         def tile(shape, dtype, name, tag=None):
@@ -62,10 +57,12 @@ def tile_picked_devox_none_p_kernel(tc, x_words, x_scales, w1, w2, gate, emb, of
             nc.sync.dma_start(out=words[:], in_=x_words[g].rearrange("p n t -> p (n t)").bitcast(I32))
             return words
 
-        def load_w1(g, half):
-            raw = tile([P, PACK, HALF_H], F32, f"w1_raw{half}{g}", f"w1_raw{g}")
-            rows = w1[g * K_PASS : (g + 1) * K_PASS, half * HALF_H : (half + 1) * HALF_H]
-            (nc.sync if half else nc.scalar).dma_start(out=raw[:], in_=rows.rearrange("(p j) c -> p j c", j=PACK))
+        def load_w1(g):
+            raw = tile([P, PACK, H], F32, f"w1_raw{g}")
+            rows = w1[g * K_PASS : (g + 1) * K_PASS].rearrange("(p j) c -> p j c", j=PACK)
+            step = PACK // (g + 1)
+            for j in range(0, PACK, step):
+                nc.sync.dma_start(out=raw[:, j : j + step], in_=rows[:, j : j + step])
             return raw
 
         def quantize(grouped_flat, width, name):
@@ -74,25 +71,43 @@ def tile_picked_devox_none_p_kernel(tc, x_words, x_scales, w1, w2, gate, emb, of
             nc.vector.quantize_mx(out=codes[:].bitcast(FP8X4), scales=scales[:], in_=grouped_flat)
             return codes, scales
 
-        def quantize_w1(raws, half, tags):
-            planes = {}
-            for u in (1, 0):
-                grouped = tile([P, PASSES * K_PASS], BF16, f"w1_grouped{half}{u}", tags[u])
-                for g in range(PASSES):
-                    columns = raws[g][:].rearrange("p j (m t) -> p m j t", t=PACK)
-                    part = grouped[:, g * K_PASS : (g + 1) * K_PASS].rearrange("p (m e j) -> p m j e", e=2, j=PACK)
-                    nc.scalar.activation(part, columns[:, :, :, 2 * u : 2 * u + 2], COPY)
-                planes[u] = quantize(grouped[:], PASSES * P, f"w1q{half}{u}")
-            return planes
+        def quantize_w1(raw, g):
+            grouped = tile([P, PACK, P, PACK], BF16, f"w1_grouped{g}")
+            target = grouped[:].rearrange("p t m j -> p m t j")
+            source = raw[:].rearrange("p j (m t) -> p m t j", t=PACK)
+            split = P // (g + 1)
+            nc.scalar.copy(target[:, :split], source[:, :split])
+            if split < P:
+                nc.vector.tensor_copy(target[:, split:], source[:, split:])
+            return quantize(grouped[:].rearrange("p t m j -> p (t m j)"), H, f"w1q{g}")
+
+        def product(target, weights, weight_scales, values, value_scales, start, stop):
+            nc.tensor.matmul_mx(
+                out=target,
+                lhsT=weights.bitcast(FP8X4),
+                lhsT_scale=weight_scales,
+                rhs=values.bitcast(FP8X4),
+                rhs_scale=value_scales,
+                start=start,
+                stop=stop,
+            )
+
+        def copy(target, source, by_vector):
+            if by_vector:
+                nc.vector.tensor_copy(target, source)
+            else:
+                nc.scalar.copy(target, source)
 
         offs_t = load_list(offs, "offs_t")
-        x_scale_rows = keep.tile([P, T], U8, name="x_scale_rows", align_bytes=64)
+        x_scale_rows = tile([P, T], U8, "x_scale_rows")
         nc.gpsimd.memset(x_scale_rows[:SCALE_BASE].bitcast(I32), 0)
         nc.sync.dma_start(out=x_scale_rows[SCALE_BASE:].bitcast(I32), in_=x_scales.rearrange("g r c -> r g c").bitcast(I32))
-        left_raw = [load_w1(g, 0) for g in range(PASSES)]
-        x_tiles = [load_words(g) for g in range(PASSES)]
+        w1_raw = [load_w1(0)]
         cell_t = load_list(cell, "cell_t")
-        pos_t = [load_list(pos1, "pos1_t"), load_list(pos2, "pos2_t")]
+        pos_t = [load_list(pos1, "pos1_t")]
+        w1_raw.append(load_w1(1))
+        x_tiles = [load_words(g) for g in range(PASSES)]
+        pos_t.append(load_list(pos2, "pos2_t"))
 
         picked_scales = keep.tile([P, S], U8, name="picked_scales", align_bytes=64)
         nc.vector.tensor_copy(picked_scales[:], x_scale_rows[:].indirect(offs_t[:]))
@@ -104,14 +119,11 @@ def tile_picked_devox_none_p_kernel(tc, x_words, x_scales, w1, w2, gate, emb, of
                 in_=picked_scales[SCALE_BASE + 8 * q : SCALE_BASE + 8 * q + 8].bitcast(I32),
             )
 
-        ident = tile([P, P], F32, "ident")
-        make_identity(nc, ident[:])
-        windows = [tile([P, U], F32, f"window{n}") for n in range(4)]
+        windows = [tile([P, 2 * U], F32, f"window{n}") for n in range(4)]
         for n in range(4):
-            (nc.vector if n < 2 else nc.gpsimd).memset(windows[n][:].bitcast(I32), 0)
+            (nc.vector if n < 2 else nc.gpsimd).memset(windows[n][:, :U].bitcast(I32), 0)
 
-        w1q = [quantize_w1(left_raw, 0, ("left_grouped0", "left_grouped1"))]
-        right_raw = [load_w1(g, 1) for g in range(PASSES)]
+        w1q = [quantize_w1(w1_raw[g], g) for g in range(PASSES)]
 
         xg = [tile([P, S], U32, f"xg{g}") for g in range(PASSES)]
         nc.vector.tensor_copy(xg[0][:], x_tiles[0][:].bitcast(U32).indirect(offs_t[:]))
@@ -122,164 +134,91 @@ def tile_picked_devox_none_p_kernel(tc, x_words, x_scales, w1, w2, gate, emb, of
             )
 
         emb_rows = emb.rearrange("(p t) u -> p t u", t=PACK)
-
-        def load_emb(n, tag):
-            half, u = PLANES[n]
-            rows = tile([P, U], F32, f"emb{n}", tag)
-            nc.sync.dma_start(out=rows[:], in_=emb_rows[half * HALF_P : (half + 1) * HALF_P, 2 * u : 2 * u + 2, :])
-            return rows
-
-        def scatter(index, n, first, count, tag):
-            half, u = PLANES[n]
-            codes, scales = w1q[half][u]
-            acc = bank(index, f"h{n}_{first}")
-            lead = count % (S // 2)
-            for start, size in ((0, lead), (lead, count - lead)):
-                if size:
-                    for g in range(PASSES):
-                        column = g * P
-                        nc.tensor.matmul_mx(
-                            out=acc[:, start : start + size],
-                            lhsT=codes[:, column : column + P].bitcast(FP8X4),
-                            lhsT_scale=scales[:, column : column + P],
-                            rhs=xg[g][:, first + start : first + start + size].bitcast(FP8X4),
-                            rhs_scale=xg_scales[:, g, first + start : first + start + size],
-                            start=(g == 0),
-                            stop=(g == PASSES - 1),
-                        )
-            staged = tile([P, count], F32, f"h_sb{n}_{first}", tag)
-            if index == 0 and n == 0:
-                nc.vector.tensor_scalar_max(staged[:], acc[:, :count], 0.0)
-            else:
-                nc.scalar.activation(staged[:], acc[:, :count], RELU)
-            nc.vector.tensor_copy(windows[n][:].indirect(entries(cell_t, first, count)), staged[:])
-
-        emb_t = [load_emb(0, "left_grouped0")]
-        scatter(0, 0, 0, OPENING, "staged0")
-        scatter(1, 1, 0, OPENING, "staged1")
-        scatter(2, 0, OPENING, S - OPENING, "staged2")
-        emb_t.append(load_emb(1, "left_grouped1"))
-        w1q.append(quantize_w1(right_raw, 1, ("staged1", "staged0")))
-        scatter(3, 1, OPENING, S - OPENING, "w1_raw1")
-        emb_t.append(load_emb(2, "w1_raw0"))
-        emb_t.append(load_emb(3, "staged2"))
-        scatter(0, 2, 0, S, "staged4")
-        scatter(1, 3, 0, S, "staged5")
-
-        w2_raw = tile([P, PACK, N], F32, "w2_raw", "staged0")
+        for n in range(4):
+            nc.sync.dma_start(out=windows[n][:, U:], in_=emb_rows[:, n ^ 1, :])
+        w2_raw = tile([P, PACK, N], F32, "w2_raw", "w1_raw0")
         nc.sync.dma_start(out=w2_raw[:], in_=w2.rearrange("(p j) n -> p j n", j=PACK))
         gate_t = tile([P, 2, V], F32, "gate_t", "w1_raw1")
         nc.sync.dma_start(out=gate_t[:], in_=gate.rearrange("d p v -> p d v"))
-        w2_grouped = keep.tile([P, N, PACK], BF16, name="w2_grouped", align_bytes=64)
-        nc.scalar.activation(
+
+        def first_product(index, n, first, staged, by_vector):
+            count = staged.shape[1]
+            acc = bank(index, f"h{n}_{first}")
+            for start in range(0, count, HALF_S):
+                for g in range(PASSES):
+                    codes, scales = w1q[g]
+                    picked = slice(first + start, first + start + HALF_S)
+                    product(acc[:, start : start + HALF_S], codes[:, n * P : (n + 1) * P], scales[:, n * P : (n + 1) * P],
+                            xg[g][:, picked], xg_scales[:, g, picked], g == 0, g == PASSES - 1)
+            if by_vector:
+                nc.vector.tensor_scalar_max(staged, acc[:, :count], 0.0)
+            else:
+                nc.scalar.activation(staged, acc[:, :count], RELU)
+            return staged
+
+        def scatter(n, first, count, values, by_vector):
+            target = windows[n][:].indirect(entries(cell_t, first, count))
+            if by_vector:
+                nc.vector.tensor_copy(target, values)
+            else:
+                nc.scalar.activation(target, values, COPY)
+
+        early = laid.tile([P, 5, HALF_S], F32, name="early", offset=1536, align_bytes=64)
+        pairs = [laid.tile([P, 2, count * 2], BF16, name=f"pairs{first}", offset=place, align_bytes=64) for (first, count), place in zip(CELL_CHUNKS, PAIR_PLACES)]
+
+        def add_emb(u, q):
+            first, count = CELL_CHUNKS[q]
+            even = windows[2 * u][:].rearrange("p (e r) -> p e r", e=2)[:, :, first : first + count]
+            odd = windows[2 * u + 1][:].rearrange("p (e r) -> p e r", e=2)[:, ::-1, first : first + count]
+            nc.vector.tensor_tensor(
+                pairs[q][:, u].rearrange("p (c i e) -> p c e i", i=4, e=2),
+                even.rearrange("p e (c i) -> p c e i", i=4),
+                odd.rearrange("p e (c i) -> p c e i", i=4),
+                ADD,
+            )
+
+        scatter(0, 0, HALF_S, first_product(0, 0, 0, early[:, 0], False), False)
+        scatter(1, 0, HALF_S, first_product(1, 1, 0, early[:, 1], True), True)
+        scatter(0, HALF_S, HALF_S, first_product(2, 0, HALF_S, early[:, 4], False), False)
+        scatter(1, HALF_S, HALF_S, first_product(3, 1, HALF_S, early[:, 2], True), True)
+        third = first_product(0, 2, 0, tile([P, S], F32, "h_sb2")[:], False)
+        for half in range(2):
+            scatter(2, half * HALF_S, HALF_S, third[:, half * HALF_S : (half + 1) * HALF_S], False)
+        scatter(3, 0, HALF_S, first_product(1, 3, 0, early[:, 3], True), True)
+        scatter(3, HALF_S, HALF_S, first_product(2, 3, HALF_S, tile([P, HALF_S], F32, "h_sb3")[:], True), False)
+
+        w2_grouped = tile([P, N, PACK], BF16, "w2_grouped")
+        nc.vector.tensor_copy(
             w2_grouped[:].rearrange("p (c i) j -> p c j i", i=4),
             w2_raw[:].rearrange("p j (c i) -> p c j i", i=4),
-            COPY,
         )
+        for q in range(len(CELL_CHUNKS)):
+            add_emb(0, q)
         w2_codes, w2_scales = quantize(w2_grouped[:].rearrange("p c j -> p (c j)"), N, "w2q")
-
-        groups = U // P // PAIR_BLOCKS
-        width = PAIR_BLOCKS * P
-        rows = [[tile([P, PAIR_BLOCKS, 2, P], BF16, f"z_rows{u}{q}") for q in range(groups)] for u in range(2)]
-
-        def transpose(target, source, start, stop):
-            nc.tensor.matmul(target, source, ident[:], start=start, stop=stop, is_transpose=True)
-
-        def round_out(n, q, sums, by_vector=False):
-            half, u = PLANES[n]
-            blocks = sums.rearrange("r (b c) -> r b c", b=PAIR_BLOCKS)
-            if by_vector:
-                nc.vector.tensor_copy(rows[u][q][:, :, half, :], blocks)
-            else:
-                nc.scalar.copy(rows[u][q][:, :, half, :], blocks)
-
-        def words(u, q, b):
-            return rows[u][q][:].rearrange("r b h c -> r (b h c)").bitcast(F32)[:, b * P : (b + 1) * P]
-
-        for n in range(3):
-            sums = [bank(4 + 2 * (n % 2) + side, f"zt{n}_{side}") for side in range(2)]
-            for k, source in enumerate((emb_t[n], windows[n])):
-                for side in range(2):
-                    for b in range(BANK_BLOCKS):
-                        column = (side * BANK_BLOCKS + b) * P
-                        first, last = k == 0 and b == 0, k == 1 and b == BANK_BLOCKS - 1
-                        transpose(sums[side][:, b * P : (b + 1) * P], source[:, column : column + P], first, last)
-            for q in range(groups):
-                side, part = divmod(q, 2)
-                round_out(n, q, sums[side][:, part * width : (part + 1) * width])
-
-        backs = [bank(q, f"zw{q}") for q in range(groups)]
-        for q in range(groups):
-            for b in range(PAIR_BLOCKS):
-                column = q * width + b * P
-                transpose(backs[q][:, b * P : (b + 1) * P], emb_t[3][:, column : column + P], b == 0, False)
-        unread = bank(4, "warm_up")
-        codes, scales = w1q[1][0]
-        nc.tensor.matmul_mx(
-            out=unread[:],
-            lhsT=codes[:, :P].bitcast(FP8X4),
-            lhsT_scale=scales[:, :P],
-            rhs=xg[0][:].bitcast(FP8X4),
-            rhs_scale=xg_scales[:, 0],
-            start=True,
-            stop=True,
-        )
-        for q in range(groups):
-            for b in range(PAIR_BLOCKS):
-                transpose(backs[q][:, width + b * P : width + (b + 1) * P], words(1, q, b), False, False)
-        for q in range(groups):
-            for b in range(PAIR_BLOCKS):
-                column = q * width + b * P
-                transpose(backs[q][:, b * P : (b + 1) * P], windows[3][:, column : column + P], False, b == PAIR_BLOCKS - 1)
-            round_out(3, q, backs[q][:, :width], q in ROUNDED_BY_VECTOR)
-        z_grouped = []
-        for q in range(groups):
-            for b in range(PAIR_BLOCKS):
-                transpose(backs[q][:, b * P : (b + 1) * P], words(0, q, b), True, True)
-            grouped = tile([P, width * PACK], BF16, f"z_grouped{q}")
-            woven = grouped[:].bitcast(F32).rearrange("p (c i u) -> p c u i", i=2, u=2)
-            pairs = backs[q][:].rearrange("p (u c i) -> p c u i", u=2, i=2)
-            if q in WOVEN_BY_VECTOR:
-                nc.vector.tensor_copy(woven, pairs)
-            else:
-                nc.scalar.copy(woven, pairs)
-            z_grouped.append(grouped)
+        for q in range(len(CELL_CHUNKS)):
+            add_emb(1, q)
 
         y = keep.tile([P, U], F32, name="y")
         for q, (first, count) in enumerate(CELL_CHUNKS):
-            group, start = divmod(first, PAIR_BLOCKS)
-            codes, scales = quantize(z_grouped[group][:, start * P * PACK : (start + count) * P * PACK], count * P, f"zq{q}")
-            acc = bank(4 + (q + 2) % 4, f"y{q}")
-            nc.tensor.matmul_mx(
-                out=acc[:, : count * P],
-                lhsT=w2_codes[:].bitcast(FP8X4),
-                lhsT_scale=w2_scales[:],
-                rhs=codes[:].bitcast(FP8X4),
-                rhs_scale=scales[:],
-                start=True,
-                stop=True,
-            )
-            if q not in COPIED_BY_VECTOR:
-                nc.scalar.copy(y[:, first * P : (first + count) * P], acc[:, : count * P])
-            else:
-                nc.vector.tensor_copy(y[:, first * P : (first + count) * P], acc[:, : count * P])
+            grouped = tile([P, count * PACK], BF16, f"z_grouped{q}")
+            woven = grouped[:].bitcast(F32).rearrange("p (c i u) -> p c u i", i=2, u=2)
+            words = pairs[q][:].bitcast(F32).rearrange("p u (c i) -> p c u i", i=2)
+            copy(woven, words, q in WOVEN_BY_VECTOR)
+            codes, scales = quantize(grouped[:], count, f"zq{q}")
+            acc = bank(2 + q, f"y{q}")
+            product(acc[:, :count], w2_codes[:], w2_scales[:], codes[:], scales[:], True, True)
+            copy(y[:, first : first + count], acc[:, :count], q in COPIED_BY_VECTOR)
 
         first_term = keep.tile([P, V], F32, name="first_term")
         nc.vector.tensor_tensor(first_term[:], y[:].indirect(pos_t[0][:]), gate_t[:, 0], MULT)
-
-        def second_term(first, count):
+        terms = []
+        for first, count in OUT_PIECES:
+            fetched = keep.tile([P, count], F32, name=f"fetched{first}")
+            nc.scalar.activation(fetched[:], y[:].indirect(entries(pos_t[1], first, count)), COPY)
             term = keep.tile([P, count], F32, name=f"second_term{first}")
-            nc.vector.tensor_tensor(term[:], y[:].indirect(entries(pos_t[1], first, count)), gate_t[:, 1, first : first + count], MULT)
-            return term
-
-        def add_and_store(first, count, term):
+            nc.vector.tensor_tensor(term[:], fetched[:], gate_t[:, 1, first : first + count], MULT)
+            terms.append(term)
+        for (first, count), term in zip(OUT_PIECES, terms):
             result = keep.tile([P, count], F32, name=f"result{first}")
             nc.vector.tensor_tensor(result[:], first_term[:, first : first + count], term[:], ADD)
             nc.sync.dma_start(out=out[:, first : first + count], in_=result[:])
-
-        waiting = second_term(*OUT_PIECES[0])
-        for done, ahead in zip(OUT_PIECES, OUT_PIECES[1:]):
-            term = second_term(*ahead)
-            add_and_store(*done, waiting)
-            waiting = term
-        add_and_store(*OUT_PIECES[-1], waiting)

@@ -26,9 +26,9 @@ SCALE_BASE = 96
 HALF_S = S // 2
 CELL_CHUNKS = ((0, 256), (256, 256), (512, 256), (768, 128), (896, 128))
 PAIR_PLACES = (0, 6144, 2048, 4096, 5120)
-WOVEN_BY_VECTOR = (2,)
+WOVEN_BY_VECTOR = ()
 COPIED_BY_VECTOR = (3,)
-OUT_PIECES = ((0, 256), (256, 256))
+OUT_PIECES = ((0, 384), (384, 128))
 
 
 def tile_picked_devox_none_p_kernel(tc, x_words, x_scales, w1, w2, gate, emb, offs, cell, pos1, pos2, out):
@@ -54,7 +54,9 @@ def tile_picked_devox_none_p_kernel(tc, x_words, x_scales, w1, w2, gate, emb, of
 
         def load_words(g):
             words = tile([P, T], I32, f"x_words{g}")
-            nc.sync.dma_start(out=words[:], in_=x_words[g].rearrange("p n t -> p (n t)").bitcast(I32))
+            rows = x_words[g].rearrange("p n t -> p (n t)").bitcast(I32)
+            for first in range(0, T, T // 2):
+                nc.sync.dma_start(out=words[:, first : first + T // 2], in_=rows[:, first : first + T // 2])
             return words
 
         def load_w1(g):
@@ -102,12 +104,9 @@ def tile_picked_devox_none_p_kernel(tc, x_words, x_scales, w1, w2, gate, emb, of
         x_scale_rows = tile([P, T], U8, "x_scale_rows")
         nc.gpsimd.memset(x_scale_rows[:SCALE_BASE].bitcast(I32), 0)
         nc.sync.dma_start(out=x_scale_rows[SCALE_BASE:].bitcast(I32), in_=x_scales.rearrange("g r c -> r g c").bitcast(I32))
-        w1_raw = [load_w1(0)]
-        cell_t = load_list(cell, "cell_t")
-        pos_t = [load_list(pos1, "pos1_t")]
-        w1_raw.append(load_w1(1))
+        w1_raw = [load_w1(g) for g in range(PASSES)]
         x_tiles = [load_words(g) for g in range(PASSES)]
-        pos_t.append(load_list(pos2, "pos2_t"))
+        cell_t = load_list(cell, "cell_t")
 
         picked_scales = keep.tile([P, S], U8, name="picked_scales", align_bytes=64)
         nc.vector.tensor_copy(picked_scales[:], x_scale_rows[:].indirect(offs_t[:]))
@@ -140,6 +139,7 @@ def tile_picked_devox_none_p_kernel(tc, x_words, x_scales, w1, w2, gate, emb, of
         nc.sync.dma_start(out=w2_raw[:], in_=w2.rearrange("(p j) n -> p j n", j=PACK))
         gate_t = tile([P, 2, V], F32, "gate_t", "w1_raw1")
         nc.sync.dma_start(out=gate_t[:], in_=gate.rearrange("d p v -> p d v"))
+        pos_t = [load_list(pos1, "pos1_t"), load_list(pos2, "pos2_t")]
 
         def first_product(index, n, first, staged, by_vector):
             count = staged.shape[1]
@@ -177,25 +177,35 @@ def tile_picked_devox_none_p_kernel(tc, x_words, x_scales, w1, w2, gate, emb, of
                 ADD,
             )
 
-        scatter(0, 0, HALF_S, first_product(0, 0, 0, early[:, 0], False), False)
-        scatter(1, 0, HALF_S, first_product(1, 1, 0, early[:, 1], True), True)
-        scatter(0, HALF_S, HALF_S, first_product(2, 0, HALF_S, early[:, 4], False), False)
-        scatter(1, HALF_S, HALF_S, first_product(3, 1, HALF_S, early[:, 2], True), True)
-        third = first_product(0, 2, 0, tile([P, S], F32, "h_sb2")[:], False)
-        for half in range(2):
-            scatter(2, half * HALF_S, HALF_S, third[:, half * HALF_S : (half + 1) * HALF_S], False)
-        scatter(3, 0, HALF_S, first_product(1, 3, 0, early[:, 3], True), True)
-        scatter(3, HALF_S, HALF_S, first_product(2, 3, HALF_S, tile([P, HALF_S], F32, "h_sb3")[:], True), False)
+        def staging(name):
+            return tile([P, HALF_S], F32, name)[:]
 
-        w2_grouped = tile([P, N, PACK], BF16, "w2_grouped")
-        nc.vector.tensor_copy(
+        scatter(0, 0, HALF_S, first_product(0, 0, 0, early[:, 0], False), False)
+        b1 = first_product(1, 1, 0, early[:, 1], True)
+        a2 = first_product(2, 0, HALF_S, early[:, 4], True)
+        b2 = first_product(3, 1, HALF_S, early[:, 2], False)
+        scatter(1, 0, HALF_S, b1, True)
+        scatter(0, HALF_S, HALF_S, a2, False)
+        c1 = first_product(0, 2, 0, staging("c1"), True)
+        scatter(1, HALF_S, HALF_S, b2, True)
+        d1 = first_product(1, 3, 0, early[:, 3], True)
+        scatter(2, 0, HALF_S, c1, False)
+        c2 = first_product(2, 2, HALF_S, staging("c2"), False)
+        d2 = first_product(3, 3, HALF_S, staging("d2"), False)
+        scatter(2, HALF_S, HALF_S, c2, False)
+        scatter(3, 0, HALF_S, d1, True)
+        scatter(3, HALF_S, HALF_S, d2, False)
+
+        w2_grouped = tile([P, N, PACK], BF16, "w2_grouped", "d2")
+        nc.scalar.copy(
             w2_grouped[:].rearrange("p (c i) j -> p c j i", i=4),
             w2_raw[:].rearrange("p j (c i) -> p c j i", i=4),
         )
         for q in range(len(CELL_CHUNKS)):
             add_emb(0, q)
+        add_emb(1, 0)
         w2_codes, w2_scales = quantize(w2_grouped[:].rearrange("p c j -> p (c j)"), N, "w2q")
-        for q in range(len(CELL_CHUNKS)):
+        for q in range(1, len(CELL_CHUNKS)):
             add_emb(1, q)
 
         y = keep.tile([P, U], F32, name="y")

@@ -25,17 +25,15 @@ LIST_COLS = S // 16
 SCALE_BASE = 96
 HALF_S = S // 2
 CELL_CHUNKS = ((0, 256), (256, 256), (512, 256), (768, 128), (896, 128))
-PAIR_PLACES = (0, 6144, 2048, 4096, 5120)
 WOVEN_BY_VECTOR = ()
 COPIED_BY_VECTOR = (3,)
-OUT_PIECES = ((0, 384), (384, 128))
+OUT_PIECES = ((0, 256), (256, 256))
 
 
 def tile_picked_devox_none_p_kernel(tc, x_words, x_scales, w1, w2, gate, emb, offs, cell, pos1, pos2, out):
     nc = tc.nc
     with ExitStack() as ctx:
         keep = ctx.enter_context(tc.tile_pool(name="keep", bufs=1))
-        laid = ctx.enter_context(tc.tile_pool(name="laid", bufs=1))
         psum = ctx.enter_context(tc.psum_pool(name="psum", bufs=1))
 
         def tile(shape, dtype, name, tag=None):
@@ -133,7 +131,7 @@ def tile_picked_devox_none_p_kernel(tc, x_words, x_scales, w1, w2, gate, emb, of
             )
 
         emb_rows = emb.rearrange("(p t) u -> p t u", t=PACK)
-        for n in range(4):
+        for n in (0, 1, 3, 2):
             nc.sync.dma_start(out=windows[n][:, U:], in_=emb_rows[:, n ^ 1, :])
         w2_raw = tile([P, PACK, N], F32, "w2_raw", "w1_raw0")
         nc.sync.dma_start(out=w2_raw[:], in_=w2.rearrange("(p j) n -> p j n", j=PACK))
@@ -163,8 +161,7 @@ def tile_picked_devox_none_p_kernel(tc, x_words, x_scales, w1, w2, gate, emb, of
             else:
                 nc.scalar.activation(target, values, COPY)
 
-        early = laid.tile([P, 5, HALF_S], F32, name="early", offset=1536, align_bytes=64)
-        pairs = [laid.tile([P, 2, count * 2], BF16, name=f"pairs{first}", offset=place, align_bytes=64) for (first, count), place in zip(CELL_CHUNKS, PAIR_PLACES)]
+        pairs = [tile([P, 2, count * 2], BF16, f"pairs{first}") for first, count in CELL_CHUNKS]
 
         def add_emb(u, q):
             first, count = CELL_CHUNKS[q]
@@ -177,32 +174,32 @@ def tile_picked_devox_none_p_kernel(tc, x_words, x_scales, w1, w2, gate, emb, of
                 ADD,
             )
 
-        def staging(name):
-            return tile([P, HALF_S], F32, name)[:]
+        def staging(name, tag=None):
+            return tile([P, HALF_S], F32, name, tag)[:]
 
-        scatter(0, 0, HALF_S, first_product(0, 0, 0, early[:, 0], False), False)
-        b1 = first_product(1, 1, 0, early[:, 1], True)
-        a2 = first_product(2, 0, HALF_S, early[:, 4], True)
-        b2 = first_product(3, 1, HALF_S, early[:, 2], False)
+        scatter(0, 0, HALF_S, first_product(0, 0, 0, staging("a1"), False), False)
+        b1 = first_product(1, 1, 0, staging("b1"), True)
+        a2 = first_product(2, 0, HALF_S, staging("a2"), True)
         scatter(1, 0, HALF_S, b1, True)
+        b2 = first_product(3, 1, HALF_S, staging("b2", "b1"), True)
         scatter(0, HALF_S, HALF_S, a2, False)
-        c1 = first_product(0, 2, 0, staging("c1"), True)
+        d1 = first_product(0, 3, 0, staging("d1"), False)
         scatter(1, HALF_S, HALF_S, b2, True)
-        d1 = first_product(1, 3, 0, early[:, 3], True)
-        scatter(2, 0, HALF_S, c1, False)
+        c1 = first_product(1, 2, 0, staging("c1"), False)
         c2 = first_product(2, 2, HALF_S, staging("c2"), False)
-        d2 = first_product(3, 3, HALF_S, staging("d2"), False)
+        d2 = first_product(3, 3, HALF_S, staging("d2", "b1"), True)
+        scatter(3, 0, HALF_S, d1, False)
+        scatter(2, 0, HALF_S, c1, False)
         scatter(2, HALF_S, HALF_S, c2, False)
-        scatter(3, 0, HALF_S, d1, True)
-        scatter(3, HALF_S, HALF_S, d2, False)
+        for q in range(len(CELL_CHUNKS)):
+            add_emb(0, q)
+        scatter(3, HALF_S, HALF_S, d2, True)
 
-        w2_grouped = tile([P, N, PACK], BF16, "w2_grouped", "d2")
+        w2_grouped = tile([P, N, PACK], BF16, "w2_grouped", "c2")
         nc.scalar.copy(
             w2_grouped[:].rearrange("p (c i) j -> p c j i", i=4),
             w2_raw[:].rearrange("p j (c i) -> p c j i", i=4),
         )
-        for q in range(len(CELL_CHUNKS)):
-            add_emb(0, q)
         add_emb(1, 0)
         w2_codes, w2_scales = quantize(w2_grouped[:].rearrange("p c j -> p (c j)"), N, "w2q")
         for q in range(1, len(CELL_CHUNKS)):

@@ -24,6 +24,7 @@ PASSES = K // K_PASS
 LIST_COLS = S // 16
 SCALE_BASE = 96
 HALF_S = S // 2
+CAST_BY_SCALAR = (64, 32)
 CELL_CHUNKS = ((0, 256), (256, 256), (512, 256), (768, 128), (896, 128))
 WOVEN_BY_VECTOR = ()
 COPIED_BY_VECTOR = (3,)
@@ -34,6 +35,7 @@ def tile_picked_devox_none_p_kernel(tc, x_words, x_scales, w1, w2, gate, emb, of
     nc = tc.nc
     with ExitStack() as ctx:
         keep = ctx.enter_context(tc.tile_pool(name="keep", bufs=1))
+        laid = ctx.enter_context(tc.tile_pool(name="laid", bufs=1))
         psum = ctx.enter_context(tc.psum_pool(name="psum", bufs=1))
 
         def tile(shape, dtype, name, tag=None):
@@ -75,10 +77,9 @@ def tile_picked_devox_none_p_kernel(tc, x_words, x_scales, w1, w2, gate, emb, of
             grouped = tile([P, PACK, P, PACK], BF16, f"w1_grouped{g}")
             target = grouped[:].rearrange("p t m j -> p m t j")
             source = raw[:].rearrange("p j (m t) -> p m t j", t=PACK)
-            split = P // (g + 1)
+            split = CAST_BY_SCALAR[g]
             nc.scalar.copy(target[:, :split], source[:, :split])
-            if split < P:
-                nc.vector.tensor_copy(target[:, split:], source[:, split:])
+            nc.vector.tensor_copy(target[:, split:], source[:, split:])
             return quantize(grouped[:].rearrange("p t m j -> p (t m j)"), H, f"w1q{g}")
 
         def product(target, weights, weight_scales, values, value_scales, start, stop):
@@ -174,20 +175,23 @@ def tile_picked_devox_none_p_kernel(tc, x_words, x_scales, w1, w2, gate, emb, of
                 ADD,
             )
 
-        def staging(name, tag=None):
-            return tile([P, HALF_S], F32, name, tag)[:]
+        def staging(name):
+            return tile([P, HALF_S], F32, name)[:]
+
+        def shared_staging(name, place):
+            return laid.tile([P, HALF_S], F32, name=name, offset=place, align_bytes=64)[:]
 
         scatter(0, 0, HALF_S, first_product(0, 0, 0, staging("a1"), False), False)
-        b1 = first_product(1, 1, 0, staging("b1"), True)
+        b1 = first_product(1, 1, 0, shared_staging("b1", 512), True)
         a2 = first_product(2, 0, HALF_S, staging("a2"), True)
         scatter(1, 0, HALF_S, b1, True)
-        b2 = first_product(3, 1, HALF_S, staging("b2", "b1"), True)
+        b2 = first_product(3, 1, HALF_S, shared_staging("b2", 512), True)
         scatter(0, HALF_S, HALF_S, a2, False)
         d1 = first_product(0, 3, 0, staging("d1"), False)
         scatter(1, HALF_S, HALF_S, b2, True)
         c1 = first_product(1, 2, 0, staging("c1"), False)
-        c2 = first_product(2, 2, HALF_S, staging("c2"), False)
-        d2 = first_product(3, 3, HALF_S, staging("d2", "b1"), True)
+        c2 = first_product(2, 2, HALF_S, shared_staging("c2", 0), True)
+        d2 = first_product(3, 3, HALF_S, shared_staging("d2", 1024), True)
         scatter(3, 0, HALF_S, d1, False)
         scatter(2, 0, HALF_S, c1, False)
         scatter(2, HALF_S, HALF_S, c2, False)
@@ -195,7 +199,7 @@ def tile_picked_devox_none_p_kernel(tc, x_words, x_scales, w1, w2, gate, emb, of
             add_emb(0, q)
         scatter(3, HALF_S, HALF_S, d2, True)
 
-        w2_grouped = tile([P, N, PACK], BF16, "w2_grouped", "c2")
+        w2_grouped = tile([P, N, PACK], BF16, "w2_grouped", "c1")
         nc.scalar.copy(
             w2_grouped[:].rearrange("p (c i) j -> p c j i", i=4),
             w2_raw[:].rearrange("p j (c i) -> p c j i", i=4),
@@ -208,8 +212,8 @@ def tile_picked_devox_none_p_kernel(tc, x_words, x_scales, w1, w2, gate, emb, of
         y = keep.tile([P, U], F32, name="y")
         for q, (first, count) in enumerate(CELL_CHUNKS):
             grouped = tile([P, count * PACK], BF16, f"z_grouped{q}")
-            woven = grouped[:].bitcast(F32).rearrange("p (c i u) -> p c u i", i=2, u=2)
-            words = pairs[q][:].bitcast(F32).rearrange("p u (c i) -> p c u i", i=2)
+            woven = grouped[:].bitcast(F32).rearrange("p (c i u) -> p c u i", i=4, u=2)
+            words = pairs[q][:].bitcast(F32).rearrange("p u (c i) -> p c u i", i=4)
             copy(woven, words, q in WOVEN_BY_VECTOR)
             codes, scales = quantize(grouped[:], count, f"zq{q}")
             acc = bank(2 + q, f"y{q}")

@@ -185,21 +185,20 @@ def tile_picked_devox_none_p_kernel(tc, x_words, x_scales, w1, w2, gate, emb, of
         b1 = first_product(1, 1, 0, shared_staging("b1", 512), True)
         a2 = first_product(2, 0, HALF_S, staging("a2"), True)
         scatter(1, 0, HALF_S, b1, True)
-        b2 = first_product(3, 1, HALF_S, shared_staging("b2", 512), True)
+        b2 = first_product(3, 1, HALF_S, shared_staging("b2", 0), True)
         scatter(0, HALF_S, HALF_S, a2, False)
-        d1 = first_product(0, 3, 0, staging("d1"), False)
+        d1 = first_product(0, 3, 0, shared_staging("d1", 1024), True)
         scatter(1, HALF_S, HALF_S, b2, True)
-        c1 = first_product(1, 2, 0, staging("c1"), False)
-        c2 = first_product(2, 2, HALF_S, shared_staging("c2", 0), True)
-        d2 = first_product(3, 3, HALF_S, shared_staging("d2", 1024), True)
+        third = first_product(1, 2, 0, tile([P, S], F32, "third")[:], False)
+        d2 = first_product(2, 3, HALF_S, shared_staging("d2", 0), True)
         scatter(3, 0, HALF_S, d1, False)
-        scatter(2, 0, HALF_S, c1, False)
-        scatter(2, HALF_S, HALF_S, c2, False)
+        scatter(2, 0, HALF_S, third[:, :HALF_S], False)
+        scatter(2, HALF_S, HALF_S, third[:, HALF_S:], False)
         for q in range(len(CELL_CHUNKS)):
             add_emb(0, q)
         scatter(3, HALF_S, HALF_S, d2, True)
 
-        w2_grouped = tile([P, N, PACK], BF16, "w2_grouped", "c1")
+        w2_grouped = tile([P, N, PACK], BF16, "w2_grouped")
         nc.scalar.copy(
             w2_grouped[:].rearrange("p (c i) j -> p c j i", i=4),
             w2_raw[:].rearrange("p j (c i) -> p c j i", i=4),

from contextlib import ExitStack

import concourse.mybir as mybir

K, T, S, V, H, N, U = 1024, 2048, 512, 512, 512, 128, 1024
FLOPS = 2 * (K * H * S + H * N * U)

F32 = mybir.dt.float32
BF16 = mybir.dt.bfloat16
I32 = mybir.dt.int32
U32 = mybir.dt.uint32
U16 = mybir.dt.uint16
U8 = mybir.dt.uint8
FP8X4 = mybir.dt.float8_e4m3fn_x4
RELU = mybir.ActivationFunctionType.Relu
COPY = mybir.ActivationFunctionType.Copy
MULT = mybir.AluOpType.mult
ADD = mybir.AluOpType.add

P = 128
PACK = 4
K_PASS = P * PACK
PASSES = K // K_PASS
LIST_COLS = S // 16
SCALE_BASE = 96
HALF_S = S // 2
CAST_BY_SCALAR = (64, 32)
CELL_CHUNKS = ((0, 256), (256, 256), (512, 256), (768, 128), (896, 128))
WOVEN_BY_VECTOR = ()
COPIED_BY_VECTOR = (3,)
OUT_PIECES = ((0, 256), (256, 256))


def tile_picked_devox_none_p_kernel(tc, x_words, x_scales, w1, w2, gate, emb, offs, cell, pos1, pos2, out):
    nc = tc.nc
    with ExitStack() as ctx:
        keep = ctx.enter_context(tc.tile_pool(name="keep", bufs=1))
        laid = ctx.enter_context(tc.tile_pool(name="laid", bufs=1))
        psum = ctx.enter_context(tc.psum_pool(name="psum", bufs=1))

        def tile(shape, dtype, name, tag=None):
            return keep.tile(shape, dtype, name=name, tag=tag or name, align_bytes=64)

        def bank(index, name):
            return psum.tile([P, 512], F32, name=name, tag=f"bank{index}")

        def load_list(src, name):
            offsets = keep.tile([P, LIST_COLS], U16, name=name)
            nc.sync.dma_start(offsets[:], src)
            return offsets

        def entries(offsets, first, count):
            return offsets[:, first // 16 : (first + count) // 16]

        def load_words(g):
            words = tile([P, T], I32, f"x_words{g}")
            rows = x_words[g].rearrange("p n t -> p (n t)").bitcast(I32)
            for first in range(0, T, T // 2):
                nc.sync.dma_start(out=words[:, first : first + T // 2], in_=rows[:, first : first + T // 2])
            return words

        def load_w1(g):
            raw = tile([P, PACK, H], F32, f"w1_raw{g}")
            rows = w1[g * K_PASS : (g + 1) * K_PASS].rearrange("(p j) c -> p j c", j=PACK)
            step = PACK // (g + 1)
            for j in range(0, PACK, step):
                nc.sync.dma_start(out=raw[:, j : j + step], in_=rows[:, j : j + step])
            return raw

        def quantize(grouped_flat, width, name):
            codes = tile([P, width], U32, name + "_codes")
            scales = tile([P, width], U8, name + "_scales")
            nc.vector.quantize_mx(out=codes[:].bitcast(FP8X4), scales=scales[:], in_=grouped_flat)
            return codes, scales

        def quantize_w1(raw, g):
            grouped = tile([P, PACK, P, PACK], BF16, f"w1_grouped{g}")
            target = grouped[:].rearrange("p t m j -> p m t j")
            source = raw[:].rearrange("p j (m t) -> p m t j", t=PACK)
            split = CAST_BY_SCALAR[g]
            nc.scalar.copy(target[:, :split], source[:, :split])
            nc.vector.tensor_copy(target[:, split:], source[:, split:])
            return quantize(grouped[:].rearrange("p t m j -> p (t m j)"), H, f"w1q{g}")

        def product(target, weights, weight_scales, values, value_scales, start, stop):
            nc.tensor.matmul_mx(
                out=target,
                lhsT=weights.bitcast(FP8X4),
                lhsT_scale=weight_scales,
                rhs=values.bitcast(FP8X4),
                rhs_scale=value_scales,
                start=start,
                stop=stop,
            )

        def copy(target, source, by_vector):
            if by_vector:
                nc.vector.tensor_copy(target, source)
            else:
                nc.scalar.copy(target, source)

        offs_t = load_list(offs, "offs_t")
        x_scale_rows = tile([P, T], U8, "x_scale_rows")
        nc.gpsimd.memset(x_scale_rows[:SCALE_BASE].bitcast(I32), 0)
        nc.sync.dma_start(out=x_scale_rows[SCALE_BASE:].bitcast(I32), in_=x_scales.rearrange("g r c -> r g c").bitcast(I32))
        w1_raw = [load_w1(g) for g in range(PASSES)]
        x_tiles = [load_words(g) for g in range(PASSES)]
        cell_t = load_list(cell, "cell_t")

        picked_scales = keep.tile([P, S], U8, name="picked_scales", align_bytes=64)
        nc.vector.tensor_copy(picked_scales[:], x_scale_rows[:].indirect(offs_t[:]))
        xg_scales = keep.tile([P, PASSES, S], U8, name="xg_scales", align_bytes=64)
        nc.gpsimd.memset(xg_scales[:].rearrange("p g s -> p (g s)").bitcast(I32), 0)
        for q in range(4):
            nc.sync.dma_start(
                out=xg_scales[32 * q : 32 * q + 4].bitcast(I32),
                in_=picked_scales[SCALE_BASE + 8 * q : SCALE_BASE + 8 * q + 8].bitcast(I32),
            )

        windows = [tile([P, 2 * U], F32, f"window{n}") for n in range(4)]
        for n in range(4):
            (nc.vector if n < 2 else nc.gpsimd).memset(windows[n][:, :U].bitcast(I32), 0)

        w1q = [quantize_w1(w1_raw[g], g) for g in range(PASSES)]

        xg = [tile([P, S], U32, f"xg{g}") for g in range(PASSES)]
        nc.vector.tensor_copy(xg[0][:], x_tiles[0][:].bitcast(U32).indirect(offs_t[:]))
        for half in range(2):
            nc.vector.tensor_copy(
                xg[1][:, half * S // 2 : (half + 1) * S // 2],
                x_tiles[1][:].bitcast(U32).indirect(entries(offs_t, half * S // 2, S // 2)),
            )

        emb_rows = emb.rearrange("(p t) u -> p t u", t=PACK)
        for n in (0, 1, 3, 2):
            nc.sync.dma_start(out=windows[n][:, U:], in_=emb_rows[:, n ^ 1, :])
        w2_raw = tile([P, PACK, N], F32, "w2_raw", "w1_raw0")
        nc.sync.dma_start(out=w2_raw[:], in_=w2.rearrange("(p j) n -> p j n", j=PACK))
        gate_t = tile([P, 2, V], F32, "gate_t", "w1_raw1")
        nc.sync.dma_start(out=gate_t[:], in_=gate.rearrange("d p v -> p d v"))
        pos_t = [load_list(pos1, "pos1_t"), load_list(pos2, "pos2_t")]

        def first_product(index, n, first, staged, by_vector):
            count = staged.shape[1]
            acc = bank(index, f"h{n}_{first}")
            for start in range(0, count, HALF_S):
                for g in range(PASSES):
                    codes, scales = w1q[g]
                    picked = slice(first + start, first + start + HALF_S)
                    product(acc[:, start : start + HALF_S], codes[:, n * P : (n + 1) * P], scales[:, n * P : (n + 1) * P],
                            xg[g][:, picked], xg_scales[:, g, picked], g == 0, g == PASSES - 1)
            if by_vector:
                nc.vector.tensor_scalar_max(staged, acc[:, :count], 0.0)
            else:
                nc.scalar.activation(staged, acc[:, :count], RELU)
            return staged

        def scatter(n, first, count, values, by_vector):
            target = windows[n][:].indirect(entries(cell_t, first, count))
            if by_vector:
                nc.vector.tensor_copy(target, values)
            else:
                nc.scalar.activation(target, values, COPY)

        pairs = [tile([P, 2, count * 2], BF16, f"pairs{first}") for first, count in CELL_CHUNKS]

        def add_emb(u, q):
            first, count = CELL_CHUNKS[q]
            even = windows[2 * u][:].rearrange("p (e r) -> p e r", e=2)[:, :, first : first + count]
            odd = windows[2 * u + 1][:].rearrange("p (e r) -> p e r", e=2)[:, ::-1, first : first + count]
            nc.vector.tensor_tensor(
                pairs[q][:, u].rearrange("p (c i e) -> p c e i", i=4, e=2),
                even.rearrange("p e (c i) -> p c e i", i=4),
                odd.rearrange("p e (c i) -> p c e i", i=4),
                ADD,
            )

        def staging(name):
            return tile([P, HALF_S], F32, name)[:]

        def shared_staging(name, place):
            return laid.tile([P, HALF_S], F32, name=name, offset=place, align_bytes=64)[:]

        scatter(0, 0, HALF_S, first_product(0, 0, 0, staging("a1"), False), False)
        b1 = first_product(1, 1, 0, shared_staging("b1", 512), True)
        a2 = first_product(2, 0, HALF_S, staging("a2"), True)
        scatter(1, 0, HALF_S, b1, True)
        b2 = first_product(3, 1, HALF_S, shared_staging("b2", 0), True)
        scatter(0, HALF_S, HALF_S, a2, False)
        d1 = first_product(0, 3, 0, shared_staging("d1", 1024), True)
        scatter(1, HALF_S, HALF_S, b2, True)
        third = first_product(1, 2, 0, tile([P, S], F32, "third")[:], False)
        d2 = first_product(2, 3, HALF_S, shared_staging("d2", 0), True)
        scatter(3, 0, HALF_S, d1, False)
        scatter(2, 0, HALF_S, third[:, :HALF_S], False)
        scatter(2, HALF_S, HALF_S, third[:, HALF_S:], False)
        for q in range(len(CELL_CHUNKS)):
            add_emb(0, q)
        scatter(3, HALF_S, HALF_S, d2, True)

        w2_grouped = tile([P, N, PACK], BF16, "w2_grouped")
        nc.scalar.copy(
            w2_grouped[:].rearrange("p (c i) j -> p c j i", i=4),
            w2_raw[:].rearrange("p j (c i) -> p c j i", i=4),
        )
        add_emb(1, 0)
        w2_codes, w2_scales = quantize(w2_grouped[:].rearrange("p c j -> p (c j)"), N, "w2q")
        for q in range(1, len(CELL_CHUNKS)):
            add_emb(1, q)

        y = keep.tile([P, U], F32, name="y")
        for q, (first, count) in enumerate(CELL_CHUNKS):
            grouped = tile([P, count * PACK], BF16, f"z_grouped{q}")
            woven = grouped[:].bitcast(F32).rearrange("p (c i u) -> p c u i", i=4, u=2)
            words = pairs[q][:].bitcast(F32).rearrange("p u (c i) -> p c u i", i=4)
            copy(woven, words, q in WOVEN_BY_VECTOR)
            codes, scales = quantize(grouped[:], count, f"zq{q}")
            acc = bank(2 + q, f"y{q}")
            product(acc[:, :count], w2_codes[:], w2_scales[:], codes[:], scales[:], True, True)
            copy(y[:, first : first + count], acc[:, :count], q in COPIED_BY_VECTOR)

        first_term = keep.tile([P, V], F32, name="first_term")
        nc.vector.tensor_tensor(first_term[:], y[:].indirect(pos_t[0][:]), gate_t[:, 0], MULT)
        terms = []
        for first, count in OUT_PIECES:
            fetched = keep.tile([P, count], F32, name=f"fetched{first}")
            nc.scalar.activation(fetched[:], y[:].indirect(entries(pos_t[1], first, count)), COPY)
            term = keep.tile([P, count], F32, name=f"second_term{first}")
            nc.vector.tensor_tensor(term[:], fetched[:], gate_t[:, 1, first : first + count], MULT)
            terms.append(term)
        for (first, count), term in zip(OUT_PIECES, terms):
            result = keep.tile([P, count], F32, name=f"result{first}")
            nc.vector.tensor_tensor(result[:], first_term[:, first : first + count], term[:], ADD)
            nc.sync.dma_start(out=out[:, first : first + count], in_=result[:])
